import numpy as np, ml_dtypes
CORES = [3,7,11,15,131,135,139,143]
N = 8
import mx_ref
BF = ml_dtypes.bfloat16
def cols(t, e):
    v = np.concatenate([t.reshape(128, -1, 4), np.zeros((128, 1, 4), BF)], axis=1)
    return np.ascontiguousarray(v[:, e]).reshape(128, -1)
def tile(rs):
    return np.stack(rs, axis=2).reshape(128, -1).astype(BF)
def pick(q, e):
    c = np.concatenate([q[0].reshape(128, -1, 4), np.zeros((128, 1, 4), np.uint8)], axis=1); s = np.concatenate([q[1], np.ones((16, 1), np.uint8)], axis=1)
    return (np.ascontiguousarray(c[:, e].reshape(128, -1)), np.ascontiguousarray(s[:, e]))
def join(*qs):
    return (np.concatenate([q[0] for q in qs], axis=1), np.concatenate([q[1] for q in qs], axis=1))
def put(q, e, v):
    c, s = q[0].reshape(128, -1, 4).copy(), q[1].copy(); c[:, e] = v[0].reshape(128, -1, 4); s[:, e] = v[1]
    return (c.reshape(128, -1), s)
def pk(c, s):
    return (np.ascontiguousarray(c), mx_ref.live(s))
def emit(q):
    return q[0], q[1]
def packed(v, rng):
    q = [mx_ref.quantize(np.ascontiguousarray(v[r])) for r in range(N)]
    return np.stack([a for a, b in q]), np.stack([mx_ref.plane(b, rng) for a, b in q])
def decode(q):
    o = []
    for b in range(4):
        e = np.zeros((128, 128, 4), np.float32); e[np.arange(128), np.arange(128), b] = 1
        o.append(mx_ref.matmul(mx_ref.quantize(e.reshape(128, 512).astype(BF)), q))
    return np.stack(o, axis=2).reshape(128, -1)
def f(rng, *shape):
    return mx_ref.flush((rng.standard_normal(shape, dtype=np.float32) * np.exp2(rng.integers(-2, 3, shape[:-1] + (1,)))).astype(BF))
def wide(rng, *shape, cols=0):
    v = rng.standard_normal(shape, dtype=np.float32) * np.exp2(rng.integers(-12, 13, shape)).astype(np.float32)
    if cols: v *= np.repeat(np.exp2(rng.integers(-cols, cols + 1, shape[:-2] + (1, shape[-1] // 4))) * (rng.random(shape[:-2] + (1, shape[-1] // 4)) > 0.0625), 4, axis=-1).astype(np.float32)
    return mx_ref.flush(v.astype(BF))
C, S, K, R = 384, 48, 4, 3
def home(j):
    return j % N * S + j // N
def choose(z):
    e = np.arange(C).reshape(S, N)
    return np.concatenate([e[np.argsort(-z[e[:, a]], kind="stable")[:K], a] for a in range(N)])
def big(v, k):
    v = v.astype(np.float32) * np.float32(k)
    v[np.abs(v) < np.float32(2.0 ** -16)] = 0
    return v.astype(BF)
def weights(rng, k, zero=0, still=slice(0)):
    w = big(f(rng, 128, 2048), k)
    w[:zero] = 0
    w = w.reshape(128, 4, 128, 4)
    w[:, :, still] = 0
    w = w.reshape(128, 2048)
    c, p = packed(np.stack([w] * N), rng)
    return {"wc": c, "ws": p}
def numbers_of(rng):
    return {"x": big(f(rng, N, 128, 4 * C), 1), "pr": big(f(rng, N, 128, 4 * S), 1), "pd": big(f(rng, N, 128, 4 * S), 1), "u": np.array(f(rng, N, 128, 512)), "v": np.array(f(rng, N, 128, 512))}
def signs(rng):
    g = np.stack([rng.permutation(N) % 2 * 2.0 - 1.0 for r in range(N)])
    return g[:, np.arange(C) % N].astype(np.float32)
def setup_inputs(rng):
    return {**numbers_of(rng), **weights(rng, 0.25)}
def setup_inputs_ties(rng):
    d = setup_inputs(rng)
    for r in range(N):
        k = np.stack([rng.permutation(S) % 3 for a in range(N)], axis=1).reshape(-1)
        d["x"][r] = cols(d["x"][r], np.where(k == 2, -1, k))
        for n in ("pr", "pd"): d[n][r] = cols(d[n][r], np.zeros(S, int))
    return d
def setup_inputs_near(rng):
    d = {**numbers_of(rng), **weights(rng, 0.25, 0, np.r_[0:16, 64:64 + 8 * R])}
    x = d["x"].reshape(N, 128, C, 4)
    d["u"][:, :, :4 * R] = 0
    d["v"][:, :, :4 * R] = 0
    for n, g in (("pr", -1), ("pd", 1)):
        p = d[n].reshape(N, 128, S, 4)
        p[:, 0, :, 0] = g
        d[n] = p.reshape(N, 128, 4 * S)
    x[:, :8] = 0
    x[:, 8, :, 0] = signs(rng).astype(BF)
    x[:, 64:64 + 8 * R] = 0
    for t in range(R):
        p = 64 + 8 * t
        d["v"][:, 0, 4 * t] = 1
        d["u"][:, 8, 4 * t] = 1
        d["u"][:, p:p + 2, 4 * t:4 * t + 4] = 1
        s = (np.arange(C) // N + t * (K + 1)) % S + K % 4
        v = (((s[:, None] >> np.arange(8)) & 1) * np.exp2(np.arange(8) - 23.0)).astype(np.float32).astype(BF)
        x[:, p] = v[None, :, :4]
        x[:, p + 1] = v[None, :, 4:]
    return {**d, "x": x.reshape(N, 128, 4 * C)}
def setup_inputs_huge(rng):
    d = numbers_of(rng)
    d["u"][:, :, :4 * R] = ((1.5 + 0.5 * rng.random((N, 128, 4 * R))) * 2.0 ** 29).astype(np.float32).astype(BF)
    g = signs(rng)
    top = (np.arange(C) // N // K)[None, :] == np.arange(N)[:, None]
    size = np.repeat(np.where(top == (g > 0), 1.5, 1.0625), 4, axis=1)[:, None, :]
    x = (size + 0.25 * rng.random((N, 128, 4 * C))) * np.repeat(np.where(g > 0, 2.0 ** 26, -2.0 ** 28), 4, axis=1)[:, None, :]
    return {**d, "x": x.astype(np.float32).astype(BF), "pr": big(d["pr"], 2.0 ** 22), "pd": big(d["pd"], 2.0 ** 22), "v": big(d["v"], 2.0 ** 25), **weights(rng, 2.0 ** -7)}
def setup_inputs_crowd(rng):
    d = {**numbers_of(rng), **weights(rng, 0.25, 64)}
    x = d["x"].reshape(N, 128, C, 4)
    d["u"][:, :, :4 * R] = 0
    d["u"][:, :8, :4 * R] = 1
    d["v"][:, :8, :4 * R] = 0
    for kind, lo, hi, n in (("pr", 0, S // 2, K // 2), ("pd", S // 2, S - 1, K - K // 2)):
        p = d[kind].reshape(N, 128, S, 4)
        for a in range(N):
            for i, s in enumerate(lo + rng.permutation(hi - lo)[:R * n]):
                v = rng.integers(4, 8, (56, 4)) * np.exp2(rng.integers(-2, 1, (56, 4))) * rng.choice([-1.0, 1.0], (56, 4))
                o = rng.permutation(N)
                for r in range(N):
                    j = s * N + a + (r if kind == "pd" else 0)
                    g = 1.0 if r == o[0] else -1.0 if r == o[1] else 2.0 ** -26
                    x[r, :8, j] = 256 * 2 ** (R - 1 - i // n)
                    x[r, 8:64, j] = (v * g).astype(np.float32).astype(BF)
                    x[r, 64:, j] = 0
                p[a, 8:64, s] = (v * 2.0 ** -25).astype(np.float32).astype(BF)
        d[kind] = p.reshape(N, 128, 4 * S)
    return {**d, "x": x.reshape(N, 128, 4 * C)}
def setup_inputs_spread(rng):
    d = setup_inputs(rng)
    d["x"] = big(wide(rng, N, 128, 4 * C, cols=6), 1)
    for n in ("pr", "pd"): d[n] = big(wide(rng, N, 128, 4 * S, cols=6), 1)
    return d
def check_inputs(d):
    b = []
    for k in ("x", "pr", "pd", "u", "v"):
        a = np.abs(d[k].astype(np.float32))
        if not (np.isfinite(a).all() and ((a == 0) | (a >= 2.0 ** -30) & (a <= 2.0 ** 30)).all()): b.append("a value of " + k)
    if (d["wc"] != d["wc"][:1]).any(): b.append("wc differs between ranks")
    s = [mx_ref.live(p) for p in d["ws"]]
    if any((p != s[0]).any() for p in s): b.append("ws differs between ranks")
    return b
def reference(x, pr, pd, u, v, wc, ws):
    w = pk(wc[0], ws[0])
    qu, qv = [mx_ref.quantize(u[r]) for r in range(N)], [mx_ref.quantize(v[r]) for r in range(N)]
    data = join(*[mx_ref.quantize(x[r]) for r in range(N)])
    par = join(*[mx_ref.quantize(pr[r]) for r in range(N)], *[mx_ref.quantize(pd[r]) for r in range(N)])
    mine = [C * r + np.arange(C) for r in range(N)]
    own = [np.concatenate([S * r + np.arange(S), C + S * r + np.arange(S)]) for r in range(N)]
    n = N * K
    for t in range(R):
        s = np.zeros(2 * C, np.float32)
        for r in range(N): s[own[r]] = mx_ref.matmul(qv[r], pick(par, own[r]))[t]
        took, rows, diags = [], [], []
        for r in range(N):
            j = np.arange(C)
            a = mx_ref.matmul(qu[r], pick(data, mine[r]))[t]
            z = (a - s[home(j)]) - s[C + home((j - r) % C)]
            e = choose(z + np.float32(0.0))
            took.append(C * r + e)
            rows.append(home(e))
            diags.append(C + home((e - r) % C))
        at = np.concatenate(took)
        old = pick(data, at)
        new = mx_ref.quantize(tile([np.maximum(mx_ref.matmul(pick(w, np.arange(128 * b, 128 * b + 128)), old), np.float32(0.0)) * np.float32(0.0625) for b in range(4)]))
        delta = decode(mx_ref.quantize((decode(new) - decode(old)).astype(BF))).reshape(128, -1, 4)
        p, anew = decode(par).reshape(128, -1, 4), np.zeros(2 * C, bool)
        for r in range(N):
            for h in (rows[r], diags[r]):
                p[:, h] = p[:, h] + delta[:, n * r:n * r + n]
                anew[h] = True
        e = np.flatnonzero(anew)
        par = put(par, e, pick(mx_ref.quantize(np.ascontiguousarray(p.reshape(128, -1).astype(BF))), e))
        data = put(data, at, new)
    y = np.zeros((N, 128, C + 2 * S), np.float32)
    oc, osc = np.zeros((N, 128, 4 * (C + 2 * S)), np.uint8), np.zeros((N, 16, C + 2 * S), np.uint8)
    for r in range(N):
        a, b = pick(data, mine[r]), pick(par, own[r])
        y[r] = np.concatenate([mx_ref.matmul(qu[r], a), mx_ref.matmul(qv[r], b)], axis=1)
        oc[r], osc[r] = emit(join(a, b))
    return {"y": y, "oc": oc, "osc": osc}

@@ -1,0 +1,664 @@
+from concourse.bass import DstId, RemoteDMATransfer
+from concourse.mybir import dt, AluOpType, AxisListType, ActivationFunctionType
+
+ALU = AluOpType
+ACT = ActivationFunctionType
+NR, C, S, R = 8, 384, 48, 3
+BIG = 1.0e29
+KP = 1024.0
+KS = 131072.0
+US = 2 * KS
+YO = 464
+PN = 224
+ZC = 192
+
+SCRATCH = {}
+
+
+def _pair(name, n):
+    SCRATCH[name + "q"] = ("sbuf", [128, n], "float8_e4m3fn_x4")
+    SCRATCH[name + "s"] = ("sbuf", [128, n], "uint8")
+
+
+for _n, _w in (("xn", 384), ("pin", 128), ("v3", 152), ("u3", 224), ("vn", 128), ("un", 128), ("ep", 512), ("em", 512),
+               ("wt", 512), ("D0", 528), ("D1", 528), ("D2", 528), ("D3", 384), ("Dn", 384),
+               ("N0", 528), ("N1", 528), ("N2", 384), ("L0", 528), ("L1", 528), ("L2", 384),
+               ("P0", 352), ("P1", 352), ("P2", 352), ("P3", 128)):
+    _pair(_n, _w)
+for _t in range(R):
+    _pair("S%d" % _t, 64)
+    _pair("G%d" % _t, 72)
+    _pair("H%d" % _t, 192)
+    SCRATCH["la%d" % _t] = ("sbuf", [128, 64], "float32")
+    SCRATCH["ms%d" % _t] = ("sbuf", [128, 32], "float32")
+    SCRATCH["osn%d" % _t] = ("sbuf", [128, 4], "uint16")
+    SCRATCH["oup%d" % _t] = ("sbuf", [128, 32], "uint16")
+    SCRATCH["ow%d" % _t] = ("sbuf", [128, 16], "uint16")
+    SCRATCH["oar%d" % _t] = ("sbuf", [128, 14], "uint16")
+for _n, _w in (("xt", 1536), ("pt", 512), ("vsm", 16), ("usm", 16), ("vt", 608), ("ut", 896), ("vf", 512), ("uf", 512),
+               ("et", 1040), ("ht", 1536), ("nt", 512)):
+    SCRATCH[_n] = ("sbuf", [128, _w], "bfloat16")
+for _n, _w in (("lb", 12), ("msb", 32), ("cf", 20), ("kf", 904), ("tt", 168), ("tb", 504), ("yb", 480),
+               ("nn", 192), ("z1", 224), ("z2", 224), ("w1", 272), ("w2", 272), ("ff", 160), ("sa", 320),
+               ("sb", 128), ("wr", 256), ("wx", 448), ("up", 384), ("kp", 64)):
+    SCRATCH[_n] = ("sbuf", [128, _w], "float32")
+for _n, _w in (("ci", 16), ("ia", 128), ("ib", 128), ("si", 144)):
+    SCRATCH[_n] = ("sbuf", [128, _w], "int32")
+for _n, _w in (("co", 144), ("opos", 4)):
+    SCRATCH[_n] = ("sbuf", [128, _w], "uint16")
+for _n in ("h0", "h1", "h2", "h3", "pa", "pm", "py", "pz"):
+    SCRATCH[_n] = ("psum", [128, 512], "float32")
+
+SEMAPHORES = (["qv", "qa", "qp", "qg", "sent", "stS", "stA", "ab"] + ["l%d" % _i for _i in range(9)]
+              + ["a%d" % _t for _t in range(R)] + ["b%d" % _t for _t in range(R)])
+
+
+def deal(src, cores, topo):
+    near = [d for d in cores if d != src and d in topo.cores_of(src)]
+    far = [d for d in cores if d != src and d not in near]
+    far.sort(key=lambda d: (topo.mates(src, d), topo.same_plane(src, d), topo.die(d) == topo.die(src)))
+    out = topo.engines(src, far[0])
+    inn = [e for e in topo.engines(src, near[0]) if e not in out]
+
+    def m(es):
+        return sum(1 << e for e in es)
+    a1 = {far[i]: m(out[2 * i:2 * i + 2]) for i in range(4)}
+    a2 = {far[4]: m(out[:4]), far[5]: m(out[4:])}
+    b1 = {far[0]: m(out[0:2]), far[1]: m(out[2:4])}
+    b1.update({far[2 + i]: m(out[4 + i:5 + i]) for i in range(4)})
+    b2 = {far[0]: m(out[4:6]), far[1]: m(out[6:8])}
+    b2.update({far[2 + i]: m(out[i:i + 1]) for i in range(4)})
+    for tab in (a1, b1, b2):
+        tab[near[0]] = m(inn[:2])
+    return a1, a2, b1, b2
+
+
+def bits(x):
+    return bin(x).count("1")
+
+
+def rank_program(g, core, T, topo):
+    m = T.rank_of(core)
+    if m is None:
+        return
+    cores = list(T.cores)
+    eng = {"v": g.vector, "a": g.scalar, "p": g.tensor, "g": g, "s": g.sync}
+    qsem = {"v": "qv", "a": "qa", "p": "qp", "g": "qg"}
+
+    ops, touch, clock, seq = [], {}, {q: {} for q in eng}, {q: 0 for q in eng}
+
+    def V(name, c0, c1, step=1, p0=0, p1=128):
+        return (name, p0, p1, c0, c1, step)
+
+    def ap(v):
+        if v[5] == 1:
+            return T[v[0]][v[1]:v[2], v[3]:v[4]]
+        return T[v[0]][v[1]:v[2], v[3]:v[4]:v[5]]
+
+    def meet(a, b):
+        if SCRATCH[a[0]][0] == "psum":
+            return True
+        if a[2] <= b[1] or b[2] <= a[1] or a[4] <= b[3] or b[4] <= a[3]:
+            return False
+        if a[5] == 1 and b[5] == 1:
+            return True
+        return bool(set(range(a[3], a[4], a[5])) & set(range(b[3], b[4], b[5])))
+
+    def add(q, fn, reads, writes, sem=None, count=16):
+        o = {"q": q, "fn": fn, "waits": [], "inc": False, "sem": sem}
+        need = {}
+        for v, wr in [(v, False) for v in reads] + [(v, True) for v in writes]:
+            ps = SCRATCH[v[0]][0] == "psum"
+            for u, uw, x in touch.get(v[0], []):
+                if (wr or uw or ps) and meet(u, v) and not (ps and q == "p" and x["q"] == "p"):
+                    k, n = x["tok"]
+                    if k not in need or need[k]["tok"][1] < n:
+                        need[k] = x
+        if q is not None:
+            known = clock[q]
+            for x in sorted(need.values(), key=lambda y: -y["at"]):
+                k, n = x["tok"]
+                if known.get(k, 0) < n:
+                    o["waits"].append(x)
+                    x["inc"] = True
+                    for kk, nn in list(x["clock"].items()) + [(k, n)]:
+                        if known.get(kk, 0) < nn:
+                            known[kk] = nn
+            o["clock"] = dict(known)
+        else:
+            o["clock"] = {}
+        if sem is None:
+            seq[q] += 1
+            o["tok"] = (q, seq[q])
+        else:
+            o["tok"] = ("#" + sem, count)
+        o["at"] = len(ops)
+        ops.append(o)
+        for v in reads:
+            touch.setdefault(v[0], []).append((v, False, o))
+        for v in writes:
+            touch.setdefault(v[0], []).append((v, True, o))
+        return o
+
+    def sc(x):
+        return ap(x) if isinstance(x, tuple) else x
+
+    def src(v, off):
+        return ap(v) if off is None else ap(v).indirect(ap(off))
+
+    def vs(*xs):
+        return [x for x in xs if isinstance(x, tuple)]
+
+    def ts(out, a, s1, op0, s2=None, op1=None, off=None):
+        if op1 is None:
+            add("v", lambda: g.vector.tensor_scalar(ap(out), src(a, off), sc(s1), None, op0), vs(a, s1, off), [out])
+        else:
+            add("v", lambda: g.vector.tensor_scalar(ap(out), src(a, off), sc(s1), sc(s2), op0, op1), vs(a, s1, s2, off), [out])
+
+    def tt(out, a, b, op, off=None):
+        add("v", lambda: g.vector.tensor_tensor(ap(out), src(a, off), ap(b), op), vs(a, b, off), [out])
+
+    def cp(out, a, off=None):
+        add("v", lambda: g.vector.tensor_copy(ap(out), src(a, off)), vs(a, off), [out])
+
+    def scat(win, off, a):
+        add("v", lambda: g.vector.tensor_copy(src(win, off), ap(a)), [a, off], [win])
+
+    def act(out, a, func, scale=1.0, off=None, bias=None):
+        if bias is not None:
+            add("a", lambda: g.scalar.activation(ap(out), ap(a), func, bias=ap(bias), scale=scale), [a, bias], [out])
+        elif scale == 1.0:
+            add("a", lambda: g.scalar.activation(ap(out), src(a, off), func), vs(a, off), [out])
+        else:
+            add("a", lambda: g.scalar.activation(ap(out), src(a, off), func, scale=scale), vs(a, off), [out])
+
+    def scan(out, d0, d1, init, op0, op1):
+        add("v", lambda: g.vector.tensor_tensor_scan(ap(out), ap(d0), ap(d1), sc(init), op0, op1), vs(d0, d1, init), [out])
+
+    def tr(out, a):
+        add("v", lambda: g.vector.transpose(ap(out), ap(a)), [a], [out])
+
+    def mset(out, x):
+        add("v", lambda: g.vector.memset(ap(out), x), [], [out])
+
+    def iota(out, pat, base=0, mult=0):
+        if SCRATCH[out[0]][2] == "int32":
+            add("g", lambda: g.iota(ap(out), pat, base, mult), [], [out])
+        else:
+            add("g", lambda: g.iota(ap(out), pat, base, mult, allow_small_or_imprecise_dtypes=True), [], [out])
+
+    def fill(out, x):
+        iota(out, [[0, len(range(out[3], out[4], out[5]))]], x)
+
+    def quant(name, c0, tile, n, e0=0):
+        q, s, a = V(name + "q", c0, c0 + n), V(name + "s", c0, c0 + n), V(tile, e0, e0 + 4 * n)
+        add("v", lambda: g.vector.quantize_mx(ap(q), ap(s), ap(a)), [a], [q, s])
+
+    def mm(bank, st, s0, mv, m0, n, start, stop):
+        o = V(bank, 0, n)
+        r = [V(st + "q", s0, s0 + 128), V(st + "s", s0, s0 + 128), V(mv + "q", m0, m0 + n), V(mv + "s", m0, m0 + n)]
+        add("p", lambda: g.tensor.matmul_mx(ap(o), ap(r[0]), ap(r[1]), ap(r[2]), ap(r[3]), start, stop), r, [o])
+
+    def pickq(dst, d0, frm, wide, off):
+        oq, iq = V(dst + "q", d0, d0 + 16 * (off[4] - off[3])), V(frm + "q", 0, wide)
+        add("v", lambda: g.vector.tensor_copy(ap(oq).bitcast(dt.uint32), ap(iq).bitcast(dt.uint32).indirect(ap(off))), [iq, off], [oq])
+
+    def picks(dst, d0, frm, wide, off):
+        o2, i2 = V(dst + "s", d0, d0 + 16 * (off[4] - off[3])), V(frm + "s", 0, wide)
+        add("a", lambda: g.scalar.activation(ap(o2), ap(i2).indirect(ap(off)), ACT.Copy), [i2, off], [o2])
+
+    def pick(*a):
+        pickq(*a)
+        picks(*a)
+
+    def dma(q, sem, fo, fi, reads, writes):
+        add(q, lambda: eng[q].dma_start(fo(), fi()), reads, writes, sem=sem)
+
+    plans = {c: deal(c, cores, topo) for c in cores}
+    sent = [0]
+
+    def push(tab, sem, frm, to, code=False):
+        items = [(d, frm((T.rank_of(d) - m) % NR), to((m - T.rank_of(d)) % NR)) for d in tab]
+
+        def fn():
+            trs = []
+            for d, u, v in items:
+                rid, pid = topo.addr(d, core)
+                a, b = ap(u), ap(v)
+                if code:
+                    a, b = a.bitcast(dt.uint8), b.bitcast(dt.uint8)
+                trs.append(RemoteDMATransfer(dst_ids=[DstId(rid=rid, pnc=pid)], dma_engine_mask=tab[d], remote_sem=T.sem[sem], src=a, dst=b))
+            return g.remote_dma_fused(trs, local_sem=T.sem["sent"])
+        o = add("g", fn, [u for d, u, v in items], [], sem="sent")
+        o["remote"] = True
+        sent[0] += sum(bits(x) for x in tab.values())
+
+    def arrive(sem, which, writes):
+        n = sum(bits(plans[c][w].get(core, 0)) for c in cores if c != core for w in which)
+        add(None, None, [], writes, sem=sem, count=n)
+
+    a1, a2, b1, b2 = plans[core]
+
+    def load(q, sem, dst, fi, after=()):
+        dma(q, sem, lambda: ap(dst), fi, list(after), [dst])
+    load("s", "l0", V("pt", 0, 192), lambda: T.pr[:])
+    load("a", "l1", V("pt", 192, 384), lambda: T.pd[:])
+    load("s", "l2", V("vsm", 0, 16), lambda: T.v[:, 0:16])
+    load("a", "l3", V("usm", 0, 16), lambda: T.u[:, 0:16])
+    load("s", "l4", V("xt", 0, 1536), lambda: T.x[:])
+    dma("s", "l5", lambda: T["wtq"][:].bitcast(dt.uint8), lambda: T.wc[:], [], [V("wtq", 0, 512)])
+    load("s", "l6", V("wts", 0, 512), lambda: T.ws[:])
+
+    def ci(k):
+        return V("ci", k, k + 1)
+
+    def cf(k, p0=0, p1=128):
+        return V("cf", k, k + 1, 1, p0, p1)
+
+    def ib(c0, c1):
+        return V("ib", c0, c1)
+
+    def co(k, n):
+        return V("co", k, k + n)
+
+    def kf(k, n, st=1, P=128):
+        return V("kf", k, k + n, st, 0, P)
+    PP, I16, Q4, HI, P31, UP, PAR, I8, K1, R8, K8 = range(11)
+    O_ARR, O_ARX, O_M0, O_M, O_CM, O_WL, O_U = 0, 14, 28, 30, 32, 62, 76
+    O_C0, O_C1, O_SG, O_UP, O_NAT = 82, 92, 102, 106, 114
+    NI, TG, SP, K4, WS, C224, ONE, C97, TK = 0, 96, 224, 360, 488, 540, 604, 636, 704
+    iota(ci(PP), [[0, 1]], 0, 1)
+    iota(V("ia", 0, 14), [[16, 14]])
+    iota(V("ia", 14, 28), [[32, 7], [0, 2]])
+    iota(V("ia", 28, 30), [[4, 2]])
+    mset(V("et", 0, 516), 1.0)
+    mset(V("pt", 384, 512), 0.0)
+    mset(V("vt", 0, 608), 0.0)
+    iota(V("ia", 30, 54), [[1, 8], [128, 3]])
+    iota(V("ia", 54, 60), [[1, 2], [128, 3]])
+    add("g", lambda: g.affine_select(T["et"][:, 0:516], T["et"][:, 0:516], [[-1, 516]], ALU.is_equal, 0.0, 3, 4), [V("et", 0, 516)], [V("et", 0, 516)])
+    iota(kf(NI, 96), [[1, 96]])
+    iota(V("ia", 60, 64), [[16, 2], [0, 2]])
+    act(V("et", 520, 1036), V("et", 0, 516), ACT.Copy, -1.0)
+
+    def field(k, sh, an):
+        ts(ci(k), ci(PP), sh, ALU.arith_shift_right, an, ALU.bitwise_and)
+    for k, sh, an in ((I16, 0, 15), (Q4, 0, 3), (HI, 2, 3), (P31, 0, 31)):
+        field(k, sh, an)
+    ts(ci(UP), ci(PP), float(S), ALU.is_ge)
+    cp(V("cf", 0, 6), V("ci", 0, 6))
+    n_, a_, b_, c_ = ib(0, 28), ib(28, 56), ib(56, 84), ib(84, 112)
+    kk, d_, e_, f_, h_ = ib(112, 114), ib(114, 116), ib(116, 118), ib(118, 120), ib(120, 122)
+    ts(ib(0, 14), V("ia", 0, 14), cf(I16), ALU.add)
+    ts(ib(14, 28), V("ia", 14, 28), cf(P31), ALU.add)
+    ts(kk, V("ia", 28, 30), cf(HI), ALU.add)
+    ts(cf(11), cf(Q4), 1.0, ALU.is_equal, cf(UP), ALU.subtract)
+    ts(cf(12), cf(Q4), 0.0, ALU.is_equal, cf(UP), ALU.mult)
+    ts(a_, n_, 96.0, ALU.is_ge, -49.0, ALU.mult)
+    ts(b_, n_, 96.0, ALU.is_equal, 48.0, ALU.mult)
+    ts(c_, n_, 144.0, ALU.is_ge, -95.0, ALU.mult)
+    ts(d_, kk, float(m), ALU.add)
+    ts(cf(11), cf(11), 0.0, ALU.max)
+    tt(a_, a_, b_, ALU.add)
+    tt(c_, c_, n_, ALU.add)
+    ts(d_, d_, 7, ALU.bitwise_and)
+    ts(b_, n_, 192.0, ALU.is_ge, 1000.0, ALU.mult)
+    tt(a_, a_, c_, ALU.add)
+    ts(e_, d_, float(8 - m), ALU.is_ge, 1.0, ALU.add)
+    ts(f_, d_, float(m), ALU.is_lt, cf(12), ALU.mult)
+    tt(a_, a_, b_, ALU.add)
+    ts(e_, e_, cf(11), ALU.mult)
+    ts(co(O_ARR, 28), a_, 96.0, ALU.min)
+    tt(e_, e_, f_, ALU.add)
+    for t in range(R):
+        cp(V("vt", 32 * (t + 1), 32 * (t + 1) + 4), V("vsm", 4 * t, 4 * t + 4))
+    cp(co(O_M0, 2), e_)
+
+    def scores(t, lst):
+        la = "la%d" % t
+        for j in range(3):
+            mm("pm", "P%d" % t, S * j, "v3", 8 * (t + 1) - 2 * j, 128, j == 0, j == 2)
+        cp(V(la, 0, 3), V("pm", 0, 5, 2))
+        cp(V("ms%d" % t, 0, 32), V(la, 0, 36 if t else 3), co(lst, 2))
+        w = 3 if t else 2
+        base = 40 - w
+        for tab in (a1, a2):
+            push(tab, "a%d" % t, lambda dl: V("ms%d" % t, 4 * dl, 4 * dl + w), lambda dl: V(la, base + w * dl, base + w * dl + w))
+        arrive("a%d" % t, (0, 1), [V(la, 40, 40 + 7 * w)])
+        cp(V(la, base, 40), V("ms%d" % t, 0, w))
+
+    def own_products(t):
+        for k in range(NR):
+            mm("pa", "D%d" % t, S * k, "u3", 32 * (t + 1) - 4 * k, 128, k == 0, k == NR - 1)
+
+    def own_scores(t):
+        act(V("la%d" % t, 4, 36), V("pa", 0, 32), ACT.Copy)
+        act(V("nn", 160, 192), V("pa", 0, 32), ACT.Copy)
+
+    quant("pin", 0, "pt", 128)
+    quant("v3", 0, "vt", 152)
+    pick("P0", 0, "pin", 128, co(O_ARR, 14))
+    ts(cf(15), cf(I16), 8.0, ALU.mult)
+    for t in range(R):
+        ts(co(O_U + 2 * t, 1), ci(Q4), float(4 * t), ALU.add)
+    scores(0, O_M0)
+    mset(V("ut", 0, 896), 0.0)
+    ts(co(O_CM, 30), V("ia", 30, 60), cf(15), ALU.add)
+
+    for buf, c0, c1, st, x in (("la0", 3, 4, 1, 0), ("la0", 36, 38, 1, 0), ("lb", 0, 3, 1, 0), ("w1", 155, 192, 1, 0), ("ib", 12, 14, 1, 2)):
+        fill(V(buf, c0, c1, st), x)
+    iota(V("ia", 64, 72), [[4, 8]])
+    iota(kf(TG, 96), [[16, 24], [0, 4]])
+    iota(kf(TG + 96, 32), [[16, 8], [0, 4]])
+    fill(V("w2", 155, 192), 0)
+    fill(kf(ONE, 32), int(KS))
+
+    H = ["h0", "h1", "h2", "h3"]
+
+    def rewrite(t, c0, n):
+        for b in range(4):
+            mm(H[b], "wt", 128 * b, "D%d" % t, c0, n, True, True)
+            act(V("ht", b, 4 * n, 4), V(H[b], 0, n), ACT.Relu, 0.0625)
+
+    def differ(t, c0, n):
+        quant("N%d" % t, c0, "ht", n)
+        for b in range(4):
+            mm(H[b], "ep", 128 * b, "N%d" % t, c0, n, True, False)
+            mm(H[b], "em", 128 * b, "D%d" % t, c0, n, False, True)
+            act(V("ht", b, 4 * n, 4), V(H[b], 0, n), ACT.Copy)
+
+    for t in range(R):
+        act(V("ut", 128 * (t + 1), 128 * (t + 1) + 16), V("usm", 0, 16), ACT.Copy, off=co(O_U + 2 * t, 1))
+    quant("xn", 0, "xt", C)
+    pick("D0", 0, "xn", C, co(O_CM, 29))
+    quant("u3", 0, "ut", 224)
+    own_products(0)
+    own_scores(0)
+    rewrite(0, 0, C)
+    ts(cf(13), cf(UP), float(-1 - m), ALU.mult, float(m + 8), ALU.add)
+    ts(cf(14), cf(Q4), 2.0, ALU.is_equal, 4.0, ALU.mult)
+    field(PAR, 4, 1)
+    ts(h_, d_, cf(13), ALU.add)
+    field(I8, 3, 1)
+    ts(h_, h_, 7, ALU.bitwise_and)
+    field(K1, 2, 1)
+    ts(h_, h_, 1.0, ALU.add, cf(14), ALU.mult)
+    field(R8, 2, 7)
+    tt(h_, h_, e_, ALU.add)
+    field(K8, 0, 7)
+    cp(co(O_M, 2), h_)
+    cp(V("cf", 6, 11), V("ci", 6, 11))
+    cp(V("msb", 0, 32), V("la0", 0, 36), co(O_M, 2))
+    for tab in (a1, a2):
+        push(tab, "ab", lambda dl: V("msb", 4 * dl + 2, 4 * dl + 3), lambda dl: V("lb", 3 + dl, 4 + dl))
+    arrive("ab", (0, 1), [V("lb", 4, 11)])
+    for b in range(4):
+        quant("ep", 128 * b, "et", 128, 3 - b)
+    for b in range(4):
+        quant("em", 128 * b, "et", 128, 523 - b)
+    k = 0
+    while k < 11:
+        dl = (k - m) % NR
+        n = min(NR - dl, 11 - k)
+        iota(kf(SP + 12 * k, 12 * n), [[8, n], [0, 3], [1, 4]], YO + 8 * dl)
+        k += n
+    iota(kf(K4, 128), [[0, 32], [1000, 4]])
+    iota(kf(C224, 64), [[1, 64]], PN)
+    iota(kf(C97, 64), [[1, 64]], 97)
+    fill(V("si", 64, 130, 65), -1)
+    fill(kf(TK, 200), 0)
+    fill(kf(TK + ZC, 1), 1)
+    iota(V("tb", 0, 168), [[1, 168]])
+    fill(V("tb", 96, 97), ZC)
+    fill(V("la1", 3, 37, 33), 0)
+
+    lo_, hi_ = ib(8, 12), ib(12, 16)
+    ts(cf(15), cf(R8), 48.0, ALU.mult)
+    cp(co(O_WL, 14), ib(14, 28))
+    ts(ib(0, 2), kk, float(8 - m), ALU.add)
+    ts(ib(2, 4), kk, float(16 - 2 * m), ALU.add)
+    cp(ib(4, 6), kk)
+    ts(ib(6, 8), kk, -1.0, ALU.mult, 8.0, ALU.add)
+    ts(ib(10, 12), kk, float(8 - m), ALU.is_ge, 1.0, ALU.add)
+    differ(0, 0, C)
+    ts(cf(11), cf(PAR), 2.0, ALU.mult, cf(I8), ALU.add)
+    ts(cf(12), cf(K1), float(4 * m), ALU.mult, cf(Q4), ALU.add)
+    ts(ib(0, 8), ib(0, 8), 7, ALU.bitwise_and)
+    act(V("tt", 0, 84), kf(NI, 84), ACT.Identity, 1.0, None, cf(15))
+    ts(cf(11), cf(11), 4.0, ALU.mult, cf(12), ALU.add)
+    for lv in range(3):
+        ts(V("z1", 13 + lv, 14 + lv), cf(Q4), float(3 - lv), ALU.is_ge, -0.5, ALU.add)
+    ts(ib(20, 24), V("ia", 60, 64), cf(11), ALU.add, float(4 * m), ALU.add)
+    mset(kf(WS, 52), 1.0)
+    ts(V("z1", 13, 16), V("z1", 13, 16), 2.0 * BIG, ALU.mult)
+    ts(ib(20, 24), ib(20, 24), 31, ALU.bitwise_and)
+    mset(V("sb", 64, 112), -BIG)
+    cp(co(O_SG, 4), ib(20, 24))
+    mset(kf(WS + 3, 1), -1.0)
+
+    def lists(o, w):
+        base = 40.0 - w
+        ts(co(o, 2), ib(0, 2), float(w), ALU.mult, base, ALU.add)
+        ts(ib(8, 10), ib(4, 6), float(w), ALU.mult, base, ALU.add)
+        ts(ib(14, 16), ib(6, 8), float(w), ALU.mult, base, ALU.add)
+        ts(co(o + 2, 2), ib(2, 4), float(w), ALU.mult, base + 1, ALU.add)
+        tt(ib(16, 20), hi_, lo_, ALU.subtract)
+        if w == 2:
+            ts(co(o + 4, 2), ib(0, 2), 3.0, ALU.add)
+        else:
+            ts(co(o + 4, 2), ib(0, 2), 3.0, ALU.mult, base + 2, ALU.add)
+        ts(ib(16, 20), ib(16, 20), cf(UP), ALU.mult)
+        tt(ib(16, 20), ib(16, 20), lo_, ALU.add)
+        cp(co(o + 6, 4), ib(16, 20))
+    lists(O_C0, 2)
+    act(kf(TG, 128), kf(TG, 128), ACT.Identity, 1.0, None, cf(I16))
+    ts(ib(24, 25), ci(R8), float(8 - m), ALU.add)
+    ts(cf(16), cf(R8), 128.0, ALU.mult, cf(Q4), ALU.add)
+    ts(cf(13), cf(R8), float(8 - m), ALU.is_ge, -KP, ALU.mult)
+    ts(cf(14), cf(PP), 32.0, ALU.is_ge)
+    ts(ib(24, 25), ib(24, 25), 7, ALU.bitwise_and)
+    ts(cf(17), cf(R8), float(m), ALU.not_equal, 8.0, ALU.mult)
+    ts(cf(13), cf(13), KP * S + 4, ALU.add, cf(14), ALU.mult)
+    ts(cf(18), ib(24, 25), 8.0, ALU.mult, cf(16), ALU.add)
+    ts(cf(14), cf(14), KP * S, ALU.mult)
+    ts(V("up", 0, 8), V("ia", 64, 72), cf(HI), ALU.add, -1.0, ALU.add)
+    ts(cf(13), cf(13), cf(17), ALU.add, cf(18), ALU.add)
+    ts(V("up", 8, 16), V("up", 0, 8), 1.0 / 3.0, ALU.mult)
+    quant("L0", 0, "ht", C)
+    cp(V("z2", 13, 16), V("z1", 13, 16))
+    act(V("tt", 84, 168), kf(NI, 84), ACT.Identity, KP, None, cf(13))
+    cp(ib(24, 32), V("up", 8, 16))
+    cp(V("lb", 3, 4), V("msb", 2, 3))
+    ts(ib(24, 32), ib(24, 32), 7, ALU.bitwise_and)
+    mset(V("ow0", 12, 16), ZC)
+    ts(co(O_UP, 8), ib(24, 32), 4.0, ALU.mult, cf(Q4), ALU.add)
+    mset(V("nt", 256, 512), 0.0)
+
+    def later(t):
+        if t == 0:
+            iota(V("tb", 168, 504), [[0, 2], [1, 168]])
+            fill(V("tb", 264, 504, 168), ZC)
+            fill(V("la2", 3, 37, 33), 0)
+            iota(V("ia", 72, 96), [[2, 24]])
+            lists(O_C1, 3)
+            ts(cf(19), cf(K8), 48.0, ALU.mult, cf(I8), ALU.add)
+            for x in range(1, R):
+                mset(V("ow%d" % x, 12, 16), ZC)
+        else:
+            quant("un", 0, "uf", 128)
+            quant("vn", 0, "vf", 128)
+            ts(co(O_NAT, 24), V("ia", 72, 96), cf(19), ALU.add)
+
+    def top(z, w, P, t0):
+        def Z(c0, c1, st=1):
+            return V(z, c0, c1, st, 0, P)
+
+        def W(c0, c1):
+            return V(w, c0, c1, 1, 0, P)
+        sc0 = Z(160, 208)
+        scan(Z(16, 160, 3), sc0, V("sb", 64, 112, 1, 0, P), Z(13, 14), ALU.min, ALU.max)
+        scan(Z(17, 160, 3), sc0, Z(13, 157, 3), Z(14, 15), ALU.min, ALU.max)
+        scan(Z(18, 160, 3), sc0, Z(14, 158, 3), Z(15, 16), ALU.min, ALU.max)
+        scan(W(0, 48), sc0, Z(15, 159, 3), BIG, ALU.min, ALU.max)
+        ts(W(48, 99), Z(157, 208), W(47, 48), ALU.is_equal, US, ALU.mult)
+        scan(W(104, 155), kf(WS, 51, 1, P), W(48, 99), -US, ALU.mult, ALU.subtract)
+        scan(W(192, 272), W(107, 187), V("tt", t0 + 1, t0 + 81, 1, 0, P), V("tt", t0, t0 + 1, 1, 0, P), ALU.max, ALU.min)
+
+    def Q(name, a, c0, n=32):
+        return V(name, c0, c0 + n, 1, 32 * a, 32 * a + 32)
+
+    def turn(out, n):
+        tr(V("wx", 224, 224 + 16 * n), V("wx", 0, 16 * n))
+        cp(out, V("wx", 224, 224 + 16 * n, 16))
+
+    def A(c0, c1, P=64):
+        return V("sa", c0, c1, 1, 0, P)
+
+    for t in range(R):
+        la, o = "la%d" % t, (O_C1 if t else O_C0)
+        win = V(la, 0, 61 if t else 54)
+        D, N_, L, P, G, HS, SS = ("%s%d" % (x, t) for x in "DNLPGHS")
+        osn, oup, ow, oar = ("%s%d" % (x, t) for x in ("osn", "oup", "ow", "oar"))
+        tt(V("nn", 0, 32), win, V("nn", 160, 192), ALU.subtract, co(o, 2))
+        tt(V("nn", 32, 64), win, V("nn", 0, 32), ALU.add, co(o + 2, 2))
+        tr(Q("z1", 0, 160), Q("nn", 0, 32))
+        tr(Q("z1", 0, 192), Q("nn", 1, 32))
+        top("z1", "w1", 32, 0)
+        for a in range(4):
+            tr(Q("ff", a, 0), Q("w1", 0, 240))
+        cp(V("ff", 32, 96), V("ff", 0, 32), co(O_SG, 4))
+        tr(V("ff", 96, 160), V("ff", 32, 96))
+        cp(V(osn, 0, 4), V("ff", 96, 160, 16))
+        pick(SS, 0, L, C, V(osn, 0, 4))
+        push(b1, "b%d" % t, lambda dl: V(SS + "q", 8 * dl, 8 * dl + 8), lambda dl: V(G + "q", 8 * dl + 8, 8 * dl + 16), True)
+        push(b2, "b%d" % t, lambda dl: V(SS + "s", 8 * dl, 8 * dl + 8), lambda dl: V(G + "s", 8 * dl + 8, 8 * dl + 16))
+        arrive("b%d" % t, (2, 3), [V(G + "q", 16, 72), V(G + "s", 16, 72)])
+        if t == 0:
+            load("s", "l7", V("uf", 0, 512), lambda: T.u[:], [V(G + "s", 16, 72)])
+            load("s", "l8", V("vf", 0, 512), lambda: T.v[:])
+        if t:
+            cp(V("nn", 64, 96), win, co(o + 4, 2))
+        pick(D, YO, N_, C, V(osn, 0, 4))
+        pick(G, 0, L, C, V(osn, 0, 1))
+        if t < R - 1:
+            rewrite(t, YO - 64, 128)
+        if not t:
+            cp(V("nn", 64, 96), V("lb", 0, 11), co(o + 4, 2))
+        tt(V("nn", 96, 128), win, V("nn", 64, 96), ALU.subtract, co(o + 6, 2))
+        tt(V("nn", 128, 160), win, V("nn", 96, 128), ALU.add, co(o + 8, 2))
+        tr(Q("z2", 0, 144), Q("nn", 1, 128))
+        tr(Q("z2", 0, 176), Q("nn", 2, 128))
+        tr(Q("z2", 1, 160), Q("nn", 0, 128))
+        tr(Q("z2", 1, 192), Q("nn", 1, 128))
+        top("z2", "w2", 64, 84)
+        key = V("w2", 240, 272, 1, 0, 64)
+        ts(A(0, 32), key, cf(14, 0, 64), ALU.is_lt, KP * S, ALU.mult)
+        tt(A(32, 64), A(0, 32), key, ALU.add)
+        for a in range(2):
+            for b in range(2):
+                tr(Q("sa", a, 64 + 32 * b), Q("sa", b, 32))
+        ts(A(128, 192), A(64, 128), A(32, 33), ALU.is_lt)
+        add("v", lambda: g.vector.tensor_reduce(ap(A(192, 193)), ap(A(128, 192)), AxisListType.X, ALU.add), [A(128, 192)], [A(192, 193)])
+        ts(A(200, 232), kf(ONE, 32, 1, 64), A(192, 193), ALU.mult, A(32, 33), ALU.add)
+        for b in range(2):
+            tr(Q("sa", 0, 256 + 32 * b), Q("sa", b, 200))
+        add("g", lambda: g.partition_broadcast(T["sb"][:, 0:64], T["sa"][0:1, 256:320], 128), [V("sa", 256, 320, 1, 0, 1)], [V("sb", 0, 64)])
+        tt(V("up", 0, 128), V("ff", 0, 32), kf(TG, 128), ALU.is_equal, co(O_UP, 8))
+        tt(V("up", 128, 256), V("up", 0, 128), kf(SP, 128), ALU.mult)
+        scan(V("up", 256, 384), kf(K4, 128), V("up", 128, 256), 0.0, ALU.min, ALU.max)
+        cp(V("wx", 0, 64), V("sb", 0, 64), co(O_WL, 4))
+        tt(V("up", 0, 32), V("up", 259, 384, 4), kf(TG, 128, 4), ALU.max)
+        tr(V("wx", 224, 288), V("wx", 0, 64))
+        cp(V(oup, 0, 32), V("up", 0, 32))
+        cp(V("si", 132, 136), V("wx", 224, 288, 16))
+        nd = 29 if t < R - 1 else 24
+        picks("D%d" % (t + 1), 0, D, 528, V(oup, 0, nd))
+        ts(V("si", 136, 140), V("si", 132, 136), 17, ALU.arith_shift_right)
+        cp(V("opos", 0, 4), V("si", 136, 140))
+        scat(V("si", 0, 64), V("opos", 0, 4), V("sb", 0, 64))
+        pl, same, kp = V("si", 65, 129), V("wr", 192, 256), V("kp", 0, 64)
+        ts(pl, V("si", 0, 64), 10, ALU.arith_shift_right, 127, ALU.bitwise_and)
+        ts(ib(32, 96), V("si", 0, 64), 127, ALU.bitwise_and)
+        tt(same, pl, V("si", 64, 128), ALU.is_equal)
+        tt(A(0, 64, 128), pl, V("si", 66, 130), ALU.is_equal)
+        cp(V("wr", 0, 64), ib(32, 96))
+        ts(A(128, 192, 128), same, float(ZC), ALU.mult)
+        tt(A(64, 128, 128), kf(C97, 64), A(0, 64, 128), ALU.mult)
+        tt(V("wr", 128, 192), A(128, 192, 128), pl, ALU.max)
+        tt(V("wr", 64, 128), A(64, 128, 128), pl, ALU.max)
+        act(V("wx", 0, 192), V("wr", 0, 192), ACT.Copy, off=co(O_WL, 12))
+        pickq("D%d" % (t + 1), 0, D, 528, V(oup, 0, nd))
+        if t < R - 1:
+            own_products(t + 1)
+        turn(V(ow, 0, 12), 12)
+        tb = V("tb", 168 * t, 168 * t + 161)
+        scat(tb, V(ow, 4, 8), kf(C224, 64))
+        pick(HS, 64, P, PN, V(ow, 8, 16))
+        for b in range(4):
+            mm(H[b], "ep", 128 * b, HS, 64, 128, True, False)
+        na = 14 if t < R - 1 else 8
+        act(V("wx", 0, 16 * na), tb, ACT.Copy, off=co(O_ARX, na))
+        cp(kp, kf(TK, 200), V(ow, 8, 12))
+        if t < R - 1:
+            turn(V(oar, 0, na), na)
+        else:
+            pick("Dn", 0, "D3", C, co(O_NAT, 24))
+            turn(V(oar, 0, na), na)
+            mm("py", "un", 0, "Dn", 0, C, True, True)
+            dma("s", "stS", lambda: T.oc[:, 0:4 * C], lambda: T["Dnq"][:].bitcast(dt.uint8), [V("Dnq", 0, C)], [])
+            for k in range(4):
+                dma("s", "stS", lambda k=k: T.osc[4 * k:4 * k + 4, 0:C], lambda k=k: T["Dns"][32 * k:32 * k + 4, 0:C], [V("Dns", 0, C)], [])
+        if t < R - 1:
+            act(V("la%d" % (t + 1), 4, 36), V("pa", 0, 32), ACT.Copy)
+        pick(HS, 0, G, 72, V(ow, 0, 4))
+        for b in range(4):
+            mm(H[b], "ep", 128 * b, HS, 0, 128, False, True)
+            scan(V("nt", b, 256, 4), kp, V(H[b], 0, 64), 0.0, ALU.mult, ALU.add)
+        if t == R - 1:
+            act(V("yb", 0, C), V("py", 0, C), ACT.Copy)
+            dma("s", "stS", lambda: T.y[:, 0:C], lambda: T["yb"][:, 0:C], [V("yb", 0, C)], [])
+        else:
+            act(V("nn", 160, 192), V("pa", 0, 32), ACT.Copy)
+        quant(P, PN, "nt", 128)
+        pick("P%d" % (t + 1), 0, P, 352, V(oar, 0, na))
+        if t < R - 1:
+            scores(t + 1, O_M)
+            differ(t, YO - 64, 128)
+            pick("N%d" % (t + 1), 0, N_, 528, V(oup, 0, 24))
+            later(t)
+            quant(L, YO - 64, "ht", 128)
+            pick("L%d" % (t + 1), 0, L, 528, V(oup, 0, 24))
+    mm("pz", "vn", 0, "P3", 0, 128, True, True)
+    dma("s", "stS", lambda: T.oc[:, 4 * C:4 * C + 8 * S], lambda: T["P3q"][:, 0:2 * S].bitcast(dt.uint8), [V("P3q", 0, 2 * S)], [])
+    for k in range(4):
+        dma("a" if k % 2 else "s", "stA" if k % 2 else "stS", lambda k=k: T.osc[4 * k:4 * k + 4, C:C + 2 * S],
+            lambda k=k: T["P3s"][32 * k:32 * k + 4, 0:2 * S], [V("P3s", 0, 2 * S)], [])
+    cp(V("yb", C, C + 2 * S), V("pz", 0, 2 * S))
+    dma("a", "stA", lambda: T.y[:, C:C + 2 * S], lambda: T["yb"][:, C:C + 2 * S], [V("yb", C, C + 2 * S)], [])
+
+    cnt = {q: 0 for q in qsem}
+    stores = {"stS": 0, "stA": 0}
+    for o in ops:
+        if o["sem"] is None and o["inc"]:
+            cnt[o["q"]] += 1
+            o["val"] = cnt[o["q"]]
+    for o in ops:
+        if o["q"] is None:
+            continue
+        for x in o["waits"]:
+            if x["sem"] is None:
+                eng[o["q"]].wait_ge(T.sem[qsem[x["q"]]], x["val"])
+            else:
+                eng[o["q"]].wait_ge(T.sem[x["sem"]], x["tok"][1])
+        ins = o["fn"]()
+        if o.get("remote"):
+            continue
+        if o["sem"] is not None:
+            ins.then_inc(T.sem[o["sem"]], 16)
+            if o["sem"] in stores:
+                stores[o["sem"]] += 16
+        elif o["inc"]:
+            ins.then_inc(T.sem[qsem[o["q"]]], 1)
+    g.sync.wait_ge(T.sem["stS"], stores["stS"])
+    g.scalar.wait_ge(T.sem["stA"], stores["stA"])
+    g.wait_ge(T.sem["sent"], sent[0])

@@ -1,16 +1,15 @@
 from concourse.bass import DstId, RemoteDMATransfer
-from concourse.mybir import dt, AluOpType, AxisListType, ActivationFunctionType
+from concourse.mybir import dt, AluOpType, ActivationFunctionType
 
 ALU = AluOpType
 ACT = ActivationFunctionType
 NR, C, S, R = 8, 384, 48, 3
 BIG = 1.0e29
-KP = 1024.0
-KS = 131072.0
-US = 2 * KS
+US = 262144.0
 YO = 464
-PN = 224
-ZC = 192
+PR = 16
+PN = 240
+LB = 13
 
 SCRATCH = {}
 
@@ -20,36 +19,34 @@ def _pair(name, n):
     SCRATCH[name + "s"] = ("sbuf", [128, n], "uint8")
 
 
-for _n, _w in (("xn", 384), ("pin", 128), ("v3", 152), ("u3", 224), ("vn", 128), ("un", 128), ("ep", 512), ("em", 512),
+for _n, _w in (("Dc", 464), ("v3", 168), ("vn", 128), ("un", 128), ("ep", 512), ("em", 512),
                ("wt", 512), ("D0", 528), ("D1", 528), ("D2", 528), ("D3", 384), ("Dn", 384),
                ("N0", 528), ("N1", 528), ("N2", 384), ("L0", 528), ("L1", 528), ("L2", 384),
-               ("P0", 352), ("P1", 352), ("P2", 352), ("P3", 128)):
+               ("P0", 368), ("P1", 368), ("P2", 368), ("P3", 144)):
     _pair(_n, _w)
 for _t in range(R):
     _pair("S%d" % _t, 64)
-    _pair("G%d" % _t, 72)
+    _pair("G%d" % _t, 128)
     _pair("H%d" % _t, 192)
-    SCRATCH["la%d" % _t] = ("sbuf", [128, 64], "float32")
+    SCRATCH["la%d" % _t] = ("sbuf", [128, 40], "float32")
     SCRATCH["ms%d" % _t] = ("sbuf", [128, 32], "float32")
     SCRATCH["osn%d" % _t] = ("sbuf", [128, 4], "uint16")
     SCRATCH["oup%d" % _t] = ("sbuf", [128, 32], "uint16")
-    SCRATCH["ow%d" % _t] = ("sbuf", [128, 16], "uint16")
-    SCRATCH["oar%d" % _t] = ("sbuf", [128, 14], "uint16")
-for _n, _w in (("xt", 1536), ("pt", 512), ("vsm", 16), ("usm", 16), ("vt", 608), ("ut", 896), ("vf", 512), ("uf", 512),
-               ("et", 1040), ("ht", 1536), ("nt", 512)):
+    SCRATCH["ow%d" % _t] = ("sbuf", [128, 32], "uint16")
+for _n, _w in (("xt", 1536), ("pt", 960), ("vt", 688), ("vf", 512), ("uf", 512),
+               ("et", 1040), ("ht", 1536), ("hu", 1536), ("nt", 512)):
     SCRATCH[_n] = ("sbuf", [128, _w], "bfloat16")
-for _n, _w in (("lb", 12), ("msb", 32), ("cf", 20), ("kf", 904), ("tt", 168), ("tb", 504), ("yb", 480),
-               ("nn", 192), ("z1", 224), ("z2", 224), ("w1", 272), ("w2", 272), ("ff", 160), ("sa", 320),
-               ("sb", 128), ("wr", 256), ("wx", 448), ("up", 384), ("kp", 64)):
+for _n, _w in (("msb", 32), ("cf", 32), ("kf", 1568), ("tt", 84), ("yb", 480), ("nn", 192), ("zz", 224), ("ww", 272),
+               ("ff", 160), ("sa", 112), ("sc", 8), ("oh", 320), ("ot", 320), ("oc2", 320), ("wb", 24), ("wf", 32),
+               ("up", 384), ("kp", 64), ("tm", 128)):
     SCRATCH[_n] = ("sbuf", [128, _w], "float32")
-for _n, _w in (("ci", 16), ("ia", 128), ("ib", 128), ("si", 144)):
+for _n, _w in (("ci", 16), ("ia", 96), ("ib", 64)):
     SCRATCH[_n] = ("sbuf", [128, _w], "int32")
-for _n, _w in (("co", 144), ("opos", 4)):
-    SCRATCH[_n] = ("sbuf", [128, _w], "uint16")
+SCRATCH["co"] = ("sbuf", [128, 96], "uint16")
 for _n in ("h0", "h1", "h2", "h3", "pa", "pm", "py", "pz"):
     SCRATCH[_n] = ("psum", [128, 512], "float32")
 
-SEMAPHORES = (["qv", "qa", "qp", "qg", "sent", "stS", "stA", "ab"] + ["l%d" % _i for _i in range(9)]
+SEMAPHORES = (["qv", "qa", "qp", "qg", "sent", "stS", "stA", "ab"] + ["l%d" % _i for _i in range(12)]
               + ["a%d" % _t for _t in range(R)] + ["b%d" % _t for _t in range(R)])
 
 
@@ -77,6 +74,24 @@ def bits(x):
     return bin(x).count("1")
 
 
+def arrange(ops):
+    hop = 0.15
+    for o in reversed(ops):
+        o["tail"] = o["lat"] + max([hop + x["tail"] for x in o["users"]] + [0.0])
+    busy = {}
+    for o in sorted(ops, key=lambda y: (-y["tail"], y["at"])):
+        t = max([x["start"] + (x["cost"] if x["q"] == o["q"] == "p" or x.get("remote") else x["lat"] + hop) for x in o["deps"]] + [0.0])
+        if o["q"] is not None:
+            line = busy.setdefault(o["q"], [])
+            k = 0
+            while k < len(line) and line[k][0] < t + o["cost"]:
+                t = max(t, line[k][1])
+                k += 1
+            line.insert(k, (t, t + o["cost"]))
+        o["start"] = t
+    return sorted(ops, key=lambda y: (y["start"], y["at"]))
+
+
 def rank_program(g, core, T, topo):
     m = T.rank_of(core)
     if m is None:
@@ -85,7 +100,7 @@ def rank_program(g, core, T, topo):
     eng = {"v": g.vector, "a": g.scalar, "p": g.tensor, "g": g, "s": g.sync}
     qsem = {"v": "qv", "a": "qa", "p": "qp", "g": "qg"}
 
-    ops, touch, clock, seq = [], {}, {q: {} for q in eng}, {q: 0 for q in eng}
+    ops, touch = [], {}
 
     def V(name, c0, c1, step=1, p0=0, p1=128):
         return (name, p0, p1, c0, c1, step)
@@ -94,6 +109,9 @@ def rank_program(g, core, T, topo):
         if v[5] == 1:
             return T[v[0]][v[1]:v[2], v[3]:v[4]]
         return T[v[0]][v[1]:v[2], v[3]:v[4]:v[5]]
+
+    def wide(v):
+        return len(range(v[3], v[4], v[5]))
 
     def meet(a, b):
         if SCRATCH[a[0]][0] == "psum":
@@ -104,35 +122,18 @@ def rank_program(g, core, T, topo):
             return True
         return bool(set(range(a[3], a[4], a[5])) & set(range(b[3], b[4], b[5])))
 
-    def add(q, fn, reads, writes, sem=None, count=16):
-        o = {"q": q, "fn": fn, "waits": [], "inc": False, "sem": sem}
-        need = {}
+    def add(q, fn, reads, writes, cost, lat=None, sem=None, count=16, after=()):
+        o = {"q": q, "fn": fn, "inc": False, "sem": sem, "count": count, "cost": cost, "lat": cost if lat is None else lat,
+             "at": len(ops), "users": [], "deps": list(after)}
+        seen = {x["at"] for x in after}
         for v, wr in [(v, False) for v in reads] + [(v, True) for v in writes]:
             ps = SCRATCH[v[0]][0] == "psum"
             for u, uw, x in touch.get(v[0], []):
-                if (wr or uw or ps) and meet(u, v) and not (ps and q == "p" and x["q"] == "p"):
-                    k, n = x["tok"]
-                    if k not in need or need[k]["tok"][1] < n:
-                        need[k] = x
-        if q is not None:
-            known = clock[q]
-            for x in sorted(need.values(), key=lambda y: -y["at"]):
-                k, n = x["tok"]
-                if known.get(k, 0) < n:
-                    o["waits"].append(x)
-                    x["inc"] = True
-                    for kk, nn in list(x["clock"].items()) + [(k, n)]:
-                        if known.get(kk, 0) < nn:
-                            known[kk] = nn
-            o["clock"] = dict(known)
-        else:
-            o["clock"] = {}
-        if sem is None:
-            seq[q] += 1
-            o["tok"] = (q, seq[q])
-        else:
-            o["tok"] = ("#" + sem, count)
-        o["at"] = len(ops)
+                if x["at"] not in seen and (wr or uw or ps) and meet(u, v) and not (q is None and x["q"] is None):
+                    seen.add(x["at"])
+                    o["deps"].append(x)
+        for x in o["deps"]:
+            x["users"].append(o)
         ops.append(o)
         for v in reads:
             touch.setdefault(v[0], []).append((v, False, o))
@@ -149,76 +150,76 @@ def rank_program(g, core, T, topo):
     def vs(*xs):
         return [x for x in xs if isinstance(x, tuple)]
 
+    def span(out, off=None, k=1):
+        n = wide(out)
+        return 0.05 + 0.0016 * n if off is not None else max(64, k * n) * 0.001
+
     def ts(out, a, s1, op0, s2=None, op1=None, off=None):
         if op1 is None:
-            add("v", lambda: g.vector.tensor_scalar(ap(out), src(a, off), sc(s1), None, op0), vs(a, s1, off), [out])
+            add("v", lambda: g.vector.tensor_scalar(ap(out), src(a, off), sc(s1), None, op0), vs(a, s1, off), [out], span(out, off))
         else:
-            add("v", lambda: g.vector.tensor_scalar(ap(out), src(a, off), sc(s1), sc(s2), op0, op1), vs(a, s1, s2, off), [out])
+            add("v", lambda: g.vector.tensor_scalar(ap(out), src(a, off), sc(s1), sc(s2), op0, op1), vs(a, s1, s2, off), [out], span(out, off))
 
     def tt(out, a, b, op, off=None):
-        add("v", lambda: g.vector.tensor_tensor(ap(out), src(a, off), ap(b), op), vs(a, b, off), [out])
+        add("v", lambda: g.vector.tensor_tensor(ap(out), src(a, off), ap(b), op), vs(a, b, off), [out], span(out, off, 2))
 
     def cp(out, a, off=None):
-        add("v", lambda: g.vector.tensor_copy(ap(out), src(a, off)), vs(a, off), [out])
+        add("v", lambda: g.vector.tensor_copy(ap(out), src(a, off)), vs(a, off), [out], span(out, off))
 
-    def scat(win, off, a):
-        add("v", lambda: g.vector.tensor_copy(src(win, off), ap(a)), [a, off], [win])
-
-    def act(out, a, func, scale=1.0, off=None, bias=None):
+    def act(out, a, func, scale=1.0, off=None, bias=None, acc=None):
+        kw = {}
         if bias is not None:
-            add("a", lambda: g.scalar.activation(ap(out), ap(a), func, bias=ap(bias), scale=scale), [a, bias], [out])
-        elif scale == 1.0:
-            add("a", lambda: g.scalar.activation(ap(out), src(a, off), func), vs(a, off), [out])
-        else:
-            add("a", lambda: g.scalar.activation(ap(out), src(a, off), func, scale=scale), vs(a, off), [out])
+            kw["bias"] = ap(bias)
+        if scale != 1.0:
+            kw["scale"] = scale
+        if acc is not None:
+            kw["accum_out"] = ap(acc)
+        add("a", lambda: g.scalar.activation(ap(out), src(a, off), func, **kw), vs(a, off, bias), vs(out, acc),
+            0.07 + wide(out) * (0.001 if off is None else 0.0016))
 
     def scan(out, d0, d1, init, op0, op1):
-        add("v", lambda: g.vector.tensor_tensor_scan(ap(out), ap(d0), ap(d1), sc(init), op0, op1), vs(d0, d1, init), [out])
+        add("v", lambda: g.vector.tensor_tensor_scan(ap(out), ap(d0), ap(d1), sc(init), op0, op1), vs(d0, d1, init), [out], span(out))
 
     def tr(out, a):
-        add("v", lambda: g.vector.transpose(ap(out), ap(a)), [a], [out])
+        add("v", lambda: g.vector.transpose(ap(out), ap(a)), [a], [out], span(out))
 
     def mset(out, x):
-        add("v", lambda: g.vector.memset(ap(out), x), [], [out])
+        add("v", lambda: g.vector.memset(ap(out), x), [], [out], span(out, None, 0.5 if SCRATCH[out[0]][2] == "bfloat16" else 1))
 
     def iota(out, pat, base=0, mult=0):
         if SCRATCH[out[0]][2] == "int32":
-            add("g", lambda: g.iota(ap(out), pat, base, mult), [], [out])
+            add("g", lambda: g.iota(ap(out), pat, base, mult), [], [out], 0.13 + 0.002 * wide(out))
         else:
-            add("g", lambda: g.iota(ap(out), pat, base, mult, allow_small_or_imprecise_dtypes=True), [], [out])
+            add("g", lambda: g.iota(ap(out), pat, base, mult, allow_small_or_imprecise_dtypes=True), [], [out], 0.13 + 0.002 * wide(out))
 
     def fill(out, x):
-        iota(out, [[0, len(range(out[3], out[4], out[5]))]], x)
+        iota(out, [[0, wide(out)]], x)
 
     def quant(name, c0, tile, n, e0=0):
         q, s, a = V(name + "q", c0, c0 + n), V(name + "s", c0, c0 + n), V(tile, e0, e0 + 4 * n)
-        add("v", lambda: g.vector.quantize_mx(ap(q), ap(s), ap(a)), [a], [q, s])
+        add("v", lambda: g.vector.quantize_mx(ap(q), ap(s), ap(a)), [a], [q, s], 0.02 + 0.0011 * n)
 
     def mm(bank, st, s0, mv, m0, n, start, stop):
         o = V(bank, 0, n)
         r = [V(st + "q", s0, s0 + 128), V(st + "s", s0, s0 + 128), V(mv + "q", m0, m0 + n), V(mv + "s", m0, m0 + n)]
-        add("p", lambda: g.tensor.matmul_mx(ap(o), ap(r[0]), ap(r[1]), ap(r[2]), ap(r[3]), start, stop), r, [o])
+        add("p", lambda: g.tensor.matmul_mx(ap(o), ap(r[0]), ap(r[1]), ap(r[2]), ap(r[3]), start, stop), r, [o], 0.0006 * (n + 16),
+            0.0006 * (n + 16) + 0.06)
 
-    def pickq(dst, d0, frm, wide, off):
-        oq, iq = V(dst + "q", d0, d0 + 16 * (off[4] - off[3])), V(frm + "q", 0, wide)
-        add("v", lambda: g.vector.tensor_copy(ap(oq).bitcast(dt.uint32), ap(iq).bitcast(dt.uint32).indirect(ap(off))), [iq, off], [oq])
+    def pick(dst, d0, frm, n, off):
+        oq, iq = V(dst + "q", d0, d0 + 16 * wide(off)), V(frm + "q", 0, n)
+        add("v", lambda: g.vector.tensor_copy(ap(oq).bitcast(dt.uint32), ap(iq).bitcast(dt.uint32).indirect(ap(off))), [iq, off], [oq],
+            span(oq, off))
+        o2, i2 = V(dst + "s", d0, d0 + 16 * wide(off)), V(frm + "s", 0, n)
+        add("a", lambda: g.scalar.activation(ap(o2), ap(i2).indirect(ap(off)), ACT.Copy), [i2, off], [o2], span(o2, off))
 
-    def picks(dst, d0, frm, wide, off):
-        o2, i2 = V(dst + "s", d0, d0 + 16 * (off[4] - off[3])), V(frm + "s", 0, wide)
-        add("a", lambda: g.scalar.activation(ap(o2), ap(i2).indirect(ap(off)), ACT.Copy), [i2, off], [o2])
-
-    def pick(*a):
-        pickq(*a)
-        picks(*a)
-
-    def dma(q, sem, fo, fi, reads, writes):
-        add(q, lambda: eng[q].dma_start(fo(), fi()), reads, writes, sem=sem)
+    def dma(q, sem, fo, fi, reads, writes, lat=2.0, after=()):
+        return add(q, lambda: eng[q].dma_start(fo(), fi()), reads, writes, 0.06, lat, sem=sem, after=after)
 
     plans = {c: deal(c, cores, topo) for c in cores}
-    sent = [0]
+    sent, calls = [0], []
 
     def push(tab, sem, frm, to, code=False):
-        items = [(d, frm((T.rank_of(d) - m) % NR), to((m - T.rank_of(d)) % NR)) for d in tab]
+        items = [(d, frm(T.rank_of(d)), to(T.rank_of(d))) for d in tab]
 
         def fn():
             trs = []
@@ -229,25 +230,38 @@ def rank_program(g, core, T, topo):
                     a, b = a.bitcast(dt.uint8), b.bitcast(dt.uint8)
                 trs.append(RemoteDMATransfer(dst_ids=[DstId(rid=rid, pnc=pid)], dma_engine_mask=tab[d], remote_sem=T.sem[sem], src=a, dst=b))
             return g.remote_dma_fused(trs, local_sem=T.sem["sent"])
-        o = add("g", fn, [u for d, u, v in items], [], sem="sent")
+        o = add("g", fn, [u for d, u, v in items], [], 0.4 if calls else 3.0, sem="sent", after=calls[-1:])
         o["remote"] = True
+        calls.append(o)
         sent[0] += sum(bits(x) for x in tab.values())
 
-    def arrive(sem, which, writes):
+    def arrive(sem, which, writes, lat):
         n = sum(bits(plans[c][w].get(core, 0)) for c in cores if c != core for w in which)
-        add(None, None, [], writes, sem=sem, count=n)
+        return add(None, None, [], writes, lat, sem=sem, count=n, after=calls[-1:])
 
     a1, a2, b1, b2 = plans[core]
 
-    def load(q, sem, dst, fi, after=()):
-        dma(q, sem, lambda: ap(dst), fi, list(after), [dst])
-    load("s", "l0", V("pt", 0, 192), lambda: T.pr[:])
-    load("a", "l1", V("pt", 192, 384), lambda: T.pd[:])
-    load("s", "l2", V("vsm", 0, 16), lambda: T.v[:, 0:16])
-    load("a", "l3", V("usm", 0, 16), lambda: T.u[:, 0:16])
-    load("s", "l4", V("xt", 0, 1536), lambda: T.x[:])
-    dma("s", "l5", lambda: T["wtq"][:].bitcast(dt.uint8), lambda: T.wc[:], [], [V("wtq", 0, 512)])
-    load("s", "l6", V("wts", 0, 512), lambda: T.ws[:])
+    loads = []
+
+    def load(q, dst, fi, lat=2.0, after=()):
+        loads.append(dma(q, "l%d" % len(loads), lambda: ap(dst), fi, [], [dst], lat, after))
+    e0 = 4 * PR
+    load("s", V("pt", e0, e0 + 192), lambda: T.pr[:])
+    load("a", V("pt", e0 + 192, e0 + 384), lambda: T.pd[:])
+    load("s", V("vt", 32, 48), lambda: T.v[:, 0:16])
+    load("a", V("pt", e0 + 388, e0 + 576), lambda: T.pd[:, 0:188])
+    load("s", V("pt", e0 + 576, e0 + 768), lambda: T.pr[:])
+    load("a", V("pt", e0 + 384, e0 + 388), lambda: T.pd[:, 188:192])
+    load("s", V("xt", 0, 1536), lambda: T.x[:], 3.8)
+    load("a", V("vt", 160, 176), lambda: T.u[:, 0:16])
+    loads.append(dma("s", "l8", lambda: T["wtq"][:].bitcast(dt.uint8), lambda: T.wc[:], [], [V("wtq", 0, 512)], 3.5))
+    load("a", V("wts", 0, 512), lambda: T.ws[:], 2.5)
+    mset(V("pt", 0, e0), 0.0)
+    mset(V("pt", e0 + 768, 960), 0.0)
+    mset(V("vt", 0, 32), 0.0)
+    mset(V("vt", 48, 160), 0.0)
+    mset(V("vt", 176, 688), 0.0)
+    mset(V("nt", 256, 512), 0.0)
 
     def ci(k):
         return V("ci", k, k + 1)
@@ -255,147 +269,193 @@ def rank_program(g, core, T, topo):
     def cf(k, p0=0, p1=128):
         return V("cf", k, k + 1, 1, p0, p1)
 
+    def ia(c0, c1):
+        return V("ia", c0, c1)
+
     def ib(c0, c1):
         return V("ib", c0, c1)
+
+    def tm(c0, c1, st=1):
+        return V("tm", c0, c1, st)
 
     def co(k, n):
         return V("co", k, k + n)
 
-    def kf(k, n, st=1, P=128):
-        return V("kf", k, k + n, st, 0, P)
-    PP, I16, Q4, HI, P31, UP, PAR, I8, K1, R8, K8 = range(11)
-    O_ARR, O_ARX, O_M0, O_M, O_CM, O_WL, O_U = 0, 14, 28, 30, 32, 62, 76
-    O_C0, O_C1, O_SG, O_UP, O_NAT = 82, 92, 102, 106, 114
-    NI, TG, SP, K4, WS, C224, ONE, C97, TK = 0, 96, 224, 360, 488, 540, 604, 636, 704
+    def kf(k, n, st=1, p0=0, p1=128):
+        return V("kf", k, k + n, st, p0, p1)
+    PP, Q4, HI, UP, I16, E, F12, I8, K1, R8, K8 = range(11)
+    QU, SG, W8, C48, AK, SH, VA, BF, BP, BN, NAT, FX = range(11, 23)
+    O_M, O_A, O_B, O_C, O_SG, O_UP, O_CM, O_WL, O_GL, O_NAT = 0, 2, 6, 10, 14, 18, 26, 56, 58, 60
+    NI, TG, TN, SP, K4, WS, C1, C3, RS, DEF, TK, NEG = 1440, 88, 216, 352, 488, 616, 672, 736, 928, 1248, 1280, 1392
     iota(ci(PP), [[0, 1]], 0, 1)
-    iota(V("ia", 0, 14), [[16, 14]])
-    iota(V("ia", 14, 28), [[32, 7], [0, 2]])
-    iota(V("ia", 28, 30), [[4, 2]])
-    mset(V("et", 0, 516), 1.0)
-    mset(V("pt", 384, 512), 0.0)
-    mset(V("vt", 0, 608), 0.0)
-    iota(V("ia", 30, 54), [[1, 8], [128, 3]])
-    iota(V("ia", 54, 60), [[1, 2], [128, 3]])
-    add("g", lambda: g.affine_select(T["et"][:, 0:516], T["et"][:, 0:516], [[-1, 516]], ALU.is_equal, 0.0, 3, 4), [V("et", 0, 516)], [V("et", 0, 516)])
-    iota(kf(NI, 96), [[1, 96]])
-    iota(V("ia", 60, 64), [[16, 2], [0, 2]])
-    act(V("et", 520, 1036), V("et", 0, 516), ACT.Copy, -1.0)
+    iota(ia(0, 10), [[m, 5], [4, 2]], 16 - 2 * m)
+    iota(ia(10, 12), [[4, 2]], m + 7)
+    iota(ia(12, 14), [[-4, 2]], 8)
+    iota(tm(0, 8), [[1, 2], [4, 2], [0, 2]], 1)
 
     def field(k, sh, an):
         ts(ci(k), ci(PP), sh, ALU.arith_shift_right, an, ALU.bitwise_and)
-    for k, sh, an in ((I16, 0, 15), (Q4, 0, 3), (HI, 2, 3), (P31, 0, 31)):
-        field(k, sh, an)
+    field(Q4, 0, 3)
+    field(HI, 2, 3)
     ts(ci(UP), ci(PP), float(S), ALU.is_ge)
-    cp(V("cf", 0, 6), V("ci", 0, 6))
-    n_, a_, b_, c_ = ib(0, 28), ib(28, 56), ib(56, 84), ib(84, 112)
-    kk, d_, e_, f_, h_ = ib(112, 114), ib(114, 116), ib(116, 118), ib(118, 120), ib(120, 122)
-    ts(ib(0, 14), V("ia", 0, 14), cf(I16), ALU.add)
-    ts(ib(14, 28), V("ia", 14, 28), cf(P31), ALU.add)
-    ts(kk, V("ia", 28, 30), cf(HI), ALU.add)
-    ts(cf(11), cf(Q4), 1.0, ALU.is_equal, cf(UP), ALU.subtract)
-    ts(cf(12), cf(Q4), 0.0, ALU.is_equal, cf(UP), ALU.mult)
-    ts(a_, n_, 96.0, ALU.is_ge, -49.0, ALU.mult)
-    ts(b_, n_, 96.0, ALU.is_equal, 48.0, ALU.mult)
-    ts(c_, n_, 144.0, ALU.is_ge, -95.0, ALU.mult)
-    ts(d_, kk, float(m), ALU.add)
-    ts(cf(11), cf(11), 0.0, ALU.max)
-    tt(a_, a_, b_, ALU.add)
-    tt(c_, c_, n_, ALU.add)
-    ts(d_, d_, 7, ALU.bitwise_and)
-    ts(b_, n_, 192.0, ALU.is_ge, 1000.0, ALU.mult)
-    tt(a_, a_, c_, ALU.add)
-    ts(e_, d_, float(8 - m), ALU.is_ge, 1.0, ALU.add)
-    ts(f_, d_, float(m), ALU.is_lt, cf(12), ALU.mult)
-    tt(a_, a_, b_, ALU.add)
-    ts(e_, e_, cf(11), ALU.mult)
-    ts(co(O_ARR, 28), a_, 96.0, ALU.min)
-    tt(e_, e_, f_, ALU.add)
+    cp(V("cf", 0, 4), V("ci", 0, 4))
+    for k, sh, an in ((I16, 0, 15), (E, 0, 31), (F12, 1, 12), (I8, 3, 1), (K1, 2, 1), (R8, 2, 7), (K8, 0, 7)):
+        field(k, sh, an)
+    cp(V("cf", 4, 11), V("ci", 4, 11))
+    n0, n1, n2, n3, n6 = ib(0, 2), ib(2, 4), ib(4, 6), ib(6, 8), ib(12, 14)
+    ts(ib(0, 12), ia(0, 12), cf(HI), ALU.add)
+    ts(n6, ia(12, 14), cf(HI), ALU.subtract)
+    ts(ib(0, 14), ib(0, 14), 7, ALU.bitwise_and)
+    ts(cf(QU), cf(UP), 4.0, ALU.mult, cf(Q4), ALU.add)
+    ts(tm(8, 16), tm(0, 8), cf(QU), ALU.is_equal)
+    ts(tm(16, 18), n3, float(8 - m), ALU.is_ge, 1.0, ALU.add)
+    ts(tm(18, 20), n3, float(m), ALU.is_lt)
+    ts(tm(20, 24), ib(8, 12), 4.0, ALU.add)
+    tt(tm(24, 32), tm(8, 16), tm(16, 24), ALU.mult)
+    tt(tm(32, 36), tm(24, 28), tm(28, 32), ALU.add)
+    tt(tm(36, 38), tm(32, 34), tm(34, 36), ALU.add)
+    cp(co(O_M, 2), tm(36, 38))
     for t in range(R):
-        cp(V("vt", 32 * (t + 1), 32 * (t + 1) + 4), V("vsm", 4 * t, 4 * t + 4))
-    cp(co(O_M0, 2), e_)
+        mset(V("la%d" % t, 3, 13), 0.0)
 
-    def scores(t, lst):
-        la = "la%d" % t
-        for j in range(3):
-            mm("pm", "P%d" % t, S * j, "v3", 8 * (t + 1) - 2 * j, 128, j == 0, j == 2)
-        cp(V(la, 0, 3), V("pm", 0, 5, 2))
-        cp(V("ms%d" % t, 0, 32), V(la, 0, 36 if t else 3), co(lst, 2))
-        w = 3 if t else 2
-        base = 40 - w
-        for tab in (a1, a2):
-            push(tab, "a%d" % t, lambda dl: V("ms%d" % t, 4 * dl, 4 * dl + w), lambda dl: V(la, base + w * dl, base + w * dl + w))
-        arrive("a%d" % t, (0, 1), [V(la, 40, 40 + 7 * w)])
-        cp(V(la, base, 40), V("ms%d" % t, 0, w))
-
-    def own_products(t):
-        for k in range(NR):
-            mm("pa", "D%d" % t, S * k, "u3", 32 * (t + 1) - 4 * k, 128, k == 0, k == NR - 1)
-
-    def own_scores(t):
-        act(V("la%d" % t, 4, 36), V("pa", 0, 32), ACT.Copy)
-        act(V("nn", 160, 192), V("pa", 0, 32), ACT.Copy)
-
-    quant("pin", 0, "pt", 128)
-    quant("v3", 0, "vt", 152)
-    pick("P0", 0, "pin", 128, co(O_ARR, 14))
-    ts(cf(15), cf(I16), 8.0, ALU.mult)
-    for t in range(R):
-        ts(co(O_U + 2 * t, 1), ci(Q4), float(4 * t), ALU.add)
-    scores(0, O_M0)
-    mset(V("ut", 0, 896), 0.0)
-    ts(co(O_CM, 30), V("ia", 30, 60), cf(15), ALU.add)
-
-    for buf, c0, c1, st, x in (("la0", 3, 4, 1, 0), ("la0", 36, 38, 1, 0), ("lb", 0, 3, 1, 0), ("w1", 155, 192, 1, 0), ("ib", 12, 14, 1, 2)):
-        fill(V(buf, c0, c1, st), x)
-    iota(V("ia", 64, 72), [[4, 8]])
-    iota(kf(TG, 96), [[16, 24], [0, 4]])
-    iota(kf(TG + 96, 32), [[16, 8], [0, 4]])
-    fill(V("w2", 155, 192), 0)
-    fill(kf(ONE, 32), int(KS))
-
-    H = ["h0", "h1", "h2", "h3"]
-
-    def rewrite(t, c0, n):
-        for b in range(4):
-            mm(H[b], "wt", 128 * b, "D%d" % t, c0, n, True, True)
-            act(V("ht", b, 4 * n, 4), V(H[b], 0, n), ACT.Relu, 0.0625)
-
-    def differ(t, c0, n):
-        quant("N%d" % t, c0, "ht", n)
-        for b in range(4):
-            mm(H[b], "ep", 128 * b, "N%d" % t, c0, n, True, False)
-            mm(H[b], "em", 128 * b, "D%d" % t, c0, n, False, True)
-            act(V("ht", b, 4 * n, 4), V(H[b], 0, n), ACT.Copy)
-
-    for t in range(R):
-        act(V("ut", 128 * (t + 1), 128 * (t + 1) + 16), V("usm", 0, 16), ACT.Copy, off=co(O_U + 2 * t, 1))
-    quant("xn", 0, "xt", C)
-    pick("D0", 0, "xn", C, co(O_CM, 29))
-    quant("u3", 0, "ut", 224)
-    own_products(0)
-    own_scores(0)
-    rewrite(0, 0, C)
-    ts(cf(13), cf(UP), float(-1 - m), ALU.mult, float(m + 8), ALU.add)
-    ts(cf(14), cf(Q4), 2.0, ALU.is_equal, 4.0, ALU.mult)
-    field(PAR, 4, 1)
-    ts(h_, d_, cf(13), ALU.add)
-    field(I8, 3, 1)
-    ts(h_, h_, 7, ALU.bitwise_and)
-    field(K1, 2, 1)
-    ts(h_, h_, 1.0, ALU.add, cf(14), ALU.mult)
-    field(R8, 2, 7)
-    tt(h_, h_, e_, ALU.add)
-    field(K8, 0, 7)
-    cp(co(O_M, 2), h_)
-    cp(V("cf", 6, 11), V("ci", 6, 11))
-    cp(V("msb", 0, 32), V("la0", 0, 36), co(O_M, 2))
-    for tab in (a1, a2):
-        push(tab, "ab", lambda dl: V("msb", 4 * dl + 2, 4 * dl + 3), lambda dl: V("lb", 3 + dl, 4 + dl))
-    arrive("ab", (0, 1), [V("lb", 4, 11)])
+    iota(kf(NI, 128), [[1, 128]])
+    mset(V("et", 0, 516), 0.0)
+    mset(V("et", 520, 1036), 0.0)
+    ts(V("et", 3, 515, 4), kf(NI, 128), cf(PP), ALU.is_equal)
+    ts(V("et", 523, 1035, 4), kf(NI, 128), cf(PP), ALU.is_equal, -1.0, ALU.mult)
     for b in range(4):
         quant("ep", 128 * b, "et", 128, 3 - b)
     for b in range(4):
         quant("em", 128 * b, "et", 128, 523 - b)
+
+    def dist(d):
+        return (d - m) % NR
+
+    def scores(t):
+        la, w = "la%d" % t, (3 if t else 2)
+        for j in range(3):
+            mm("pm", "P%d" % t, PR + S * j, "v3", 8 - 4 * j, 128, j == 0, j == 2)
+        cp(V(la, 0, 3), V("pm", t, 12, 4))
+        cp(V("ms%d" % t, 0, 32), V(la, 0, 12), co(O_M, 2))
+        for tab in (a1, a2):
+            push(tab, "a%d" % t, lambda d: V("ms%d" % t, 4 * dist(d), 4 * dist(d) + w),
+                 lambda d: V(la, LB + 3 * ((m - d) % NR), LB + 3 * ((m - d) % NR) + w))
+        arrive("a%d" % t, (0, 1), [V(la, LB + 3, LB + 24)], 2.8)
+        act(V(la, LB, LB + w), V("ms%d" % t, 0, w), ACT.Copy)
+
+    def own_scores(t, frm):
+        for k in range(NR):
+            mm("pa", frm, S * k, "v3", 40 - 4 * k, 128, k == 0, k == NR - 1)
+        act(V("la%d" % t, 4, 12), V("pa", t, 32, 4), ACT.Copy)
+
+    quant("P0", 0, "pt", PN)
+    quant("v3", 0, "vt", 168)
+    scores(0)
+
+    H = ["h0", "h1", "h2", "h3"]
+
+    def rewrite(t, c0, n):
+        D, N_, L = "D%d" % t, "N%d" % t, "L%d" % t
+        for b in range(4):
+            mm(H[b], "wt", 128 * b, D, c0, n, True, True)
+            if n > 128 and b % 2:
+                ts(V("ht", b, 4 * n, 4), V(H[b], 0, n), 0.0, ALU.max, 0.0625, ALU.mult)
+            else:
+                act(V("ht", b, 4 * n, 4), V(H[b], 0, n), ACT.Relu, 0.0625)
+            mm(H[b], "em", 128 * b, D, c0, n, True, False)
+        quant(N_, c0, "ht", n)
+        for b in range(4):
+            mm(H[b], "ep", 128 * b, N_, c0, n, False, True)
+            if n > 128 and b % 2:
+                cp(V("hu", b, 4 * n, 4), V(H[b], 0, n))
+            else:
+                act(V("hu", b, 4 * n, 4), V(H[b], 0, n), ACT.Copy)
+        quant(L, c0, "hu", n)
+
+    iota(kf(TN, 96), [[1, 8], [128, 3], [0, 4]])
+    iota(kf(TN + 96, 36), [[1, 3], [128, 3], [0, 4]])
+    ts(cf(W8), cf(I16), 8.0, ALU.mult)
+    act(kf(TN, 132), kf(TN, 132), ACT.Identity, 1.0, None, cf(W8))
+    cp(co(O_CM, 30), kf(TN, 120, 4))
+    quant("D0", C, "vt", 128, 176)
+    quant("D0", 0, "xt", C)
+    pick("Dc", 0, "D0", C, co(O_CM, 29))
+    own_scores(0, "Dc")
+    cp(V("msb", 0, 32), V("la0", 0, 12), co(O_M, 2))
+    for tab in (a1, a2):
+        push(tab, "ab", lambda d: V("msb", 4 * dist(d) + 2, 4 * dist(d) + 3),
+             lambda d: V("la0", LB + 3 * ((m - d) % NR) + 2, LB + 3 * ((m - d) % NR) + 3))
+    arrive("ab", (0, 1), [V("la0", LB + 3, LB + 24)], 2.8)
+    act(V("la0", LB + 2, LB + 3), V("msb", 2, 3), ACT.Copy)
+    rewrite(0, 0, C)
+
+    ts(co(O_A, 2), n2, 4.0, ALU.add)
+    ts(co(O_A + 2, 2), n1, 3.0, ALU.mult, LB + 2.0, ALU.add)
+    ts(co(O_B, 2), n1, 3.0, ALU.mult, LB + 0.0, ALU.add)
+    ts(co(O_C, 2), n0, 3.0, ALU.mult, LB + 1.0, ALU.add)
+    ts(tm(40, 42), n2, 3.0, ALU.mult, LB + 0.0, ALU.add)
+    ts(tm(42, 44), n2, float(8 - m), ALU.is_ge, 1.0, ALU.add)
+    fill(tm(44, 46), 2)
+    ts(tm(46, 48), n6, 3.0, ALU.mult, LB + 1.0, ALU.add)
+    tt(tm(48, 52), tm(44, 48), tm(40, 44), ALU.subtract)
+    ts(tm(48, 52), tm(48, 52), cf(UP), ALU.mult)
+    tt(tm(52, 56), tm(48, 52), tm(40, 44), ALU.add)
+    cp(co(O_B + 2, 2), tm(52, 54))
+    cp(co(O_C + 2, 2), tm(54, 56))
+    iota(ia(16, 20), [[16, 2], [0, 2]], 4 * m)
+    ts(cf(SG), cf(K1), float(4 * m), ALU.mult, cf(Q4), ALU.add)
+    ts(ib(16, 20), ia(16, 20), cf(F12), ALU.add, cf(SG), ALU.add)
+    ts(ib(16, 20), ib(16, 20), 31, ALU.bitwise_and)
+    cp(co(O_SG, 4), ib(16, 20))
+    iota(tm(56, 59), [[-1, 3]], 3)
+    mset(V("zz", 144, 224, 1, 32, 64), 0.0)
+    ts(tm(60, 63), tm(56, 59), cf(Q4), ALU.is_le, -0.5, ALU.add)
+    ts(V("zz", 13, 16), tm(60, 63), 2.0 * BIG, ALU.mult)
+    mset(kf(NEG, 48), -BIG)
+    fill(kf(WS, 52), 1)
+    fill(kf(WS + 3, 1), -1)
+    fill(V("ww", 155, 192), int(-US / 2))
+    ts(cf(C48), cf(R8), float(S), ALU.mult)
+    ts(cf(SH, 96), cf(R8, 96), float(8 - m), ALU.is_ge)
+    ts(cf(AK, 64), cf(E, 64), 32.0, ALU.add)
+    ts(cf(FX, 96), cf(E, 96), -2.0, ALU.mult, -32.0 * S, ALU.add)
+    ts(cf(AK, 96), cf(SH, 96), -32.0, ALU.mult, cf(AK, 96), ALU.add)
+    act(V("tt", 0, 84, 1, 0, 64), kf(NI, 84, 1, 0, 64), ACT.Identity, 8.0, None, cf(R8, 0, 64))
+    act(V("tt", 0, 84, 1, 64), kf(NI, 84, 1, 64), ACT.Identity, 32.0, None, cf(AK, 64))
+    ts(V("tt", 0, 1, 1, 96), cf(FX, 96), cf(SH, 96), ALU.mult, cf(AK, 96), ALU.add)
+    ts(cf(VA, 64), cf(R8, 64), 16.0, ALU.mult, cf(Q4, 64), ALU.add)
+    ts(cf(VA, 96), cf(VA, 96), 4.0, ALU.add)
+    ts(cf(BF, 64), cf(E, 64), -1.0, ALU.mult, -0.5, ALU.add)
+    ts(cf(BP, 64, 96), cf(E, 64, 96), -1.0 / 32, ALU.mult, PR - 1.0, ALU.add)
+    ts(cf(BP, 96), cf(E, 96), -1.0 / 32, ALU.mult, PR - 1.0 + S, ALU.add)
+    mset(cf(BN, 64, 96), PN + 15.5)
+    mset(cf(BN, 96), PN + 47.5)
+    mset(V("sa", 64, 65), -BIG)
+    iota(kf(C1, 64), [[32, 2], [0, 2], [2, 16]], -31)
+    iota(kf(C3, 96), [[16, 3], [0, 2], [1, 16]], PR)
+    ts(kf(C3, 96, 1, 96), kf(C3, 96, 1, 96), float(S), ALU.add)
+    iota(kf(C3 + 96, 96), [[16, 3], [0, 2], [1, 16]], PR + S - 1)
+    fill(kf(C3 + 96, 17, 16), PR + 2 * S - 1)
+    iota(kf(RS, 320), [[0, 10], [1000, 32]])
+    iota(tm(64, 72), [[2, 2], [10, 2], [1, 2]])
+    fill(tm(72, 96), 20)
+    iota(tm(77, 80), [[1, 3]], 4)
+    iota(tm(80, 86), [[1, 6]], 14)
+    iota(tm(86, 89), [[1, 3]], 4)
+    fill(tm(96, 98), 0)
+    ts(co(O_WL, 2), tm(96, 98), cf(E), ALU.add)
+    cp(V("wf", 0, 32), tm(64, 96), co(O_WL, 2))
+    tr(V("ff", 0, 32), V("wf", 0, 32))
+    cp(co(O_GL, 2), V("ff", 0, 32, 16))
+    fill(V("wb", 20, 24), 0)
+    fill(kf(DEF, 12), 0)
+    iota(kf(DEF + 12, 20), [[16, 20]])
+    act(kf(DEF + 12, 20), kf(DEF + 12, 20), ACT.Identity, 1.0, None, cf(I16))
+    fill(kf(TK, 112), 0)
+    fill(kf(TK, 1), 1)
+    iota(kf(TG, 96), [[16, 24], [0, 4]])
+    iota(kf(TG + 96, 32), [[16, 8], [0, 4]])
+    act(kf(TG, 128), kf(TG, 128), ACT.Identity, 1.0, None, cf(I16))
     k = 0
     while k < 11:
         dl = (k - m) % NR
@@ -403,239 +463,152 @@ def rank_program(g, core, T, topo):
         iota(kf(SP + 12 * k, 12 * n), [[8, n], [0, 3], [1, 4]], YO + 8 * dl)
         k += n
     iota(kf(K4, 128), [[0, 32], [1000, 4]])
-    iota(kf(C224, 64), [[1, 64]], PN)
-    iota(kf(C97, 64), [[1, 64]], 97)
-    fill(V("si", 64, 130, 65), -1)
-    fill(kf(TK, 200), 0)
-    fill(kf(TK + ZC, 1), 1)
-    iota(V("tb", 0, 168), [[1, 168]])
-    fill(V("tb", 96, 97), ZC)
-    fill(V("la1", 3, 37, 33), 0)
-
-    lo_, hi_ = ib(8, 12), ib(12, 16)
-    ts(cf(15), cf(R8), 48.0, ALU.mult)
-    cp(co(O_WL, 14), ib(14, 28))
-    ts(ib(0, 2), kk, float(8 - m), ALU.add)
-    ts(ib(2, 4), kk, float(16 - 2 * m), ALU.add)
-    cp(ib(4, 6), kk)
-    ts(ib(6, 8), kk, -1.0, ALU.mult, 8.0, ALU.add)
-    ts(ib(10, 12), kk, float(8 - m), ALU.is_ge, 1.0, ALU.add)
-    differ(0, 0, C)
-    ts(cf(11), cf(PAR), 2.0, ALU.mult, cf(I8), ALU.add)
-    ts(cf(12), cf(K1), float(4 * m), ALU.mult, cf(Q4), ALU.add)
-    ts(ib(0, 8), ib(0, 8), 7, ALU.bitwise_and)
-    act(V("tt", 0, 84), kf(NI, 84), ACT.Identity, 1.0, None, cf(15))
-    ts(cf(11), cf(11), 4.0, ALU.mult, cf(12), ALU.add)
-    for lv in range(3):
-        ts(V("z1", 13 + lv, 14 + lv), cf(Q4), float(3 - lv), ALU.is_ge, -0.5, ALU.add)
-    ts(ib(20, 24), V("ia", 60, 64), cf(11), ALU.add, float(4 * m), ALU.add)
-    mset(kf(WS, 52), 1.0)
-    ts(V("z1", 13, 16), V("z1", 13, 16), 2.0 * BIG, ALU.mult)
-    ts(ib(20, 24), ib(20, 24), 31, ALU.bitwise_and)
-    mset(V("sb", 64, 112), -BIG)
-    cp(co(O_SG, 4), ib(20, 24))
-    mset(kf(WS + 3, 1), -1.0)
-
-    def lists(o, w):
-        base = 40.0 - w
-        ts(co(o, 2), ib(0, 2), float(w), ALU.mult, base, ALU.add)
-        ts(ib(8, 10), ib(4, 6), float(w), ALU.mult, base, ALU.add)
-        ts(ib(14, 16), ib(6, 8), float(w), ALU.mult, base, ALU.add)
-        ts(co(o + 2, 2), ib(2, 4), float(w), ALU.mult, base + 1, ALU.add)
-        tt(ib(16, 20), hi_, lo_, ALU.subtract)
-        if w == 2:
-            ts(co(o + 4, 2), ib(0, 2), 3.0, ALU.add)
-        else:
-            ts(co(o + 4, 2), ib(0, 2), 3.0, ALU.mult, base + 2, ALU.add)
-        ts(ib(16, 20), ib(16, 20), cf(UP), ALU.mult)
-        tt(ib(16, 20), ib(16, 20), lo_, ALU.add)
-        cp(co(o + 6, 4), ib(16, 20))
-    lists(O_C0, 2)
-    act(kf(TG, 128), kf(TG, 128), ACT.Identity, 1.0, None, cf(I16))
-    ts(ib(24, 25), ci(R8), float(8 - m), ALU.add)
-    ts(cf(16), cf(R8), 128.0, ALU.mult, cf(Q4), ALU.add)
-    ts(cf(13), cf(R8), float(8 - m), ALU.is_ge, -KP, ALU.mult)
-    ts(cf(14), cf(PP), 32.0, ALU.is_ge)
-    ts(ib(24, 25), ib(24, 25), 7, ALU.bitwise_and)
-    ts(cf(17), cf(R8), float(m), ALU.not_equal, 8.0, ALU.mult)
-    ts(cf(13), cf(13), KP * S + 4, ALU.add, cf(14), ALU.mult)
-    ts(cf(18), ib(24, 25), 8.0, ALU.mult, cf(16), ALU.add)
-    ts(cf(14), cf(14), KP * S, ALU.mult)
-    ts(V("up", 0, 8), V("ia", 64, 72), cf(HI), ALU.add, -1.0, ALU.add)
-    ts(cf(13), cf(13), cf(17), ALU.add, cf(18), ALU.add)
-    ts(V("up", 8, 16), V("up", 0, 8), 1.0 / 3.0, ALU.mult)
-    quant("L0", 0, "ht", C)
-    cp(V("z2", 13, 16), V("z1", 13, 16))
-    act(V("tt", 84, 168), kf(NI, 84), ACT.Identity, KP, None, cf(13))
-    cp(ib(24, 32), V("up", 8, 16))
-    cp(V("lb", 3, 4), V("msb", 2, 3))
+    iota(ia(24, 32), [[4, 8]], -1)
+    ts(tm(100, 108), ia(24, 32), cf(HI), ALU.add, 1.0 / 3.0, ALU.mult)
+    cp(ib(24, 32), tm(100, 108))
     ts(ib(24, 32), ib(24, 32), 7, ALU.bitwise_and)
-    mset(V("ow0", 12, 16), ZC)
     ts(co(O_UP, 8), ib(24, 32), 4.0, ALU.mult, cf(Q4), ALU.add)
-    mset(V("nt", 256, 512), 0.0)
+    iota(ia(32, 56), [[2, 24]])
+    ts(cf(NAT), cf(K8), float(S), ALU.mult, cf(I8), ALU.add)
+    ts(co(O_NAT, 24), ia(32, 56), cf(NAT), ALU.add)
 
-    def later(t):
-        if t == 0:
-            iota(V("tb", 168, 504), [[0, 2], [1, 168]])
-            fill(V("tb", 264, 504, 168), ZC)
-            fill(V("la2", 3, 37, 33), 0)
-            iota(V("ia", 72, 96), [[2, 24]])
-            lists(O_C1, 3)
-            ts(cf(19), cf(K8), 48.0, ALU.mult, cf(I8), ALU.add)
-            for x in range(1, R):
-                mset(V("ow%d" % x, 12, 16), ZC)
-        else:
-            quant("un", 0, "uf", 128)
-            quant("vn", 0, "vf", 128)
-            ts(co(O_NAT, 24), V("ia", 72, 96), cf(19), ALU.add)
+    def Z(c0, c1, st=1):
+        return V("zz", c0, c1, st)
 
-    def top(z, w, P, t0):
-        def Z(c0, c1, st=1):
-            return V(z, c0, c1, st, 0, P)
+    def W(c0, c1):
+        return V("ww", c0, c1)
 
-        def W(c0, c1):
-            return V(w, c0, c1, 1, 0, P)
+    def Q(name, a, c0, n=32, st=1):
+        return V(name, c0, c0 + n, st, 32 * a, 32 * a + 32)
+
+    def U(name, c0, c1, st=1):
+        return V(name, c0, c1, st, 64, 128)
+
+    for t in range(R):
+        win = V("la%d" % t, 0, LB + 24)
+        D, N_, L, P, G, HS, SS = ("%s%d" % (x, t) for x in "DNLPGHS")
+        osn, oup, ow = ("%s%d" % (x, t) for x in ("osn", "oup", "ow"))
+        cp(V("nn", 0, 64), win, co(O_A, 4))
+        tt(V("nn", 64, 128), win, V("nn", 0, 64), ALU.subtract, co(O_B, 4))
+        tt(V("nn", 128, 192), win, V("nn", 64, 128), ALU.add, co(O_C, 4))
+        tr(Q("zz", 0, 160), Q("nn", 0, 128))
+        tr(Q("zz", 0, 192), Q("nn", 1, 128))
+        tr(Q("zz", 2, 144), Q("nn", 1, 160))
+        tr(Q("zz", 2, 176), Q("nn", 2, 160))
+        tr(Q("zz", 3, 160), Q("nn", 0, 160))
+        tr(Q("zz", 3, 192), Q("nn", 1, 160))
         sc0 = Z(160, 208)
-        scan(Z(16, 160, 3), sc0, V("sb", 64, 112, 1, 0, P), Z(13, 14), ALU.min, ALU.max)
+        scan(Z(16, 160, 3), sc0, kf(NEG, 48), Z(13, 14), ALU.min, ALU.max)
         scan(Z(17, 160, 3), sc0, Z(13, 157, 3), Z(14, 15), ALU.min, ALU.max)
         scan(Z(18, 160, 3), sc0, Z(14, 158, 3), Z(15, 16), ALU.min, ALU.max)
         scan(W(0, 48), sc0, Z(15, 159, 3), BIG, ALU.min, ALU.max)
         ts(W(48, 99), Z(157, 208), W(47, 48), ALU.is_equal, US, ALU.mult)
-        scan(W(104, 155), kf(WS, 51, 1, P), W(48, 99), -US, ALU.mult, ALU.subtract)
-        scan(W(192, 272), W(107, 187), V("tt", t0 + 1, t0 + 81, 1, 0, P), V("tt", t0, t0 + 1, 1, 0, P), ALU.max, ALU.min)
-
-    def Q(name, a, c0, n=32):
-        return V(name, c0, c0 + n, 1, 32 * a, 32 * a + 32)
-
-    def turn(out, n):
-        tr(V("wx", 224, 224 + 16 * n), V("wx", 0, 16 * n))
-        cp(out, V("wx", 224, 224 + 16 * n, 16))
-
-    def A(c0, c1, P=64):
-        return V("sa", c0, c1, 1, 0, P)
-
-    for t in range(R):
-        la, o = "la%d" % t, (O_C1 if t else O_C0)
-        win = V(la, 0, 61 if t else 54)
-        D, N_, L, P, G, HS, SS = ("%s%d" % (x, t) for x in "DNLPGHS")
-        osn, oup, ow, oar = ("%s%d" % (x, t) for x in ("osn", "oup", "ow", "oar"))
-        tt(V("nn", 0, 32), win, V("nn", 160, 192), ALU.subtract, co(o, 2))
-        tt(V("nn", 32, 64), win, V("nn", 0, 32), ALU.add, co(o + 2, 2))
-        tr(Q("z1", 0, 160), Q("nn", 0, 32))
-        tr(Q("z1", 0, 192), Q("nn", 1, 32))
-        top("z1", "w1", 32, 0)
+        scan(W(104, 155), kf(WS, 51), W(48, 99), -US / 2, ALU.mult, ALU.subtract)
+        scan(W(192, 272), W(107, 187), V("tt", 1, 81), V("tt", 0, 1), ALU.max, ALU.min)
         for a in range(4):
-            tr(Q("ff", a, 0), Q("w1", 0, 240))
+            tr(Q("ff", a, 0), Q("ww", 0, 240))
         cp(V("ff", 32, 96), V("ff", 0, 32), co(O_SG, 4))
         tr(V("ff", 96, 160), V("ff", 32, 96))
         cp(V(osn, 0, 4), V("ff", 96, 160, 16))
         pick(SS, 0, L, C, V(osn, 0, 4))
-        push(b1, "b%d" % t, lambda dl: V(SS + "q", 8 * dl, 8 * dl + 8), lambda dl: V(G + "q", 8 * dl + 8, 8 * dl + 16), True)
-        push(b2, "b%d" % t, lambda dl: V(SS + "s", 8 * dl, 8 * dl + 8), lambda dl: V(G + "s", 8 * dl + 8, 8 * dl + 16))
-        arrive("b%d" % t, (2, 3), [V(G + "q", 16, 72), V(G + "s", 16, 72)])
+        push(b1, "b%d" % t, lambda d: V(SS + "q", 8 * dist(d), 8 * dist(d) + 8), lambda d: V(G + "q", 16 * m, 16 * m + 8), True)
+        push(b2, "b%d" % t, lambda d: V(SS + "s", 8 * dist(d), 8 * dist(d) + 8), lambda d: V(G + "s", 16 * m, 16 * m + 8))
+        came = arrive("b%d" % t, (2, 3), [V(G + x, 16 * r, 16 * r + 16) for x in "qs" for r in range(NR) if r != m], 3.6)
         if t == 0:
-            load("s", "l7", V("uf", 0, 512), lambda: T.u[:], [V(G + "s", 16, 72)])
-            load("s", "l8", V("vf", 0, 512), lambda: T.v[:])
-        if t:
-            cp(V("nn", 64, 96), win, co(o + 4, 2))
+            load("s", V("uf", 0, 512), lambda: T.u[:], 2.5, [came])
+            load("s", V("vf", 0, 512), lambda: T.v[:], 2.5, [came])
+            act(V("tt", 0, 84, 1, 0, 64), kf(NI, 84, 1, 0, 64), ACT.Identity, 1.0, None, cf(C48, 0, 64))
+            quant("un", 0, "uf", 128)
+            quant("vn", 0, "vf", 128)
+        pick(G, 16 * m, L, C, V(osn, 0, 1))
         pick(D, YO, N_, C, V(osn, 0, 4))
-        pick(G, 0, L, C, V(osn, 0, 1))
-        if t < R - 1:
-            rewrite(t, YO - 64, 128)
-        if not t:
-            cp(V("nn", 64, 96), V("lb", 0, 11), co(o + 4, 2))
-        tt(V("nn", 96, 128), win, V("nn", 64, 96), ALU.subtract, co(o + 6, 2))
-        tt(V("nn", 128, 160), win, V("nn", 96, 128), ALU.add, co(o + 8, 2))
-        tr(Q("z2", 0, 144), Q("nn", 1, 128))
-        tr(Q("z2", 0, 176), Q("nn", 2, 128))
-        tr(Q("z2", 1, 160), Q("nn", 0, 128))
-        tr(Q("z2", 1, 192), Q("nn", 1, 128))
-        top("z2", "w2", 64, 84)
-        key = V("w2", 240, 272, 1, 0, 64)
-        ts(A(0, 32), key, cf(14, 0, 64), ALU.is_lt, KP * S, ALU.mult)
-        tt(A(32, 64), A(0, 32), key, ALU.add)
-        for a in range(2):
-            for b in range(2):
-                tr(Q("sa", a, 64 + 32 * b), Q("sa", b, 32))
-        ts(A(128, 192), A(64, 128), A(32, 33), ALU.is_lt)
-        add("v", lambda: g.vector.tensor_reduce(ap(A(192, 193)), ap(A(128, 192)), AxisListType.X, ALU.add), [A(128, 192)], [A(192, 193)])
-        ts(A(200, 232), kf(ONE, 32, 1, 64), A(192, 193), ALU.mult, A(32, 33), ALU.add)
-        for b in range(2):
-            tr(Q("sa", 0, 256 + 32 * b), Q("sa", b, 200))
-        add("g", lambda: g.partition_broadcast(T["sb"][:, 0:64], T["sa"][0:1, 256:320], 128), [V("sa", 256, 320, 1, 0, 1)], [V("sb", 0, 64)])
-        tt(V("up", 0, 128), V("ff", 0, 32), kf(TG, 128), ALU.is_equal, co(O_UP, 8))
-        tt(V("up", 128, 256), V("up", 0, 128), kf(SP, 128), ALU.mult)
-        scan(V("up", 256, 384), kf(K4, 128), V("up", 128, 256), 0.0, ALU.min, ALU.max)
-        cp(V("wx", 0, 64), V("sb", 0, 64), co(O_WL, 4))
-        tt(V("up", 0, 32), V("up", 259, 384, 4), kf(TG, 128, 4), ALU.max)
-        tr(V("wx", 224, 288), V("wx", 0, 64))
-        cp(V(oup, 0, 32), V("up", 0, 32))
-        cp(V("si", 132, 136), V("wx", 224, 288, 16))
-        nd = 29 if t < R - 1 else 24
-        picks("D%d" % (t + 1), 0, D, 528, V(oup, 0, nd))
-        ts(V("si", 136, 140), V("si", 132, 136), 17, ALU.arith_shift_right)
-        cp(V("opos", 0, 4), V("si", 136, 140))
-        scat(V("si", 0, 64), V("opos", 0, 4), V("sb", 0, 64))
-        pl, same, kp = V("si", 65, 129), V("wr", 192, 256), V("kp", 0, 64)
-        ts(pl, V("si", 0, 64), 10, ALU.arith_shift_right, 127, ALU.bitwise_and)
-        ts(ib(32, 96), V("si", 0, 64), 127, ALU.bitwise_and)
-        tt(same, pl, V("si", 64, 128), ALU.is_equal)
-        tt(A(0, 64, 128), pl, V("si", 66, 130), ALU.is_equal)
-        cp(V("wr", 0, 64), ib(32, 96))
-        ts(A(128, 192, 128), same, float(ZC), ALU.mult)
-        tt(A(64, 128, 128), kf(C97, 64), A(0, 64, 128), ALU.mult)
-        tt(V("wr", 128, 192), A(128, 192, 128), pl, ALU.max)
-        tt(V("wr", 64, 128), A(64, 128, 128), pl, ALU.max)
-        act(V("wx", 0, 192), V("wr", 0, 192), ACT.Copy, off=co(O_WL, 12))
-        pickq("D%d" % (t + 1), 0, D, 528, V(oup, 0, nd))
-        if t < R - 1:
-            own_products(t + 1)
-        turn(V(ow, 0, 12), 12)
-        tb = V("tb", 168 * t, 168 * t + 161)
-        scat(tb, V(ow, 4, 8), kf(C224, 64))
-        pick(HS, 64, P, PN, V(ow, 8, 16))
+        key = U("sa", 0, 1)
+        act(U("sa", 0, 32), U("ww", 240, 272), ACT.Abs)
+        tr(U("sa", 32, 64), U("sa", 0, 32))
+        act(U("sc", 1, 2), key, ACT.Identity, 1.0, None, cf(BF, 64))
+        act(U("sc", 2, 3), key, ACT.Identity, 1.0 / 32, None, cf(BP, 64))
+        act(U("sa", 72, 104), U("sa", 32, 64), ACT.Sign, -1.0, None, key, U("sc", 0, 1))
+        act(U("sa", 72, 105), U("sa", 32, 65), ACT.Sign, -1.0, None, U("sc", 1, 2), U("sc", 3, 4))
+        act(U("sc", 4, 5), U("sc", 0, 1), ACT.Identity, 0.5, None, cf(BN, 64))
+        ts(U("sc", 5, 6), U("sc", 3, 4), U("sc", 0, 1), ALU.is_equal, U("sc", 2, 3), ALU.mult)
+        ts(U("oh", 0, 64), kf(C1, 64, 1, 64), U("sc", 0, 1), ALU.is_equal, cf(VA, 64), ALU.mult)
+        ts(U("oh", 64, 128), kf(C1, 64, 1, 64), U("sc", 0, 1), ALU.is_equal, U("sc", 5, 6), ALU.mult)
+        ts(U("oh", 128, 320), kf(C3, 192, 1, 64), U("sc", 2, 3), ALU.is_equal, U("sc", 4, 5), ALU.mult)
+        tr(U("ot", 0, 320), U("oh", 0, 320))
+        scan(U("oc2", 0, 320), kf(RS, 320, 1, 64), U("ot", 0, 320), 0.0, ALU.min, ALU.max)
+        cp(Q("wb", 2, 0, 10), Q("oc2", 2, 31, 289, 32))
+        act(Q("wb", 3, 0, 10), Q("oc2", 2, 31, 289, 32), ACT.Copy)
+        act(Q("wb", 2, 10, 10), Q("oc2", 3, 31, 289, 32), ACT.Copy)
+        cp(Q("wb", 3, 10, 10), Q("oc2", 3, 31, 289, 32))
+        cp(V("wb", 0, 20, 1, 0, 64), U("wb", 0, 20))
+        tt(V("wf", 0, 32), V("wb", 0, 24), kf(DEF, 32), ALU.max, co(O_GL, 2))
+        cp(V(ow, 0, 32), V("wf", 0, 32))
+        pick(HS, 64, P, PN, V(ow, 4, 12))
         for b in range(4):
             mm(H[b], "ep", 128 * b, HS, 64, 128, True, False)
-        na = 14 if t < R - 1 else 8
-        act(V("wx", 0, 16 * na), tb, ACT.Copy, off=co(O_ARX, na))
-        cp(kp, kf(TK, 200), V(ow, 8, 12))
+        kp = V("kp", 0, 64)
+        act(kp, kf(TK, 112), ACT.Copy, off=V(ow, 4, 8))
+        tg = TG if t else TN
+        tt(V("up", 0, 128), V("ff", 0, 32), kf(tg, 128), ALU.is_equal, co(O_UP, 8))
+        tt(V("up", 128, 256), V("up", 0, 128), kf(SP, 128), ALU.mult)
+        scan(V("up", 256, 384), kf(K4, 128), V("up", 128, 256), 0.0, ALU.min, ALU.max)
+        tt(V("up", 0, 32), V("up", 259, 384, 4), kf(tg, 128, 4), ALU.max)
+        cp(V(oup, 0, 32), V("up", 0, 32))
+        pick("D%d" % (t + 1), 0, D, 528, V(oup, 0, 29 if t < R - 1 else 24))
         if t < R - 1:
-            turn(V(oar, 0, na), na)
+            own_scores(t + 1, "D%d" % (t + 1))
         else:
             pick("Dn", 0, "D3", C, co(O_NAT, 24))
-            turn(V(oar, 0, na), na)
             mm("py", "un", 0, "Dn", 0, C, True, True)
-            dma("s", "stS", lambda: T.oc[:, 0:4 * C], lambda: T["Dnq"][:].bitcast(dt.uint8), [V("Dnq", 0, C)], [])
+            dma("s", "stS", lambda: T.oc[:, 0:4 * C], lambda: T["Dnq"][:].bitcast(dt.uint8), [V("Dnq", 0, C)], [], 2.7)
             for k in range(4):
                 dma("s", "stS", lambda k=k: T.osc[4 * k:4 * k + 4, 0:C], lambda k=k: T["Dns"][32 * k:32 * k + 4, 0:C], [V("Dns", 0, C)], [])
-        if t < R - 1:
-            act(V("la%d" % (t + 1), 4, 36), V("pa", 0, 32), ACT.Copy)
-        pick(HS, 0, G, 72, V(ow, 0, 4))
+            act(V("yb", 0, C), V("py", 0, C), ACT.Copy)
+            dma("s", "stS", lambda: T.y[:, 0:C], lambda: T["yb"][:, 0:C], [V("yb", 0, C)], [], 2.7)
+        pick(HS, 0, G, 128, V(ow, 0, 4))
         for b in range(4):
             mm(H[b], "ep", 128 * b, HS, 0, 128, False, True)
             scan(V("nt", b, 256, 4), kp, V(H[b], 0, 64), 0.0, ALU.mult, ALU.add)
-        if t == R - 1:
-            act(V("yb", 0, C), V("py", 0, C), ACT.Copy)
-            dma("s", "stS", lambda: T.y[:, 0:C], lambda: T["yb"][:, 0:C], [V("yb", 0, C)], [])
-        else:
-            act(V("nn", 160, 192), V("pa", 0, 32), ACT.Copy)
         quant(P, PN, "nt", 128)
-        pick("P%d" % (t + 1), 0, P, 352, V(oar, 0, na))
+        pick("P%d" % (t + 1), 0, P, 368, V(ow, 12, 27 if t < R - 1 else 21))
         if t < R - 1:
-            scores(t + 1, O_M)
-            differ(t, YO - 64, 128)
+            scores(t + 1)
+            rewrite(t, YO - 64, 128)
             pick("N%d" % (t + 1), 0, N_, 528, V(oup, 0, 24))
-            later(t)
-            quant(L, YO - 64, "ht", 128)
             pick("L%d" % (t + 1), 0, L, 528, V(oup, 0, 24))
-    mm("pz", "vn", 0, "P3", 0, 128, True, True)
-    dma("s", "stS", lambda: T.oc[:, 4 * C:4 * C + 8 * S], lambda: T["P3q"][:, 0:2 * S].bitcast(dt.uint8), [V("P3q", 0, 2 * S)], [])
+    mm("pz", "vn", 0, "P3", PR, 128, True, True)
+    dma("s", "stS", lambda: T.oc[:, 4 * C:4 * C + 8 * S], lambda: T["P3q"][:, PR:PR + 2 * S].bitcast(dt.uint8), [V("P3q", PR, PR + 2 * S)], [])
     for k in range(4):
         dma("a" if k % 2 else "s", "stA" if k % 2 else "stS", lambda k=k: T.osc[4 * k:4 * k + 4, C:C + 2 * S],
-            lambda k=k: T["P3s"][32 * k:32 * k + 4, 0:2 * S], [V("P3s", 0, 2 * S)], [])
+            lambda k=k: T["P3s"][32 * k:32 * k + 4, PR:PR + 2 * S], [V("P3s", PR, PR + 2 * S)], [])
     cp(V("yb", C, C + 2 * S), V("pz", 0, 2 * S))
     dma("a", "stA", lambda: T.y[:, C:C + 2 * S], lambda: T["yb"][:, C:C + 2 * S], [V("yb", C, C + 2 * S)], [])
 
+    ops = arrange(ops)
+    first = loads[:10]
+    ops = first + [o for o in ops if not any(o is x for x in first)]
+    clock, seq = {q: {} for q in eng}, {q: 0 for q in eng}
+    for i, o in enumerate(ops):
+        q = o["q"]
+        o["at"], o["waits"], o["clock"] = i, [], {}
+        if q is not None:
+            known = clock[q]
+            for x in sorted(o["deps"], key=lambda y: -y["at"]):
+                if x.get("remote") or x["q"] == q == "p":
+                    continue
+                k, n = x["tok"]
+                if known.get(k, 0) < n:
+                    o["waits"].append(x)
+                    x["inc"] = True
+                    for kk, nn in list(x["clock"].items()) + [(k, n)]:
+                        if known.get(kk, 0) < nn:
+                            known[kk] = nn
+            o["clock"] = dict(known)
+        if o["sem"] is None:
+            seq[q] += 1
+            o["tok"] = (q, seq[q])
+        else:
+            o["tok"] = ("#" + o["sem"], o["count"])
     cnt = {q: 0 for q in qsem}
     stores = {"stS": 0, "stA": 0}
     for o in ops:

@@ -6,10 +6,11 @@ ACT = ActivationFunctionType
 NR, C, S, R = 8, 384, 48, 3
 BIG = 1.0e29
 US = 262144.0
-YO = 464
-PR = 16
-PN = 240
-LB = 13
+DO, YO = 48, 512
+DE = DO + C
+PR = 48
+PN = 272
+LB, LA = 6, 27
 
 SCRATCH = {}
 
@@ -19,35 +20,36 @@ def _pair(name, n):
     SCRATCH[name + "s"] = ("sbuf", [128, n], "uint8")
 
 
-for _n, _w in (("Dc", 464), ("v3", 168), ("vn", 128), ("un", 128), ("ep", 512), ("em", 512),
-               ("wt", 512), ("D0", 528), ("D1", 528), ("D2", 528), ("D3", 384), ("Dn", 384),
-               ("N0", 528), ("N1", 528), ("N2", 384), ("L0", 528), ("L1", 528), ("L2", 384),
-               ("P0", 368), ("P1", 368), ("P2", 368), ("P3", 144)):
+for _n, _w in (("D0", C), ("Dc", 704), ("v3", 256), ("vn", 128), ("un", 128), ("ep", 512), ("em", 512),
+               ("wt", 512), ("Dn", C),
+               ("N0", 640), ("N1", 640), ("N2", DE), ("L0", 640), ("L1", 640), ("L2", DE),
+               ("P0", 400), ("P1", 400), ("P2", 400), ("P3", 128)):
     _pair(_n, _w)
 for _t in range(R):
     _pair("S%d" % _t, 64)
     _pair("G%d" % _t, 128)
     _pair("H%d" % _t, 192)
     SCRATCH["la%d" % _t] = ("sbuf", [128, 40], "float32")
-    SCRATCH["ms%d" % _t] = ("sbuf", [128, 32], "float32")
+    SCRATCH["ms%d" % _t] = ("sbuf", [128, 16], "float32")
+    SCRATCH["aa%d" % _t] = ("sbuf", [128, 32], "float32")
     SCRATCH["osn%d" % _t] = ("sbuf", [128, 4], "uint16")
-    SCRATCH["oup%d" % _t] = ("sbuf", [128, 32], "uint16")
+    SCRATCH["oup%d" % _t] = ("sbuf", [128, 24], "uint16")
     SCRATCH["ow%d" % _t] = ("sbuf", [128, 32], "uint16")
-for _n, _w in (("xt", 1536), ("pt", 960), ("vt", 688), ("vf", 512), ("uf", 512),
-               ("et", 1040), ("ht", 1536), ("hu", 1536), ("nt", 512)):
+for _n, _w in (("xt", 1536), ("pt", 896), ("vt", 784), ("vf", 512), ("uf", 512),
+               ("et", 520), ("ht", 1536), ("hu", 1536), ("nt", 512)):
     SCRATCH[_n] = ("sbuf", [128, _w], "bfloat16")
-for _n, _w in (("msb", 32), ("cf", 32), ("kf", 1568), ("tt", 84), ("yb", 480), ("nn", 192), ("zz", 224), ("ww", 272),
-               ("ff", 160), ("sa", 112), ("sc", 8), ("oh", 320), ("ot", 320), ("oc2", 320), ("wb", 24), ("wf", 32),
-               ("up", 384), ("kp", 64), ("tm", 128)):
+for _n, _w in (("cf", 40), ("kf", 1600), ("tt", 84), ("yb", 480), ("nn", 192), ("zz", 224), ("ww", 272),
+               ("ff", 160), ("sa", 144), ("sc", 8), ("oh", 320), ("ot", 320), ("oc2", 320), ("wb", 32), ("wf", 32),
+               ("up", 312), ("un2", 368), ("kp", 64), ("tm", 128), ("fl", 96), ("mk", 112), ("a0", 8)):
     SCRATCH[_n] = ("sbuf", [128, _w], "float32")
-for _n, _w in (("ci", 16), ("ia", 96), ("ib", 64)):
+for _n, _w in (("ci", 8), ("ib", 32)):
     SCRATCH[_n] = ("sbuf", [128, _w], "int32")
 SCRATCH["co"] = ("sbuf", [128, 96], "uint16")
 for _n in ("h0", "h1", "h2", "h3", "pa", "pm", "py", "pz"):
     SCRATCH[_n] = ("psum", [128, 512], "float32")
 
-SEMAPHORES = (["qv", "qa", "qp", "qg", "sent", "stS", "stA", "ab"] + ["l%d" % _i for _i in range(12)]
-              + ["a%d" % _t for _t in range(R)] + ["b%d" % _t for _t in range(R)])
+SEMAPHORES = (["qv", "qa", "qp", "qg", "sent", "stS", "stA"] + ["l%d" % _i for _i in range(28)]
+              + [_x + "%d" % _t for _t in range(R) for _x in "abc"])
 
 
 def deal(src, cores, topo):
@@ -77,7 +79,7 @@ def bits(x):
 def arrange(ops):
     hop = 0.15
     for o in reversed(ops):
-        o["tail"] = o["lat"] + max([hop + x["tail"] for x in o["users"]] + [0.0])
+        o["tail"] = o["lat"] + o["more"] + max([hop + x["tail"] for x in o["users"]] + [0.0])
     busy = {}
     for o in sorted(ops, key=lambda y: (-y["tail"], y["at"])):
         t = max([x["start"] + (x["cost"] if x["q"] == o["q"] == "p" or x.get("remote") else x["lat"] + hop) for x in o["deps"]] + [0.0])
@@ -124,7 +126,7 @@ def rank_program(g, core, T, topo):
 
     def add(q, fn, reads, writes, cost, lat=None, sem=None, count=16, after=()):
         o = {"q": q, "fn": fn, "inc": False, "sem": sem, "count": count, "cost": cost, "lat": cost if lat is None else lat,
-             "at": len(ops), "users": [], "deps": list(after)}
+             "at": len(ops), "users": [], "deps": list(after), "more": 0.0}
         seen = {x["at"] for x in after}
         for v, wr in [(v, False) for v in reads] + [(v, True) for v in writes]:
             ps = SCRATCH[v[0]][0] == "psum"
@@ -152,7 +154,7 @@ def rank_program(g, core, T, topo):
 
     def span(out, off=None, k=1):
         n = wide(out)
-        return 0.05 + 0.0016 * n if off is not None else max(64, k * n) * 0.001
+        return 0.06 + 0.0015 * n if off is not None else max(64, k * n) * 0.001
 
     def ts(out, a, s1, op0, s2=None, op1=None, off=None):
         if op1 is None:
@@ -169,13 +171,16 @@ def rank_program(g, core, T, topo):
     def act(out, a, func, scale=1.0, off=None, bias=None, acc=None):
         kw = {}
         if bias is not None:
-            kw["bias"] = ap(bias)
+            kw["bias"] = sc(bias)
         if scale != 1.0:
-            kw["scale"] = scale
+            kw["scale"] = sc(scale)
         if acc is not None:
             kw["accum_out"] = ap(acc)
-        add("a", lambda: g.scalar.activation(ap(out), src(a, off), func, **kw), vs(a, off, bias), vs(out, acc),
-            0.07 + wide(out) * (0.001 if off is None else 0.0016))
+        add("a", lambda: g.scalar.activation(ap(out), src(a, off), func, **kw), vs(a, off, bias, scale), vs(out, acc),
+            max(64, wide(a)) * 0.001 if off is None else 0.08 + 0.0015 * wide(out))
+
+    def lin(out, a, scale, bias):
+        act(out, a, ACT.Identity, scale, None, bias)
 
     def scan(out, d0, d1, init, op0, op1):
         add("v", lambda: g.vector.tensor_tensor_scan(ap(out), ap(d0), ap(d1), sc(init), op0, op1), vs(d0, d1, init), [out], span(out))
@@ -188,16 +193,13 @@ def rank_program(g, core, T, topo):
 
     def iota(out, pat, base=0, mult=0):
         if SCRATCH[out[0]][2] == "int32":
-            add("g", lambda: g.iota(ap(out), pat, base, mult), [], [out], 0.13 + 0.002 * wide(out))
+            add("g", lambda: g.iota(ap(out), pat, base, mult), [], [out], 0.16 + 0.002 * wide(out))
         else:
-            add("g", lambda: g.iota(ap(out), pat, base, mult, allow_small_or_imprecise_dtypes=True), [], [out], 0.13 + 0.002 * wide(out))
-
-    def fill(out, x):
-        iota(out, [[0, wide(out)]], x)
+            add("g", lambda: g.iota(ap(out), pat, base, mult, allow_small_or_imprecise_dtypes=True), [], [out], 0.16 + 0.002 * wide(out))
 
     def quant(name, c0, tile, n, e0=0):
         q, s, a = V(name + "q", c0, c0 + n), V(name + "s", c0, c0 + n), V(tile, e0, e0 + 4 * n)
-        add("v", lambda: g.vector.quantize_mx(ap(q), ap(s), ap(a)), [a], [q, s], 0.02 + 0.0011 * n)
+        add("v", lambda: g.vector.quantize_mx(ap(q), ap(s), ap(a)), [a], [q, s], 0.015 + 0.00106 * n)
 
     def mm(bank, st, s0, mv, m0, n, start, stop):
         o = V(bank, 0, n)
@@ -210,7 +212,7 @@ def rank_program(g, core, T, topo):
         add("v", lambda: g.vector.tensor_copy(ap(oq).bitcast(dt.uint32), ap(iq).bitcast(dt.uint32).indirect(ap(off))), [iq, off], [oq],
             span(oq, off))
         o2, i2 = V(dst + "s", d0, d0 + 16 * wide(off)), V(frm + "s", 0, n)
-        add("a", lambda: g.scalar.activation(ap(o2), ap(i2).indirect(ap(off)), ACT.Copy), [i2, off], [o2], span(o2, off))
+        add("a", lambda: g.scalar.activation(ap(o2), ap(i2).indirect(ap(off)), ACT.Copy), [i2, off], [o2], span(o2, off) + 0.02)
 
     def dma(q, sem, fo, fi, reads, writes, lat=2.0, after=()):
         return add(q, lambda: eng[q].dma_start(fo(), fi()), reads, writes, 0.06, lat, sem=sem, after=after)
@@ -230,7 +232,7 @@ def rank_program(g, core, T, topo):
                     a, b = a.bitcast(dt.uint8), b.bitcast(dt.uint8)
                 trs.append(RemoteDMATransfer(dst_ids=[DstId(rid=rid, pnc=pid)], dma_engine_mask=tab[d], remote_sem=T.sem[sem], src=a, dst=b))
             return g.remote_dma_fused(trs, local_sem=T.sem["sent"])
-        o = add("g", fn, [u for d, u, v in items], [], 0.4 if calls else 3.0, sem="sent", after=calls[-1:])
+        o = add("g", fn, [u for d, u, v in items], [], (0.25 + 0.03 * len(items)) if calls else 3.3, sem="sent", after=calls[-1:])
         o["remote"] = True
         calls.append(o)
         sent[0] += sum(bits(x) for x in tab.values())
@@ -245,32 +247,26 @@ def rank_program(g, core, T, topo):
 
     def load(q, dst, fi, lat=2.0, after=()):
         loads.append(dma(q, "l%d" % len(loads), lambda: ap(dst), fi, [], [dst], lat, after))
-    e0 = 4 * PR
-    load("s", V("pt", e0, e0 + 192), lambda: T.pr[:])
-    load("a", V("pt", e0 + 192, e0 + 384), lambda: T.pd[:])
-    load("s", V("vt", 32, 48), lambda: T.v[:, 0:16])
-    load("a", V("pt", e0 + 388, e0 + 576), lambda: T.pd[:, 0:188])
-    load("s", V("pt", e0 + 576, e0 + 768), lambda: T.pr[:])
-    load("a", V("pt", e0 + 384, e0 + 388), lambda: T.pd[:, 188:192])
-    load("s", V("xt", 0, 1536), lambda: T.x[:], 3.8)
-    load("a", V("vt", 160, 176), lambda: T.u[:, 0:16])
-    loads.append(dma("s", "l8", lambda: T["wtq"][:].bitcast(dt.uint8), lambda: T.wc[:], [], [V("wtq", 0, 512)], 3.5))
-    load("a", V("wts", 0, 512), lambda: T.ws[:], 2.5)
-    mset(V("pt", 0, e0), 0.0)
-    mset(V("pt", e0 + 768, 960), 0.0)
-    mset(V("vt", 0, 32), 0.0)
-    mset(V("vt", 48, 160), 0.0)
-    mset(V("vt", 176, 688), 0.0)
+    load("s", V("pt", 0, 192), lambda: T.pr[:])
+    load("a", V("pt", 192, 384), lambda: T.pd[:])
+    load("s", V("vt", 96, 112), lambda: T.v[:, 0:16])
+    load("a", V("pt", 388, 580), lambda: T.pd[:])
+    load("s", V("vt", 128, 144), lambda: T.v[:, 0:16])
+    load("a", V("pt", 580, 768), lambda: T.pd[:, 0:188])
+    load("s", V("vt", 48, 64), lambda: T.v[:, 0:16])
+    load("a", V("pt", 384, 388), lambda: T.pd[:, 188:192])
+    load("s", V("vt", 256, 272), lambda: T.u[:, 0:16], 2.2)
+    load("s", V("xt", 0, 1536), lambda: T.x[:], 3.3)
+    loads.append(dma("s", "l10", lambda: T["wtq"][:].bitcast(dt.uint8), lambda: T.wc[:], [], [V("wtq", 0, 512)], 3.8))
+    load("s", V("wts", 0, 512), lambda: T.ws[:], 3.8)
+    ZT, ZC = 272, 128
+    for c0, c1 in ((0, 48), (64, 96), (112, 128), (144, 256), (ZT, 784)):
+        mset(V("vt", c0, c1), 0.0)
+    mset(V("pt", 768, 896), 0.0)
     mset(V("nt", 256, 512), 0.0)
-
-    def ci(k):
-        return V("ci", k, k + 1)
 
     def cf(k, p0=0, p1=128):
         return V("cf", k, k + 1, 1, p0, p1)
-
-    def ia(c0, c1):
-        return V("ia", c0, c1)
 
     def ib(c0, c1):
         return V("ib", c0, c1)
@@ -278,205 +274,249 @@ def rank_program(g, core, T, topo):
     def tm(c0, c1, st=1):
         return V("tm", c0, c1, st)
 
+    def fl(k, n):
+        return V("fl", k, k + n)
+
     def co(k, n):
         return V("co", k, k + n)
 
     def kf(k, n, st=1, p0=0, p1=128):
         return V("kf", k, k + n, st, p0, p1)
-    PP, Q4, HI, UP, I16, E, F12, I8, K1, R8, K8 = range(11)
-    QU, SG, W8, C48, AK, SH, VA, BF, BP, BN, NAT, FX = range(11, 23)
-    O_M, O_A, O_B, O_C, O_SG, O_UP, O_CM, O_WL, O_GL, O_NAT = 0, 2, 6, 10, 14, 18, 26, 56, 58, 60
-    NI, TG, TN, SP, K4, WS, C1, C3, RS, DEF, TK, NEG = 1440, 88, 216, 352, 488, 616, 672, 736, 928, 1248, 1280, 1392
-    iota(ci(PP), [[0, 1]], 0, 1)
-    iota(ia(0, 10), [[m, 5], [4, 2]], 16 - 2 * m)
-    iota(ia(10, 12), [[4, 2]], m + 7)
-    iota(ia(12, 14), [[-4, 2]], 8)
-    iota(tm(0, 8), [[1, 2], [4, 2], [0, 2]], 1)
+    PP, F2, F3, F4, F5, Q4, HI, LO, I16, E, G3, I8, K1, R8, K8 = range(15)
+    SG, W8, C48, AK, SH, VA, BF, BP, BN, NAT, FX, PL, X1, X2, X3 = range(15, 30)
+    O_CM, O_MA, O_AO, O_BO, O_CO, O_WL = 0, 24, 26, 28, 30, 32
+    O_AT, O_BT, O_CT, O_SG, O_MK, O_UP, O_CH, O_NAT, O_GL = 34, 36, 38, 40, 44, 46, 52, 56, 76
+    NI, TG, SP, K4, WS, C1, C3, RS, DEF, TK, NEG, KM = 0, 128, 224, 512, 608, 664, 728, 920, 1240, 1272, 1416, 1464
+    SN = 416
 
-    def field(k, sh, an):
-        ts(ci(k), ci(PP), sh, ALU.arith_shift_right, an, ALU.bitwise_and)
-    field(Q4, 0, 3)
-    field(HI, 2, 3)
-    ts(ci(UP), ci(PP), float(S), ALU.is_ge)
-    cp(V("cf", 0, 4), V("ci", 0, 4))
-    for k, sh, an in ((I16, 0, 15), (E, 0, 31), (F12, 1, 12), (I8, 3, 1), (K1, 2, 1), (R8, 2, 7), (K8, 0, 7)):
-        field(k, sh, an)
-    cp(V("cf", 4, 11), V("ci", 4, 11))
-    n0, n1, n2, n3, n6 = ib(0, 2), ib(2, 4), ib(4, 6), ib(6, 8), ib(12, 14)
-    ts(ib(0, 12), ia(0, 12), cf(HI), ALU.add)
-    ts(n6, ia(12, 14), cf(HI), ALU.subtract)
-    ts(ib(0, 14), ib(0, 14), 7, ALU.bitwise_and)
-    ts(cf(QU), cf(UP), 4.0, ALU.mult, cf(Q4), ALU.add)
-    ts(tm(8, 16), tm(0, 8), cf(QU), ALU.is_equal)
-    ts(tm(16, 18), n3, float(8 - m), ALU.is_ge, 1.0, ALU.add)
-    ts(tm(18, 20), n3, float(m), ALU.is_lt)
-    ts(tm(20, 24), ib(8, 12), 4.0, ALU.add)
-    tt(tm(24, 32), tm(8, 16), tm(16, 24), ALU.mult)
-    tt(tm(32, 36), tm(24, 28), tm(28, 32), ALU.add)
-    tt(tm(36, 38), tm(32, 34), tm(34, 36), ALU.add)
-    cp(co(O_M, 2), tm(36, 38))
-    for t in range(R):
-        mset(V("la%d" % t, 3, 13), 0.0)
-
+    def fill(out, x):
+        lin(out, kf(NI, wide(out), 1, out[1], out[2]), 0.0, float(x))
+    iota(V("ci", 0, 1), [[0, 1]], 0, 1)
     iota(kf(NI, 128), [[1, 128]])
+    for k, sh in ((F2, 2), (F3, 3), (F4, 4), (F5, 5)):
+        ts(V("ci", k, k + 1), V("ci", 0, 1), sh, ALU.arith_shift_right)
+    cp(V("cf", 0, 5), V("ci", 0, 5))
+    for k, hi, sz, lo in ((HI, F4, 4, F2), (I16, F4, 16, PP), (Q4, F2, 4, PP), (E, F5, 32, PP), (R8, F5, 8, F2), (G3, F5, 4, F3),
+                          (K1, F3, 2, F2), (K8, F3, 8, PP), (I8, F4, 2, F3)):
+        lin(cf(k), cf(hi), -float(sz), cf(lo))
+    ts(cf(LO), cf(PP), float(S), ALU.is_lt)
+    iota(tm(0, 6), [[m, 3], [4, 2]], 16 - 2 * m)
+    iota(tm(6, 8), [[-4, 2]], 8)
+    lin(tm(8, 14), tm(0, 6), 1.0, cf(HI))
+    lin(cf(X1), cf(HI), -1.0, 0.0)
+    lin(tm(14, 16), tm(6, 8), 1.0, cf(X1))
+    lin(tm(16, 17), cf(LO), m + 1.0, cf(I16))
+    lin(tm(17, 18), cf(LO), 7.0, cf(I16))
+    cp(ib(0, 10), tm(8, 18))
+    ts(ib(0, 10), ib(0, 10), 7, ALU.bitwise_and)
+    cp(tm(20, 30), ib(0, 10))
+    n0, n1, n2, n6 = tm(20, 22), tm(22, 24), tm(24, 26), tm(26, 28)
+    iota(tm(32, 56), [[1, 8], [128, 3]])
+    lin(cf(W8), cf(I16), 8.0, 0.0)
+    ts(co(O_CM, 24), tm(32, 56), cf(W8), ALU.add)
+    lin(fl(O_MA, 1), tm(28, 29), 1.0, 0.0)
+    lin(fl(O_MA + 1, 1), tm(28, 29), 1.0, 0.0)
+    lin(fl(O_AO, 2), n2, 1.0, 0.0)
+    lin(fl(O_BO, 2), n1, 2.0, float(LB))
+    lin(fl(O_CO, 2), n0, 2.0, LB + 1.0)
+    lin(fl(O_WL, 2), kf(NI, 2), 0.0, cf(E))
+    cp(co(O_MA, 10), fl(O_MA, 10))
+
     mset(V("et", 0, 516), 0.0)
-    mset(V("et", 520, 1036), 0.0)
-    ts(V("et", 3, 515, 4), kf(NI, 128), cf(PP), ALU.is_equal)
-    ts(V("et", 523, 1035, 4), kf(NI, 128), cf(PP), ALU.is_equal, -1.0, ALU.mult)
-    for b in range(4):
-        quant("ep", 128 * b, "et", 128, 3 - b)
-    for b in range(4):
-        quant("em", 128 * b, "et", 128, 523 - b)
+    for name, sign in (("em", -1.0), ("ep", 1.0)):
+        ts(V("et", 3, 515, 4), kf(NI, 128), cf(PP), ALU.is_equal, sign, ALU.mult)
+        for b in range(4):
+            quant(name, 128 * b, "et", 128, 3 - b)
 
     def dist(d):
         return (d - m) % NR
 
     def scores(t):
-        la, w = "la%d" % t, (3 if t else 2)
-        for j in range(3):
-            mm("pm", "P%d" % t, PR + S * j, "v3", 8 - 4 * j, 128, j == 0, j == 2)
-        cp(V(la, 0, 3), V("pm", t, 12, 4))
-        cp(V("ms%d" % t, 0, 32), V(la, 0, 12), co(O_M, 2))
+        la, P = "la%d" % t, "P%d" % t
+        for j, v0 in enumerate((24, 8, 0)):
+            mm("pm", P, PR + S * j, "v3", v0, 128, j == 0, j == 2)
+        cp(V(la, 0, 4), V("pm", t, 16, 4))
+
+        def pair(d):
+            c0 = 2 if m + d >= NR else 0
+            return V(la, c0, c0 + 2)
         for tab in (a1, a2):
-            push(tab, "a%d" % t, lambda d: V("ms%d" % t, 4 * dist(d), 4 * dist(d) + w),
-                 lambda d: V(la, LB + 3 * ((m - d) % NR), LB + 3 * ((m - d) % NR) + w))
-        arrive("a%d" % t, (0, 1), [V(la, LB + 3, LB + 24)], 2.8)
-        act(V(la, LB, LB + w), V("ms%d" % t, 0, w), ACT.Copy)
+            push(tab, "a%d" % t, pair, lambda d: V(la, LB + 2 * ((m - d) % NR), LB + 2 * ((m - d) % NR) + 2))
+        arrive("a%d" % t, (0, 1), [V(la, LB + 2, LB + 16)], 2.0)
+        act(V(la, LB, LB + 2), pair(m), ACT.Copy)
+        mm("pz", P, 0, "v3", 24, 128, True, True)
+        act(V(la, 4, 6), V("pz", t, t + 2), ACT.Copy)
 
-    def own_scores(t, frm):
-        for k in range(NR):
-            mm("pa", frm, S * k, "v3", 40 - 4 * k, 128, k == 0, k == NR - 1)
-        act(V("la%d" % t, 4, 12), V("pa", t, 32, 4), ACT.Copy)
+    def table(frm):
+        for k in range(NR + 1):
+            mm("pa", frm, (DO + S * k) % (DO + C), "v3", 64 - 4 * min(k, NR - 1), 128, k == 0, k == NR)
 
-    quant("P0", 0, "pt", PN)
-    quant("v3", 0, "vt", 168)
+    def tell(t, own):
+        la, ms = "la%d" % t, "ms%d" % t
+        cp(V(ms, 0, 16), own, co(O_MA, 1))
+        for tab in (a1, a2):
+            push(tab, "c%d" % t, lambda d: V(ms, (d + 7) % NR, (d + 7) % NR + 1), lambda d: V(la, LA + (m - d) % NR, LA + (m - d) % NR + 1))
+        came = arrive("c%d" % t, (0, 1), [V(la, LA + 1, LA + 8)], 2.6)
+        act(V(la, LA - 3, LA + 1), V(ms, (m + 7) % NR + 5, (m + 7) % NR + 9), ACT.Copy)
+        return came
+
+    for name, c0 in (("v3", ZC), ("P0", 0), ("Dc", 0), ("Dc", YO - 128), ("N0", 0), ("N0", YO - 128)):
+        quant(name, c0, "vt", 128, ZT)
+    quant("P0", PR, "pt", PN - PR)
+    quant("v3", 0, "vt", 128)
     scores(0)
 
     H = ["h0", "h1", "h2", "h3"]
 
     def rewrite(t, c0, n):
-        D, N_, L = "D%d" % t, "N%d" % t, "L%d" % t
+        N_, L = "N%d" % t, "L%d" % t
         for b in range(4):
-            mm(H[b], "wt", 128 * b, D, c0, n, True, True)
+            mm(H[b], "wt", 128 * b, "Dc", c0, n, True, True)
             if n > 128 and b % 2:
                 ts(V("ht", b, 4 * n, 4), V(H[b], 0, n), 0.0, ALU.max, 0.0625, ALU.mult)
             else:
                 act(V("ht", b, 4 * n, 4), V(H[b], 0, n), ACT.Relu, 0.0625)
-            mm(H[b], "em", 128 * b, D, c0, n, True, False)
+            mm(H[b], "em", 128 * b, "Dc", c0, n, True, False)
         quant(N_, c0, "ht", n)
         for b in range(4):
             mm(H[b], "ep", 128 * b, N_, c0, n, False, True)
-            if n > 128 and b % 2:
-                cp(V("hu", b, 4 * n, 4), V(H[b], 0, n))
-            else:
-                act(V("hu", b, 4 * n, 4), V(H[b], 0, n), ACT.Copy)
-        quant(L, c0, "hu", n)
+            act(V("hu", b, 4 * n, 4), V(H[b], 0, n), ACT.Copy)
+        for c in range(0, n, 128):
+            quant(L, c0 + c, "hu", 128, 4 * c)
 
-    iota(kf(TN, 96), [[1, 8], [128, 3], [0, 4]])
-    iota(kf(TN + 96, 36), [[1, 3], [128, 3], [0, 4]])
-    ts(cf(W8), cf(I16), 8.0, ALU.mult)
-    act(kf(TN, 132), kf(TN, 132), ACT.Identity, 1.0, None, cf(W8))
-    cp(co(O_CM, 30), kf(TN, 120, 4))
-    quant("D0", C, "vt", 128, 176)
     quant("D0", 0, "xt", C)
-    pick("Dc", 0, "D0", C, co(O_CM, 29))
-    own_scores(0, "Dc")
-    cp(V("msb", 0, 32), V("la0", 0, 12), co(O_M, 2))
-    for tab in (a1, a2):
-        push(tab, "ab", lambda d: V("msb", 4 * dist(d) + 2, 4 * dist(d) + 3),
-             lambda d: V("la0", LB + 3 * ((m - d) % NR) + 2, LB + 3 * ((m - d) % NR) + 3))
-    arrive("ab", (0, 1), [V("la0", LB + 3, LB + 24)], 2.8)
-    act(V("la0", LB + 2, LB + 3), V("msb", 2, 3), ACT.Copy)
-    rewrite(0, 0, C)
+    pick("Dc", DO, "D0", C, co(O_CM, 24))
+    table("Dc")
+    act(V("a0", 0, 8), V("pa", 0, 32, 4), ACT.Copy)
+    act(V("aa0", 16, 24), V("pa", 2, 32, 4), ACT.Copy)
+    act(V("aa0", 24, 32), V("pa", 1, 32, 4), ACT.Copy)
+    mine = [V("a0", 0, 8), V("aa1", 24, 32), V("aa2", 16, 24)]
+    told = tell(0, mine[0])
+    rewrite(0, DO, C)
+    table("N0")
+    act(V("aa0", 0, 8), V("pa", 2, 32, 4), ACT.Copy)
+    act(V("aa0", 8, 16), V("pa", 1, 32, 4), ACT.Copy)
+    for dst, d0, n in (("P1", 0, PR), ("P1", PN - 32, 32), ("P2", 0, PR), ("P2", PN - 32, 32), ("P3", 2 * S, 32), ("N1", 0, DO), ("N1", DE, YO - DE)):
+        u, v = V(dst + "q", d0, d0 + n), V("v3q", ZC, ZC + n)
+        loads.append(dma("s", "l%d" % len(loads), lambda u=u: ap(u).bitcast(dt.uint8), lambda v=v: ap(v).bitcast(dt.uint8), [v], [u], 2.0, [told]))
+        u, v = V(dst + "s", d0, d0 + n), V("v3s", ZC, ZC + n)
+        loads.append(dma("s", "l%d" % len(loads), lambda u=u: ap(u), lambda v=v: ap(v), [v], [u], 2.0, [told]))
 
-    ts(co(O_A, 2), n2, 4.0, ALU.add)
-    ts(co(O_A + 2, 2), n1, 3.0, ALU.mult, LB + 2.0, ALU.add)
-    ts(co(O_B, 2), n1, 3.0, ALU.mult, LB + 0.0, ALU.add)
-    ts(co(O_C, 2), n0, 3.0, ALU.mult, LB + 1.0, ALU.add)
-    ts(tm(40, 42), n2, 3.0, ALU.mult, LB + 0.0, ALU.add)
-    ts(tm(42, 44), n2, float(8 - m), ALU.is_ge, 1.0, ALU.add)
-    fill(tm(44, 46), 2)
-    ts(tm(46, 48), n6, 3.0, ALU.mult, LB + 1.0, ALU.add)
-    tt(tm(48, 52), tm(44, 48), tm(40, 44), ALU.subtract)
-    ts(tm(48, 52), tm(48, 52), cf(UP), ALU.mult)
-    tt(tm(52, 56), tm(48, 52), tm(40, 44), ALU.add)
-    cp(co(O_B + 2, 2), tm(52, 54))
-    cp(co(O_C + 2, 2), tm(54, 56))
-    iota(ia(16, 20), [[16, 2], [0, 2]], 4 * m)
-    ts(cf(SG), cf(K1), float(4 * m), ALU.mult, cf(Q4), ALU.add)
-    ts(ib(16, 20), ia(16, 20), cf(F12), ALU.add, cf(SG), ALU.add)
-    ts(ib(16, 20), ib(16, 20), 31, ALU.bitwise_and)
-    cp(co(O_SG, 4), ib(16, 20))
-    iota(tm(56, 59), [[-1, 3]], 3)
-    mset(V("zz", 144, 224, 1, 32, 64), 0.0)
-    ts(tm(60, 63), tm(56, 59), cf(Q4), ALU.is_le, -0.5, ALU.add)
-    ts(V("zz", 13, 16), tm(60, 63), 2.0 * BIG, ALU.mult)
-    mset(kf(NEG, 48), -BIG)
+    lin(fl(O_AT, 2), n1, 1.0, 3.0)
+    lin(tm(56, 58), n2, 2.0, LB - 4.0)
+    lin(fl(O_BT, 2), tm(56, 58), cf(LO), 4.0)
+    ts(tm(58, 60), n2, float(8 - m), ALU.is_ge, 2.0, ALU.mult)
+    ts(tm(60, 62), n2, float(m), ALU.is_gt, LB - 1.0, ALU.add)
+    for c in range(2):
+        lin(tm(62 + c, 63 + c), tm(26 + c, 27 + c), 2.0, tm(60 + c, 61 + c))
+        lin(tm(64 + c, 65 + c), tm(62 + c, 63 + c), -1.0, tm(58 + c, 59 + c))
+        lin(tm(66 + c, 67 + c), tm(62 + c, 63 + c), 1.0, 1.0)
+        lin(fl(O_CT + c, 1), tm(64 + c, 65 + c), cf(LO), tm(66 + c, 67 + c))
+    iota(tm(68, 72), [[16, 2], [0, 2]], 4 * m)
+    lin(cf(X2), cf(K1), float(4 * m), cf(Q4))
+    lin(cf(SG), cf(G3), 4.0, cf(X2))
+    ts(ib(10, 14), tm(68, 72), cf(SG), ALU.add)
+    ts(ib(10, 14), ib(10, 14), 31, ALU.bitwise_and)
+    cp(fl(O_SG, 4), ib(10, 14))
+    lin(tm(72, 73), tm(29, 30), 1.0, 1.0)
+    ts(tm(73, 74), tm(72, 73), 8.0, ALU.is_lt, tm(72, 73), ALU.mult)
+    lin(tm(74, 75), tm(73, 74), 4.0, 3.0)
+    lin(fl(O_MK, 2), kf(NI, 2), 0.0, tm(74, 75))
+    iota(kf(KM, 32), [[S, 8], [0, 4]])
+    lin(cf(PL), cf(LO), float(S), cf(PP))
+    lin(kf(KM, 32), kf(KM, 32), 1.0, cf(PL))
+    iota(tm(76, 79), [[-1, 3]], 3)
+    ts(tm(80, 83), tm(76, 79), cf(Q4), ALU.is_le, -0.5, ALU.add)
+    lin(V("zz", 13, 16), tm(80, 83), 2.0 * BIG, 0.0)
+    fill(kf(NEG, 48), -BIG)
     fill(kf(WS, 52), 1)
     fill(kf(WS + 3, 1), -1)
-    fill(V("ww", 155, 192), int(-US / 2))
-    ts(cf(C48), cf(R8), float(S), ALU.mult)
+    fill(V("ww", 155, 192), -US / 2)
+    lin(cf(C48), cf(R8), float(S), float(DO))
     ts(cf(SH, 96), cf(R8, 96), float(8 - m), ALU.is_ge)
-    ts(cf(AK, 64), cf(E, 64), 32.0, ALU.add)
-    ts(cf(FX, 96), cf(E, 96), -2.0, ALU.mult, -32.0 * S, ALU.add)
-    ts(cf(AK, 96), cf(SH, 96), -32.0, ALU.mult, cf(AK, 96), ALU.add)
-    act(V("tt", 0, 84, 1, 0, 64), kf(NI, 84, 1, 0, 64), ACT.Identity, 8.0, None, cf(R8, 0, 64))
-    act(V("tt", 0, 84, 1, 64), kf(NI, 84, 1, 64), ACT.Identity, 32.0, None, cf(AK, 64))
-    ts(V("tt", 0, 1, 1, 96), cf(FX, 96), cf(SH, 96), ALU.mult, cf(AK, 96), ALU.add)
-    ts(cf(VA, 64), cf(R8, 64), 16.0, ALU.mult, cf(Q4, 64), ALU.add)
-    ts(cf(VA, 96), cf(VA, 96), 4.0, ALU.add)
-    ts(cf(BF, 64), cf(E, 64), -1.0, ALU.mult, -0.5, ALU.add)
-    ts(cf(BP, 64, 96), cf(E, 64, 96), -1.0 / 32, ALU.mult, PR - 1.0, ALU.add)
-    ts(cf(BP, 96), cf(E, 96), -1.0 / 32, ALU.mult, PR - 1.0 + S, ALU.add)
-    mset(cf(BN, 64, 96), PN + 15.5)
-    mset(cf(BN, 96), PN + 47.5)
-    mset(V("sa", 64, 65), -BIG)
+    lin(cf(32, 64), cf(E, 64), 1.0, 32.0)
+    lin(cf(AK, 64, 96), cf(E, 64, 96), 1.0, 32.0)
+    lin(cf(FX, 96), cf(E, 96), -2.0, -32.0 * S)
+    lin(cf(AK, 96), cf(SH, 96), -32.0, cf(32, 96))
+    lin(V("tt", 0, 84, 1, 0, 32), kf(NI, 84, 1, 0, 32), 1.0, cf(C48, 0, 32))
+    lin(V("tt", 0, 84, 1, 64), kf(NI, 84, 1, 64), 32.0, cf(AK, 64))
+    lin(V("tt", 0, 1, 1, 96), cf(FX, 96), cf(SH, 96), cf(AK, 96))
+    lin(cf(VA, 64), cf(R8, 64), 16.0, cf(Q4, 64))
+    lin(cf(VA, 96), cf(VA, 96), 1.0, 4.0)
+    lin(cf(BF, 64), cf(E, 64), -1.0, -0.5)
+    lin(cf(BP, 64, 96), cf(E, 64, 96), -1.0 / 32, PR - 1.0)
+    lin(cf(BP, 96), cf(E, 96), -1.0 / 32, PR - 1.0 + S)
+    fill(cf(BN, 64, 96), PN + 15.5)
+    fill(cf(BN, 96), PN + 47.5)
+    fill(V("sa", 64, 65), -BIG)
     iota(kf(C1, 64), [[32, 2], [0, 2], [2, 16]], -31)
     iota(kf(C3, 96), [[16, 3], [0, 2], [1, 16]], PR)
-    ts(kf(C3, 96, 1, 96), kf(C3, 96, 1, 96), float(S), ALU.add)
-    iota(kf(C3 + 96, 96), [[16, 3], [0, 2], [1, 16]], PR + S - 1)
+    lin(kf(C3 + 96, 96), kf(C3, 96), 1.0, S - 1.0)
+    lin(kf(C3, 96, 1, 96), kf(C3, 96, 1, 96), 1.0, float(S))
     fill(kf(C3 + 96, 17, 16), PR + 2 * S - 1)
-    iota(kf(RS, 320), [[0, 10], [1000, 32]])
-    iota(tm(64, 72), [[2, 2], [10, 2], [1, 2]])
-    fill(tm(72, 96), 20)
-    iota(tm(77, 80), [[1, 3]], 4)
-    iota(tm(80, 86), [[1, 6]], 14)
-    iota(tm(86, 89), [[1, 3]], 4)
-    fill(tm(96, 98), 0)
-    ts(co(O_WL, 2), tm(96, 98), cf(E), ALU.add)
-    cp(V("wf", 0, 32), tm(64, 96), co(O_WL, 2))
+    iota(kf(RS, 192), [[0, 6], [1000, 32]])
+    iota(tm(96, 104), [[2, 2], [4, 2], [1, 2]])
+    iota(fl(80, 8), [[2, 2], [-4, 2], [1, 2]], 4)
+    fill(tm(104, 128), 8)
+    lin(tm(112, 115), kf(NI, 3), 1.0, 0.0)
+    lin(tm(115, 121), kf(NI, 6), 1.0, 6.0)
+    lin(tm(121, 124), kf(NI, 3), 1.0, 9.0)
+    for a in (1, 3):
+        p0, p1 = 32 * a, 32 * a + 32
+        lin(V("tm", 96, 104, 1, p0, p1), V("fl", 80, 88, 1, p0, p1), 1.0, 0.0)
+        lin(V("tm", 112, 115, 1, p0, p1), V("tm", 112, 115, 1, p0, p1), 1.0, 6.0)
+        lin(V("tm", 115, 124, 1, p0, p1), V("tm", 115, 124, 1, p0, p1), 1.0, -6.0)
+    cp(V("wf", 0, 32), tm(96, 128), co(O_WL, 2))
     tr(V("ff", 0, 32), V("wf", 0, 32))
-    cp(co(O_GL, 2), V("ff", 0, 32, 16))
-    fill(V("wb", 20, 24), 0)
-    fill(kf(DEF, 12), 0)
-    iota(kf(DEF + 12, 20), [[16, 20]])
-    act(kf(DEF + 12, 20), kf(DEF + 12, 20), ACT.Identity, 1.0, None, cf(I16))
-    fill(kf(TK, 112), 0)
+    cp(co(O_GL, 4), V("ff", 0, 32, 8))
+    fill(V("wb", 8, 9), 0)
+    lin(cf(X3), cf(I16), 1.0, float(PR))
+    lin(kf(DEF, 16), kf(NI, 16), 16.0, cf(X3))
+    fill(kf(TK, 72), 0)
+    fill(kf(TK + 72, 72), 0)
     fill(kf(TK, 1), 1)
-    iota(kf(TG, 96), [[16, 24], [0, 4]])
-    iota(kf(TG + 96, 32), [[16, 8], [0, 4]])
-    act(kf(TG, 128), kf(TG, 128), ACT.Identity, 1.0, None, cf(I16))
+    iota(kf(TG, 96), [[16, 24], [0, 4]], DO)
+    lin(kf(TG, 96), kf(TG, 96), 1.0, cf(I16))
     k = 0
-    while k < 11:
+    while k < NR:
         dl = (k - m) % NR
-        n = min(NR - dl, 11 - k)
+        n = min(NR - dl, NR - k)
         iota(kf(SP + 12 * k, 12 * n), [[8, n], [0, 3], [1, 4]], YO + 8 * dl)
         k += n
-    iota(kf(K4, 128), [[0, 32], [1000, 4]])
-    iota(ia(24, 32), [[4, 8]], -1)
-    ts(tm(100, 108), ia(24, 32), cf(HI), ALU.add, 1.0 / 3.0, ALU.mult)
-    cp(ib(24, 32), tm(100, 108))
-    ts(ib(24, 32), ib(24, 32), 7, ALU.bitwise_and)
-    ts(co(O_UP, 8), ib(24, 32), 4.0, ALU.mult, cf(Q4), ALU.add)
-    iota(ia(32, 56), [[2, 24]])
-    ts(cf(NAT), cf(K8), float(S), ALU.mult, cf(I8), ALU.add)
-    ts(co(O_NAT, 24), ia(32, 56), cf(NAT), ALU.add)
+    lin(kf(SP + 96, 96), kf(SP, 96), 1.0, 64.0)
+    iota(kf(K4, 96), [[0, 24], [1000, 4]])
+    lin(cf(X1), cf(HI), 1.0 / 3.0, -1.0 / 3.0)
+    lin(tm(84, 90), kf(NI, 6), 4.0 / 3.0, cf(X1))
+    cp(ib(16, 22), tm(84, 90))
+    ts(fl(O_UP, 6), ib(16, 22), 4.0, ALU.mult, cf(Q4), ALU.add)
+    lin(cf(NAT), cf(K8), float(S), cf(I8))
+    lin(cf(NAT), cf(NAT), 1.0, float(DO))
+    lin(fl(O_NAT, 24), kf(NI, 24), 2.0, cf(NAT))
+    lin(cf(33), cf(F5), -2.0, cf(F4))
+    lin(cf(30), cf(K8), 4.0, cf(33))
+    iota(tm(90, 94), [[2, 2], [0, 2]])
+    lin(fl(O_CH, 4), tm(90, 94), 1.0, cf(30))
+    ts(cf(34), cf(K8), float(m), ALU.is_lt, 64.0, ALU.mult)
+    lin(cf(31), cf(K8), 8.0, cf(34))
+    iota(kf(SN, 12), [[64, 3], [1, 4]], YO - 8 * m)
+    lin(kf(SN, 12), kf(SN, 12), 1.0, cf(31))
+    cp(co(O_AT, 10), fl(O_AT, 10))
+    cp(co(O_MK, 12), fl(O_MK, 12))
 
-    def Z(c0, c1, st=1):
-        return V("zz", c0, c1, st)
+    def choose(p0, p1):
+        def Z(c0, c1, st=1):
+            return V("zz", c0, c1, st, p0, p1)
 
-    def W(c0, c1):
-        return V("ww", c0, c1)
+        def W(c0, c1):
+            return V("ww", c0, c1, 1, p0, p1)
+        sc0 = Z(160, 208)
+        scan(Z(16, 160, 3), sc0, kf(NEG, 48, 1, p0, p1), Z(13, 14), ALU.min, ALU.max)
+        scan(Z(17, 160, 3), sc0, Z(13, 157, 3), Z(14, 15), ALU.min, ALU.max)
+        scan(Z(18, 160, 3), sc0, Z(14, 158, 3), Z(15, 16), ALU.min, ALU.max)
+        scan(W(0, 48), sc0, Z(15, 159, 3), BIG, ALU.min, ALU.max)
+        ts(W(48, 99), Z(157, 208), W(47, 48), ALU.is_equal, US, ALU.mult)
+        scan(W(104, 155), kf(WS, 51, 1, p0, p1), W(48, 99), -US / 2, ALU.mult, ALU.subtract)
+        scan(W(192, 272), W(107, 187), V("tt", 1, 81, 1, p0, p1), V("tt", 0, 1, 1, p0, p1), ALU.max, ALU.min)
 
     def Q(name, a, c0, n=32, st=1):
         return V(name, c0, c0 + n, st, 32 * a, 32 * a + 32)
@@ -484,81 +524,100 @@ def rank_program(g, core, T, topo):
     def U(name, c0, c1, st=1):
         return V(name, c0, c1, st, 64, 128)
 
+    held = fl(O_NAT, 24)
     for t in range(R):
-        win = V("la%d" % t, 0, LB + 24)
-        D, N_, L, P, G, HS, SS = ("%s%d" % (x, t) for x in "DNLPGHS")
+        la = "la%d" % t
+        win = V(la, 0, LB + 16)
+        N_, L, P, G, HS, SS = ("%s%d" % (x, t) for x in "NLPGHS")
         osn, oup, ow = ("%s%d" % (x, t) for x in ("osn", "oup", "ow"))
-        cp(V("nn", 0, 64), win, co(O_A, 4))
-        tt(V("nn", 64, 128), win, V("nn", 0, 64), ALU.subtract, co(O_B, 4))
-        tt(V("nn", 128, 192), win, V("nn", 64, 128), ALU.add, co(O_C, 4))
-        tr(Q("zz", 0, 160), Q("nn", 0, 128))
-        tr(Q("zz", 0, 192), Q("nn", 1, 128))
+        cp(V("nn", 0, 32), mine[t], co(O_AO, 2))
+        tt(V("nn", 32, 64), win, V("nn", 0, 32), ALU.subtract, co(O_BO, 2))
+        tt(V("nn", 64, 96), win, V("nn", 32, 64), ALU.add, co(O_CO, 2))
+        tr(Q("zz", 0, 160), Q("nn", 0, 64))
+        tr(Q("zz", 0, 192), Q("nn", 1, 64))
+        choose(0, 32)
+        a, off = V(la, LA - 3, LA + 8), co(O_AT, 2)
+        add("v", lambda a=a, off=off: g.vector.tensor_copy(ap(V("nn", 96, 128)), src(a, off)), [a, off, V(la, 0, 4)], [V("nn", 96, 128)], 0.108)
+        tt(V("nn", 128, 160), win, V("nn", 96, 128), ALU.subtract, co(O_BT, 2))
+        tt(V("nn", 160, 192), win, V("nn", 128, 160), ALU.add, co(O_CT, 2))
         tr(Q("zz", 2, 144), Q("nn", 1, 160))
         tr(Q("zz", 2, 176), Q("nn", 2, 160))
         tr(Q("zz", 3, 160), Q("nn", 0, 160))
         tr(Q("zz", 3, 192), Q("nn", 1, 160))
-        sc0 = Z(160, 208)
-        scan(Z(16, 160, 3), sc0, kf(NEG, 48), Z(13, 14), ALU.min, ALU.max)
-        scan(Z(17, 160, 3), sc0, Z(13, 157, 3), Z(14, 15), ALU.min, ALU.max)
-        scan(Z(18, 160, 3), sc0, Z(14, 158, 3), Z(15, 16), ALU.min, ALU.max)
-        scan(W(0, 48), sc0, Z(15, 159, 3), BIG, ALU.min, ALU.max)
-        ts(W(48, 99), Z(157, 208), W(47, 48), ALU.is_equal, US, ALU.mult)
-        scan(W(104, 155), kf(WS, 51), W(48, 99), -US / 2, ALU.mult, ALU.subtract)
-        scan(W(192, 272), W(107, 187), V("tt", 1, 81), V("tt", 0, 1), ALU.max, ALU.min)
+        choose(64, 128)
         for a in range(4):
             tr(Q("ff", a, 0), Q("ww", 0, 240))
         cp(V("ff", 32, 96), V("ff", 0, 32), co(O_SG, 4))
         tr(V("ff", 96, 160), V("ff", 32, 96))
         cp(V(osn, 0, 4), V("ff", 96, 160, 16))
-        pick(SS, 0, L, C, V(osn, 0, 4))
+        pick(SS, 0, L, DE, V(osn, 0, 4))
         push(b1, "b%d" % t, lambda d: V(SS + "q", 8 * dist(d), 8 * dist(d) + 8), lambda d: V(G + "q", 16 * m, 16 * m + 8), True)
         push(b2, "b%d" % t, lambda d: V(SS + "s", 8 * dist(d), 8 * dist(d) + 8), lambda d: V(G + "s", 16 * m, 16 * m + 8))
-        came = arrive("b%d" % t, (2, 3), [V(G + x, 16 * r, 16 * r + 16) for x in "qs" for r in range(NR) if r != m], 3.6)
+        came = arrive("b%d" % t, (2, 3), [V(G + x, 16 * r, 16 * r + 16) for x in "qs" for r in range(NR) if r != m], 2.9)
         if t == 0:
             load("s", V("uf", 0, 512), lambda: T.u[:], 2.5, [came])
             load("s", V("vf", 0, 512), lambda: T.v[:], 2.5, [came])
-            act(V("tt", 0, 84, 1, 0, 64), kf(NI, 84, 1, 0, 64), ACT.Identity, 1.0, None, cf(C48, 0, 64))
             quant("un", 0, "uf", 128)
             quant("vn", 0, "vf", 128)
-        pick(G, 16 * m, L, C, V(osn, 0, 1))
-        pick(D, YO, N_, C, V(osn, 0, 4))
+        if t < R - 1:
+            aa, ab = "aa%d" % t, "aa%d" % (t + 1)
+            tt(V("mk", 0, 32), V("ff", 0, 32), kf(KM, 32), ALU.is_equal)
+            scan(V("mk", 32, 64), kf(K4, 32), V("mk", 0, 32), 0.0, ALU.min, ALU.max)
+            tt(V("mk", 64, 96), V("mk", 32, 64), V(aa, 0, 32), ALU.mult, co(O_MK, 2))
+            tt(V("mk", 96, 112), V(aa, 16, 32), V("mk", 80, 96), ALU.subtract)
+            tt(V(ab, 16, 32), V("mk", 96, 112), V("mk", 64, 80), ALU.add)
+            tell(t + 1, mine[t + 1])
+        pick(G, 16 * m, L, DE, V(osn, 0, 1))
+        pick("Dc", YO + 64 * t, N_, DE, V(osn, 0, 4))
         key = U("sa", 0, 1)
         act(U("sa", 0, 32), U("ww", 240, 272), ACT.Abs)
         tr(U("sa", 32, 64), U("sa", 0, 32))
         act(U("sc", 1, 2), key, ACT.Identity, 1.0, None, cf(BF, 64))
         act(U("sc", 2, 3), key, ACT.Identity, 1.0 / 32, None, cf(BP, 64))
         act(U("sa", 72, 104), U("sa", 32, 64), ACT.Sign, -1.0, None, key, U("sc", 0, 1))
-        act(U("sa", 72, 105), U("sa", 32, 65), ACT.Sign, -1.0, None, U("sc", 1, 2), U("sc", 3, 4))
+        act(U("sa", 104, 137), U("sa", 32, 65), ACT.Sign, -1.0, None, U("sc", 1, 2), U("sc", 3, 4))
         act(U("sc", 4, 5), U("sc", 0, 1), ACT.Identity, 0.5, None, cf(BN, 64))
-        ts(U("sc", 5, 6), U("sc", 3, 4), U("sc", 0, 1), ALU.is_equal, U("sc", 2, 3), ALU.mult)
         ts(U("oh", 0, 64), kf(C1, 64, 1, 64), U("sc", 0, 1), ALU.is_equal, cf(VA, 64), ALU.mult)
-        ts(U("oh", 64, 128), kf(C1, 64, 1, 64), U("sc", 0, 1), ALU.is_equal, U("sc", 5, 6), ALU.mult)
+        ts(U("oh", 64, 128), kf(C1, 64, 1, 64), U("sc", 3, 4), ALU.is_equal, U("sc", 2, 3), ALU.mult)
         ts(U("oh", 128, 320), kf(C3, 192, 1, 64), U("sc", 2, 3), ALU.is_equal, U("sc", 4, 5), ALU.mult)
-        tr(U("ot", 0, 320), U("oh", 0, 320))
-        scan(U("oc2", 0, 320), kf(RS, 320, 1, 64), U("ot", 0, 320), 0.0, ALU.min, ALU.max)
-        cp(Q("wb", 2, 0, 10), Q("oc2", 2, 31, 289, 32))
-        act(Q("wb", 3, 0, 10), Q("oc2", 2, 31, 289, 32), ACT.Copy)
-        act(Q("wb", 2, 10, 10), Q("oc2", 3, 31, 289, 32), ACT.Copy)
-        cp(Q("wb", 3, 10, 10), Q("oc2", 3, 31, 289, 32))
-        cp(V("wb", 0, 20, 1, 0, 64), U("wb", 0, 20))
-        tt(V("wf", 0, 32), V("wb", 0, 24), kf(DEF, 32), ALU.max, co(O_GL, 2))
-        cp(V(ow, 0, 32), V("wf", 0, 32))
-        pick(HS, 64, P, PN, V(ow, 4, 12))
+        for c0, n, w in ((0, 4, 0), (128, 6, 16)):
+            c1 = c0 + 32 * n
+            tr(U("ot", c0, c1), U("oh", c0, c1))
+            scan(U("oc2", c0, c1), kf(RS, 32 * n, 1, 64), U("ot", c0, c1), 0.0, ALU.min, ALU.max)
+            cp(U("wb", w, w + n), U("oc2", c0 + 31, c1, 32))
+            act(V("wb", w, w + n, 1, 0, 64), U("oc2", c0 + 31, c1, 32), ACT.Copy)
+            for a in range(4):
+                args = Q("wb", a, w + n, n), Q("oc2", 3 - a % 2, c0 + 31, 32 * n - 31, 32)
+                if a % 2:
+                    cp(*args)
+                else:
+                    act(*args, ACT.Copy)
+        cp(V(ow, 0, 16), V("wb", 0, 9), co(O_GL, 1))
+        tt(V("wf", 0, 16), V("wb", 16, 28), kf(DEF, 16), ALU.max, co(O_GL + 2, 1))
+        cp(V(ow, 16, 32), V("wf", 0, 16))
+        pick(HS, 64, P, PR + 2 * S, V(ow, 4, 12))
         for b in range(4):
             mm(H[b], "ep", 128 * b, HS, 64, 128, True, False)
         kp = V("kp", 0, 64)
-        act(kp, kf(TK, 112), ACT.Copy, off=V(ow, 4, 8))
-        tg = TG if t else TN
-        tt(V("up", 0, 128), V("ff", 0, 32), kf(tg, 128), ALU.is_equal, co(O_UP, 8))
-        tt(V("up", 128, 256), V("up", 0, 128), kf(SP, 128), ALU.mult)
-        scan(V("up", 256, 384), kf(K4, 128), V("up", 128, 256), 0.0, ALU.min, ALU.max)
-        tt(V("up", 0, 32), V("up", 259, 384, 4), kf(tg, 128, 4), ALU.max)
-        cp(V(oup, 0, 32), V("up", 0, 32))
-        pick("D%d" % (t + 1), 0, D, 528, V(oup, 0, 29 if t < R - 1 else 24))
+        act(kp, kf(TK, 144), ACT.Copy, off=V(ow, 4, 8))
         if t < R - 1:
-            own_scores(t + 1, "D%d" % (t + 1))
-        else:
-            pick("Dn", 0, "D3", C, co(O_NAT, 24))
+            tt(V("up", 0, 96), V("ff", 0, 32), kf(TG, 96), ALU.is_equal, co(O_UP, 6))
+            tt(V("up", 96, 192), V("up", 0, 96), kf(SP + 96 * t, 96), ALU.mult)
+            scan(V("up", 192, 288), kf(K4, 96), V("up", 96, 192), 0.0, ALU.min, ALU.max)
+            tt(V("up", 288, 312), V("up", 195, 288, 4), kf(TG, 96, 4), ALU.max)
+            cp(V(oup, 0, 24), V("up", 288, 312))
+        cp(V("un2", 0, 64), V("ff", 0, 32), co(O_CH, 4))
+        tr(V("un2", 64, 128), V("un2", 0, 64))
+        for q in range(4):
+            ts(V("un2", 128 + 24 * q, 152 + 24 * q), fl(O_NAT, 24), V("un2", 64 + 16 * q, 65 + 16 * q), ALU.is_equal, kf(SN + 4 * t + q, 1), ALU.mult)
+        tt(V("un2", 224, 272), V("un2", 128, 176), V("un2", 176, 224), ALU.max)
+        tt(V("un2", 272, 296), V("un2", 224, 248), V("un2", 248, 272), ALU.max)
+        now = V("un2", 296 + 24 * t, 320 + 24 * t)
+        tt(now, V("un2", 272, 296), held, ALU.max)
+        held = now
+        if t == R - 1:
+            cp(V(oup, 0, 24), now)
+            pick("Dn", 0, "Dc", YO + 64 * R, V(oup, 0, 24))
             mm("py", "un", 0, "Dn", 0, C, True, True)
             dma("s", "stS", lambda: T.oc[:, 0:4 * C], lambda: T["Dnq"][:].bitcast(dt.uint8), [V("Dnq", 0, C)], [], 2.7)
             for k in range(4):
@@ -570,22 +629,25 @@ def rank_program(g, core, T, topo):
             mm(H[b], "ep", 128 * b, HS, 0, 128, False, True)
             scan(V("nt", b, 256, 4), kp, V(H[b], 0, 64), 0.0, ALU.mult, ALU.add)
         quant(P, PN, "nt", 128)
-        pick("P%d" % (t + 1), 0, P, 368, V(ow, 12, 27 if t < R - 1 else 21))
+        pick("P%d" % (t + 1), PR if t < R - 1 else 0, P, PN + 128, V(ow, 16, 28 if t < R - 1 else 22))
         if t < R - 1:
             scores(t + 1)
-            rewrite(t, YO - 64, 128)
-            pick("N%d" % (t + 1), 0, N_, 528, V(oup, 0, 24))
-            pick("L%d" % (t + 1), 0, L, 528, V(oup, 0, 24))
-    mm("pz", "vn", 0, "P3", PR, 128, True, True)
-    dma("s", "stS", lambda: T.oc[:, 4 * C:4 * C + 8 * S], lambda: T["P3q"][:, PR:PR + 2 * S].bitcast(dt.uint8), [V("P3q", PR, PR + 2 * S)], [])
+            rewrite(t, YO + 64 * t - 64, 128)
+            pick("L%d" % (t + 1), DO, L, 640, V(oup, 0, 24))
+            pick("N%d" % (t + 1), DO, N_, 640, V(oup, 0, 24))
+        if t == 0:
+            table("N1")
+            act(V("aa1", 0, 16), V("pa", 2, 64, 4), ACT.Copy)
+    mm("pz", "vn", 0, "P3", 0, 128, True, True)
+    dma("s", "stS", lambda: T.oc[:, 4 * C:4 * C + 8 * S], lambda: T["P3q"][:, 0:2 * S].bitcast(dt.uint8), [V("P3q", 0, 2 * S)], [])
     for k in range(4):
         dma("a" if k % 2 else "s", "stA" if k % 2 else "stS", lambda k=k: T.osc[4 * k:4 * k + 4, C:C + 2 * S],
-            lambda k=k: T["P3s"][32 * k:32 * k + 4, PR:PR + 2 * S], [V("P3s", PR, PR + 2 * S)], [])
+            lambda k=k: T["P3s"][32 * k:32 * k + 4, 0:2 * S], [V("P3s", 0, 2 * S)], [])
     cp(V("yb", C, C + 2 * S), V("pz", 0, 2 * S))
     dma("a", "stA", lambda: T.y[:, C:C + 2 * S], lambda: T["yb"][:, C:C + 2 * S], [V("yb", C, C + 2 * S)], [])
 
     ops = arrange(ops)
-    first = loads[:10]
+    first = loads[:12]
     ops = first + [o for o in ops if not any(o is x for x in first)]
     clock, seq = {q: {} for q in eng}, {q: 0 for q in eng}
     for i, o in enumerate(ops):

@@ -6,11 +6,9 @@ ACT = ActivationFunctionType
 NR, C, S, R = 8, 384, 48, 3
 BIG = 1.0e29
 US = 262144.0
-DO, YO = 48, 512
-DE = DO + C
-PR = 48
-PN = 272
-LB, LA = 6, 27
+YO = C
+PR, PN = 32, 128
+LB, LA = 98, 123
 
 SCRATCH = {}
 
@@ -20,35 +18,35 @@ def _pair(name, n):
     SCRATCH[name + "s"] = ("sbuf", [128, n], "uint8")
 
 
-for _n, _w in (("D0", C), ("Dc", 704), ("v3", 256), ("vn", 128), ("un", 128), ("ep", 512), ("em", 512),
+for _n, _w in (("Dc", 528), ("v0", 128), ("vr", 132), ("u1", 128), ("ur", 128), ("vn", 128), ("un", 128), ("ep", 512), ("em", 512),
                ("wt", 512), ("Dn", C),
-               ("N0", 640), ("N1", 640), ("N2", DE), ("L0", 640), ("L1", 640), ("L2", DE),
-               ("P0", 400), ("P1", 400), ("P2", 400), ("P3", 128)):
+               ("N0", 512), ("N1", 512), ("N2", C), ("L0", 512), ("L1", 512), ("L2", C),
+               ("P0", 256), ("P1", 256), ("P2", 256), ("P3", 128)):
     _pair(_n, _w)
 for _t in range(R):
-    _pair("S%d" % _t, 64)
-    _pair("G%d" % _t, 128)
+    _pair("S%d" % _t, 48)
+    _pair("G%d" % _t, 176)
     _pair("H%d" % _t, 192)
-    SCRATCH["la%d" % _t] = ("sbuf", [128, 40], "float32")
+    SCRATCH["la%d" % _t] = ("sbuf", [128, 136], "float32")
     SCRATCH["ms%d" % _t] = ("sbuf", [128, 16], "float32")
     SCRATCH["aa%d" % _t] = ("sbuf", [128, 32], "float32")
     SCRATCH["osn%d" % _t] = ("sbuf", [128, 4], "uint16")
     SCRATCH["oup%d" % _t] = ("sbuf", [128, 24], "uint16")
     SCRATCH["ow%d" % _t] = ("sbuf", [128, 32], "uint16")
-for _n, _w in (("xt", 1536), ("pt", 896), ("vt", 784), ("vf", 512), ("uf", 512),
-               ("et", 520), ("ht", 1536), ("hu", 1536), ("nt", 512)):
+for _n, _w in (("bt", 2304), ("vz", 528), ("sv", 16), ("vf", 512), ("uf", 512), ("et", 520), ("ht", 1536), ("hu", 1536)):
     SCRATCH[_n] = ("sbuf", [128, _w], "bfloat16")
-for _n, _w in (("cf", 40), ("kf", 1600), ("tt", 84), ("yb", 480), ("nn", 192), ("zz", 224), ("ww", 272),
-               ("ff", 160), ("sa", 144), ("sc", 8), ("oh", 320), ("ot", 320), ("oc2", 320), ("wb", 32), ("wf", 32),
-               ("up", 312), ("un2", 368), ("kp", 64), ("tm", 128), ("fl", 96), ("mk", 112), ("a0", 8)):
+for _n, _w in (("cf", 48), ("kf", 1600), ("tt", 84), ("yb", 480), ("nn", 288), ("zz", 224), ("ww", 272),
+               ("ff", 64), ("sa", 144), ("sc", 8), ("oh", 320), ("ot", 320), ("oc2", 320), ("wb", 32), ("wf", 32),
+               ("ar", 384), ("ag", 128), ("ta", 128), ("un2", 392), ("kp", 64), ("tm", 192), ("fl", 96), ("mk", 112),
+               ("a0", 8), ("sr", 192), ("mg", 96), ("gl", 192)):
     SCRATCH[_n] = ("sbuf", [128, _w], "float32")
-for _n, _w in (("ci", 8), ("ib", 32)):
+for _n, _w in (("ci", 16), ("ib", 64)):
     SCRATCH[_n] = ("sbuf", [128, _w], "int32")
 SCRATCH["co"] = ("sbuf", [128, 96], "uint16")
 for _n in ("h0", "h1", "h2", "h3", "pa", "pm", "py", "pz"):
     SCRATCH[_n] = ("psum", [128, 512], "float32")
 
-SEMAPHORES = (["qv", "qa", "qp", "qg", "sent", "stS", "stA"] + ["l%d" % _i for _i in range(28)]
+SEMAPHORES = (["qv", "qa", "qp", "qg", "sent", "stS", "stA"] + ["l%d" % _i for _i in range(12)]
               + [_x + "%d" % _t for _t in range(R) for _x in "abc"])
 
 
@@ -76,22 +74,33 @@ def bits(x):
     return bin(x).count("1")
 
 
+ORDER = [
+    0,1,2,3,4,5,6,7,8,9,11,12,10,67,15,22,23,70,16,13,17,18,68,29,21,71,238,27,19,74,69,82,20,77,72,85,26,81,28,83,87,24,84,75,86,80,101,37,73,88,130,62,
+    33,31,30,224,76,102,60,49,135,38,25,34,78,42,50,44,55,36,79,32,104,111,136,14,213,103,105,51,35,210,63,112,107,52,137,214,226,39,113,237,199,216,53,114,219,
+    43,138,106,40,225,220,139,140,132,142,54,145,236,134,41,133,89,159,235,64,65,215,45,108,190,146,115,193,56,192,46,109,162,66,189,116,57,217,211,58,110,227,
+    247,47,165,147,59,117,48,119,194,195,118,246,148,141,200,61,196,120,143,160,204,168,90,221,149,197,163,122,150,191,154,223,198,121,169,265,166,212,248,228,161,
+    158,229,266,123,124,250,155,153,252,218,205,164,151,156,157,95,91,97,167,171,170,93,239,259,125,144,230,92,126,127,222,183,152,231,232,240,267,172,96,128,268,
+    174,129,270,269,271,173,176,175,272,233,280,201,178,273,94,274,179,202,275,263,255,177,99,256,281,257,258,203,276,98,184,100,261,244,241,282,277,284,283,243,
+    285,278,185,234,286,182,279,287,180,181,296,294,299,298,297,242,301,300,295,245,288,302,289,249,206,308,251,253,290,303,186,324,291,254,187,207,188,292,307,208,
+    293,322,304,305,306,309,323,131,209,325,310,260,264,326,327,311,262,321,329,312,332,330,328,331,313,333,356,357,363,334,335,314,364,336,343,337,340,338,342,339,
+    344,341,351,315,367,347,354,355,368,350,358,359,374,361,365,362,373,402,346,360,349,366,400,348,375,316,377,345,379,369,435,381,317,376,403,378,320,380,382,404,
+    407,318,405,319,370,410,383,352,413,353,371,408,384,406,414,409,411,385,392,395,412,372,386,416,419,387,393,428,391,417,401,420,415,421,418,423,394,422,424,429,
+    425,525,426,526,430,449,427,388,389,390,436,396,397,450,437,431,451,441,438,439,440,452,453,432,442,455,454,443,456,444,457,445,433,434,458,446,459,447,460,448,
+    461,465,464,468,470,466,467,463,469,462,477,476,471,494,490,478,492,472,496,479,495,398,498,480,499,399,497,491,501,481,500,502,532,482,504,493,503,505,483,533,
+    509,507,506,511,510,508,512,484,485,520,534,592,473,474,535,513,524,536,514,537,523,515,517,516,475,486,487,527,519,528,488,538,529,530,543,518,544,545,521,539,
+    522,541,540,547,549,551,531,546,489,566,548,550,552,569,572,575,567,542,553,573,554,570,571,555,576,568,565,574,556,577,562,578,579,581,557,583,558,563,585,590,
+    561,580,582,584,586,587,589,564,606,588,591,559,560,593,607,594,608,597,596,595,598,610,611,599,609,612,600,613,601,614,602,615,603,616,604,617,605,618,623,622,
+    626,620,627,621,624,625,633,634,619,629,628,635,637,641,636,642,643,630,631,639,677,645,646,644,678,638,632,648,647,649,640,681,682,679,680,651,650,683,652,659,
+    684,653,656,654,658,657,660,655,685,667,664,661,666,662,686,663,670,671,672,687,688,673,674,675,697,690,689,691,665,698,693,694,676,668,695,699,669,700,705,706,
+    703,704,696,701,702,707,708,711,709,715,710,712,713,714,716,692,717]
+
+
 def arrange(ops):
-    hop = 0.15
-    for o in reversed(ops):
-        o["tail"] = o["lat"] + o["more"] + max([hop + x["tail"] for x in o["users"]] + [0.0])
-    busy = {}
-    for o in sorted(ops, key=lambda y: (-y["tail"], y["at"])):
-        t = max([x["start"] + (x["cost"] if x["q"] == o["q"] == "p" or x.get("remote") else x["lat"] + hop) for x in o["deps"]] + [0.0])
-        if o["q"] is not None:
-            line = busy.setdefault(o["q"], [])
-            k = 0
-            while k < len(line) and line[k][0] < t + o["cost"]:
-                t = max(t, line[k][1])
-                k += 1
-            line.insert(k, (t, t + o["cost"]))
-        o["start"] = t
-    return sorted(ops, key=lambda y: (y["start"], y["at"]))
+    if len(ORDER) != len(ops):
+        return list(ops)
+    place = {k: i for i, k in enumerate(ORDER)}
+    assert all(place[x["at"]] < place[o["at"]] for o in ops for x in o["deps"])
+    return [ops[i] for i in ORDER]
 
 
 def rank_program(g, core, T, topo):
@@ -124,9 +133,8 @@ def rank_program(g, core, T, topo):
             return True
         return bool(set(range(a[3], a[4], a[5])) & set(range(b[3], b[4], b[5])))
 
-    def add(q, fn, reads, writes, cost, lat=None, sem=None, count=16, after=()):
-        o = {"q": q, "fn": fn, "inc": False, "sem": sem, "count": count, "cost": cost, "lat": cost if lat is None else lat,
-             "at": len(ops), "users": [], "deps": list(after), "more": 0.0}
+    def add(q, fn, reads, writes, sem=None, count=16, after=()):
+        o = {"q": q, "fn": fn, "inc": False, "sem": sem, "count": count, "at": len(ops), "deps": list(after)}
         seen = {x["at"] for x in after}
         for v, wr in [(v, False) for v in reads] + [(v, True) for v in writes]:
             ps = SCRATCH[v[0]][0] == "psum"
@@ -134,8 +142,6 @@ def rank_program(g, core, T, topo):
                 if x["at"] not in seen and (wr or uw or ps) and meet(u, v) and not (q is None and x["q"] is None):
                     seen.add(x["at"])
                     o["deps"].append(x)
-        for x in o["deps"]:
-            x["users"].append(o)
         ops.append(o)
         for v in reads:
             touch.setdefault(v[0], []).append((v, False, o))
@@ -152,23 +158,19 @@ def rank_program(g, core, T, topo):
     def vs(*xs):
         return [x for x in xs if isinstance(x, tuple)]
 
-    def span(out, off=None, k=1):
-        n = wide(out)
-        return 0.06 + 0.0015 * n if off is not None else max(64, k * n) * 0.001
-
-    def ts(out, a, s1, op0, s2=None, op1=None, off=None):
+    def ts(out, a, s1, op0, s2=None, op1=None):
         if op1 is None:
-            add("v", lambda: g.vector.tensor_scalar(ap(out), src(a, off), sc(s1), None, op0), vs(a, s1, off), [out], span(out, off))
+            add("v", lambda: g.vector.tensor_scalar(ap(out), ap(a), sc(s1), None, op0), vs(a, s1), [out])
         else:
-            add("v", lambda: g.vector.tensor_scalar(ap(out), src(a, off), sc(s1), sc(s2), op0, op1), vs(a, s1, s2, off), [out], span(out, off))
+            add("v", lambda: g.vector.tensor_scalar(ap(out), ap(a), sc(s1), sc(s2), op0, op1), vs(a, s1, s2), [out])
 
     def tt(out, a, b, op, off=None):
-        add("v", lambda: g.vector.tensor_tensor(ap(out), src(a, off), ap(b), op), vs(a, b, off), [out], span(out, off, 2))
+        add("v", lambda: g.vector.tensor_tensor(ap(out), src(a, off), ap(b), op), vs(a, b, off), [out])
 
     def cp(out, a, off=None):
-        add("v", lambda: g.vector.tensor_copy(ap(out), src(a, off)), vs(a, off), [out], span(out, off))
+        add("v", lambda: g.vector.tensor_copy(ap(out), src(a, off)), vs(a, off), [out])
 
-    def act(out, a, func, scale=1.0, off=None, bias=None, acc=None):
+    def act(out, a, func, scale=1.0, off=None, bias=None, acc=None, behind=None):
         kw = {}
         if bias is not None:
             kw["bias"] = sc(bias)
@@ -176,46 +178,46 @@ def rank_program(g, core, T, topo):
             kw["scale"] = sc(scale)
         if acc is not None:
             kw["accum_out"] = ap(acc)
-        add("a", lambda: g.scalar.activation(ap(out), src(a, off), func, **kw), vs(a, off, bias, scale), vs(out, acc),
-            max(64, wide(a)) * 0.001 if off is None else 0.08 + 0.0015 * wide(out))
+        add("a", lambda: g.scalar.activation(ap(out), src(a, off), func, **kw), vs(a, off, bias, scale, behind), vs(out, acc))
+
+    def ca(out, a, off=None, behind=None):
+        act(out, a, ACT.Copy, off=off, behind=behind)
 
     def lin(out, a, scale, bias):
         act(out, a, ACT.Identity, scale, None, bias)
 
     def scan(out, d0, d1, init, op0, op1):
-        add("v", lambda: g.vector.tensor_tensor_scan(ap(out), ap(d0), ap(d1), sc(init), op0, op1), vs(d0, d1, init), [out], span(out))
+        add("v", lambda: g.vector.tensor_tensor_scan(ap(out), ap(d0), ap(d1), sc(init), op0, op1), vs(d0, d1, init), [out])
 
     def tr(out, a):
-        add("v", lambda: g.vector.transpose(ap(out), ap(a)), [a], [out], span(out))
+        add("v", lambda: g.vector.transpose(ap(out), ap(a)), [a], [out])
 
     def mset(out, x):
-        add("v", lambda: g.vector.memset(ap(out), x), [], [out], span(out, None, 0.5 if SCRATCH[out[0]][2] == "bfloat16" else 1))
+        add("v", lambda: g.vector.memset(ap(out), x), [], [out])
 
     def iota(out, pat, base=0, mult=0):
         if SCRATCH[out[0]][2] == "int32":
-            add("g", lambda: g.iota(ap(out), pat, base, mult), [], [out], 0.16 + 0.002 * wide(out))
+            add("g", lambda: g.iota(ap(out), pat, base, mult), [], [out])
         else:
-            add("g", lambda: g.iota(ap(out), pat, base, mult, allow_small_or_imprecise_dtypes=True), [], [out], 0.16 + 0.002 * wide(out))
+            add("g", lambda: g.iota(ap(out), pat, base, mult, allow_small_or_imprecise_dtypes=True), [], [out])
 
     def quant(name, c0, tile, n, e0=0):
         q, s, a = V(name + "q", c0, c0 + n), V(name + "s", c0, c0 + n), V(tile, e0, e0 + 4 * n)
-        add("v", lambda: g.vector.quantize_mx(ap(q), ap(s), ap(a)), [a], [q, s], 0.015 + 0.00106 * n)
+        add("v", lambda: g.vector.quantize_mx(ap(q), ap(s), ap(a)), [a], [q, s])
 
     def mm(bank, st, s0, mv, m0, n, start, stop):
         o = V(bank, 0, n)
         r = [V(st + "q", s0, s0 + 128), V(st + "s", s0, s0 + 128), V(mv + "q", m0, m0 + n), V(mv + "s", m0, m0 + n)]
-        add("p", lambda: g.tensor.matmul_mx(ap(o), ap(r[0]), ap(r[1]), ap(r[2]), ap(r[3]), start, stop), r, [o], 0.0006 * (n + 16),
-            0.0006 * (n + 16) + 0.06)
+        add("p", lambda: g.tensor.matmul_mx(ap(o), ap(r[0]), ap(r[1]), ap(r[2]), ap(r[3]), start, stop), r, [o])
 
     def pick(dst, d0, frm, n, off):
         oq, iq = V(dst + "q", d0, d0 + 16 * wide(off)), V(frm + "q", 0, n)
-        add("v", lambda: g.vector.tensor_copy(ap(oq).bitcast(dt.uint32), ap(iq).bitcast(dt.uint32).indirect(ap(off))), [iq, off], [oq],
-            span(oq, off))
+        add("v", lambda: g.vector.tensor_copy(ap(oq).bitcast(dt.uint32), ap(iq).bitcast(dt.uint32).indirect(ap(off))), [iq, off], [oq])
         o2, i2 = V(dst + "s", d0, d0 + 16 * wide(off)), V(frm + "s", 0, n)
-        add("a", lambda: g.scalar.activation(ap(o2), ap(i2).indirect(ap(off)), ACT.Copy), [i2, off], [o2], span(o2, off) + 0.02)
+        add("a", lambda: g.scalar.activation(ap(o2), ap(i2).indirect(ap(off)), ACT.Copy), [i2, off], [o2])
 
-    def dma(q, sem, fo, fi, reads, writes, lat=2.0, after=()):
-        return add(q, lambda: eng[q].dma_start(fo(), fi()), reads, writes, 0.06, lat, sem=sem, after=after)
+    def dma(q, sem, fo, fi, reads, writes, after=()):
+        return add(q, lambda: eng[q].dma_start(fo(), fi()), reads, writes, sem=sem, after=after)
 
     plans = {c: deal(c, cores, topo) for c in cores}
     sent, calls = [0], []
@@ -232,47 +234,51 @@ def rank_program(g, core, T, topo):
                     a, b = a.bitcast(dt.uint8), b.bitcast(dt.uint8)
                 trs.append(RemoteDMATransfer(dst_ids=[DstId(rid=rid, pnc=pid)], dma_engine_mask=tab[d], remote_sem=T.sem[sem], src=a, dst=b))
             return g.remote_dma_fused(trs, local_sem=T.sem["sent"])
-        o = add("g", fn, [u for d, u, v in items], [], (0.25 + 0.03 * len(items)) if calls else 3.3, sem="sent", after=calls[-1:])
+        o = add("g", fn, [u for d, u, v in items], [], sem="sent", after=calls[-1:])
         o["remote"] = True
         calls.append(o)
         sent[0] += sum(bits(x) for x in tab.values())
 
-    def arrive(sem, which, writes, lat):
+    def arrive(sem, which, writes):
         n = sum(bits(plans[c][w].get(core, 0)) for c in cores if c != core for w in which)
-        return add(None, None, [], writes, lat, sem=sem, count=n, after=calls[-1:])
+        return add(None, None, [], writes, sem=sem, count=n, after=calls[-1:])
 
     a1, a2, b1, b2 = plans[core]
 
+    al, be, ga = (4, 1, (0, 2)) if m == 4 else (1, 2, (1, 5)) if m == 0 else (m, 2 * m, (2 * m, 6 * m) if m % 2 else (4, 1))
+    path = [(al * (k % 2) + be * (k // 2 % 2) + ga[k // 4]) % NR for k in range(NR)]
+
     loads = []
 
-    def load(q, dst, fi, lat=2.0, after=()):
-        loads.append(dma(q, "l%d" % len(loads), lambda: ap(dst), fi, [], [dst], lat, after))
-    load("s", V("pt", 0, 192), lambda: T.pr[:])
-    load("a", V("pt", 192, 384), lambda: T.pd[:])
-    load("s", V("vt", 96, 112), lambda: T.v[:, 0:16])
-    load("a", V("pt", 388, 580), lambda: T.pd[:])
-    load("s", V("vt", 128, 144), lambda: T.v[:, 0:16])
-    load("a", V("pt", 580, 768), lambda: T.pd[:, 0:188])
-    load("s", V("vt", 48, 64), lambda: T.v[:, 0:16])
-    load("a", V("pt", 384, 388), lambda: T.pd[:, 188:192])
-    load("s", V("vt", 256, 272), lambda: T.u[:, 0:16], 2.2)
-    load("s", V("xt", 0, 1536), lambda: T.x[:], 3.3)
-    loads.append(dma("s", "l10", lambda: T["wtq"][:].bitcast(dt.uint8), lambda: T.wc[:], [], [V("wtq", 0, 512)], 3.8))
-    load("s", V("wts", 0, 512), lambda: T.ws[:], 3.8)
-    ZT, ZC = 272, 128
-    for c0, c1 in ((0, 48), (64, 96), (112, 128), (144, 256), (ZT, 784)):
-        mset(V("vt", c0, c1), 0.0)
-    mset(V("pt", 768, 896), 0.0)
-    mset(V("nt", 256, 512), 0.0)
+    def load(q, dst, fi, after=()):
+        loads.append(dma(q, "l%d" % len(loads), lambda: ap(dst), fi, [], [dst], after))
+    PT, UT, XT = 384, 240, 768
+    load("s", V("sv", 0, 16), lambda: T.v[:, 0:16])
+    load("a", V("bt", PT + 192, PT + 384), lambda: T.pd[:])
+    load("s", V("bt", PT, PT + 192), lambda: T.pr[:])
+    load("a", V("bt", UT, UT + 16), lambda: T.u[:, 0:16])
+    load("s", V("bt", XT, XT + 1536), lambda: T.x[:])
+    load("s", V("wts", 0, 512), lambda: T.ws[:])
+    for b in range(4):
+        w = V("wtq", 128 * b, 128 * b + 128)
+        loads.append(dma("s", "l%d" % len(loads), lambda w=w: ap(w).bitcast(dt.uint8), lambda b=b: T.wc[:, 512 * b:512 * b + 512], [], [w]))
+    mset(V("bt", PT - 4 * PR, PT), 0.0)
+    mset(V("vz", 0, 528), 0.0)
 
     def cf(k, p0=0, p1=128):
         return V("cf", k, k + 1, 1, p0, p1)
+
+    def cf2(k):
+        return V("cf", k, k + 2)
 
     def ib(c0, c1):
         return V("ib", c0, c1)
 
     def tm(c0, c1, st=1):
         return V("tm", c0, c1, st)
+
+    def gl(c0, c1, st=1):
+        return V("gl", c0, c1, st)
 
     def fl(k, n):
         return V("fl", k, k + n)
@@ -282,45 +288,116 @@ def rank_program(g, core, T, topo):
 
     def kf(k, n, st=1, p0=0, p1=128):
         return V("kf", k, k + n, st, p0, p1)
-    PP, F2, F3, F4, F5, Q4, HI, LO, I16, E, G3, I8, K1, R8, K8 = range(15)
-    SG, W8, C48, AK, SH, VA, BF, BP, BN, NAT, FX, PL, X1, X2, X3 = range(15, 30)
-    O_CM, O_MA, O_AO, O_BO, O_CO, O_WL = 0, 24, 26, 28, 30, 32
-    O_AT, O_BT, O_CT, O_SG, O_MK, O_UP, O_CH, O_NAT, O_GL = 34, 36, 38, 40, 44, 46, 52, 56, 76
-    NI, TG, SP, K4, WS, C1, C3, RS, DEF, TK, NEG, KM = 0, 128, 224, 512, 608, 664, 728, 920, 1240, 1272, 1416, 1464
-    SN = 416
+    PP, F2, F3, F4, F5, Q4, HI, G3, K1, I8, O16, O32, K8, R8, I16, E, LO = range(17)
+    SG, W8, AK, SH, VA, BF, BP, BN, FX, PL = range(18, 28)
+    X1, X2, X3, X4, X5, X6, X8, X9, X10, X11, X12, KA, KI, Y1, Y2, Y3, Y4 = range(28, 45)
+    O_TA, O_UR, O_MA, O_AO, O_BO, O_CO, O_VR, O_M0 = 0, 8, 18, 20, 24, 28, 32, 82
+    O_AT, O_BT, O_CT, O_MK, O_CH, O_NAT, O_GL = 34, 36, 38, 44, 52, 56, 76
+    NI, SN, K4, WS, C1, C3, RS, DEF, TK, NEG, KM = 0, 416, 512, 608, 664, 728, 920, 1240, 1272, 1416, 1464
 
     def fill(out, x):
         lin(out, kf(NI, wide(out), 1, out[1], out[2]), 0.0, float(x))
     iota(V("ci", 0, 1), [[0, 1]], 0, 1)
-    iota(kf(NI, 128), [[1, 128]])
+    iota(kf(NI, 32), [[1, 32]])
+    iota(kf(NI + 32, 96), [[1, 96]], 32)
     for k, sh in ((F2, 2), (F3, 3), (F4, 4), (F5, 5)):
         ts(V("ci", k, k + 1), V("ci", 0, 1), sh, ALU.arith_shift_right)
-    cp(V("cf", 0, 5), V("ci", 0, 5))
-    for k, hi, sz, lo in ((HI, F4, 4, F2), (I16, F4, 16, PP), (Q4, F2, 4, PP), (E, F5, 32, PP), (R8, F5, 8, F2), (G3, F5, 4, F3),
-                          (K1, F3, 2, F2), (K8, F3, 8, PP), (I8, F4, 2, F3)):
-        lin(cf(k), cf(hi), -float(sz), cf(lo))
-    ts(cf(LO), cf(PP), float(S), ALU.is_lt)
-    iota(tm(0, 6), [[m, 3], [4, 2]], 16 - 2 * m)
+    for k, c0, n, an in ((Q4, 0, 3, 3), (K1, 1, 4, 1), (K8, 0, 2, 7), (I16, 0, 1, 15), (E, 0, 1, 31)):
+        ts(V("ci", k, k + n), V("ci", c0, c0 + n), an, ALU.bitwise_and)
+    cp(V("cf", 0, 16), V("ci", 0, 16))
+    ts(cf2(LO), V("cf", PP, PP + 2), float(S), ALU.is_lt)
+    iota(tm(0, 4), [[m, 2], [4, 2]], 8 - m)
     iota(tm(6, 8), [[-4, 2]], 8)
-    lin(tm(8, 14), tm(0, 6), 1.0, cf(HI))
+    iota(tm(128, 136), [[m, 2], [ga[1] - ga[0], 2], [0, 2]], ga[0] - 2 * m + 16)
+    iota(tm(136, 140), [[ga[1] - ga[0], 2], [be, 2]], ga[0])
+    lin(tm(144, 148), tm(0, 4), 1.0, cf(HI))
     lin(cf(X1), cf(HI), -1.0, 0.0)
-    lin(tm(14, 16), tm(6, 8), 1.0, cf(X1))
-    lin(tm(16, 17), cf(LO), m + 1.0, cf(I16))
-    lin(tm(17, 18), cf(LO), 7.0, cf(I16))
-    cp(ib(0, 10), tm(8, 18))
-    ts(ib(0, 10), ib(0, 10), 7, ALU.bitwise_and)
-    cp(tm(20, 30), ib(0, 10))
-    n0, n1, n2, n6 = tm(20, 22), tm(22, 24), tm(24, 26), tm(26, 28)
-    iota(tm(32, 56), [[1, 8], [128, 3]])
+    lin(tm(148, 150), tm(6, 8), 1.0, cf(X1))
+    lin(cf(X2), cf(K1), float(al), float(ga[0]))
+    lin(cf(SG), cf(I8), float(be), cf(X2))
+    ts(tm(150, 158), tm(128, 136), cf(SG), ALU.add, -float(ga[0]), ALU.add)
+    lin(tm(158, 159), cf(O32), float(ga[1] - ga[0]), cf(SG))
+    lin(cf(Y1), cf(O16), float(al), 0.0)
+    lin(tm(159, 163), tm(136, 140), 1.0, cf(Y1))
+    cp(ib(0, 19), tm(144, 163))
+    ts(ib(0, 19), ib(0, 19), 7, ALU.bitwise_and)
+    cp(tm(8, 27), ib(0, 19))
+    n1, n2 = tm(8, 10), tm(10, 12)
+    keep, turn, by = (6, 1, 1) if m == 4 else (0, 7, 0) if m == 0 else (0, 7, 1) if m % 2 else (4, 3, 1)
+    ts(ib(20, 21), cf(K8), float(by), ALU.add)
+    ts(ib(21, 22), ib(20, 21), turn, ALU.bitwise_and)
+    ts(ib(22, 23), V("ci", K8, K8 + 1), keep, ALU.bitwise_and)
+    cp(tm(28, 30), ib(21, 23))
+    lin(tm(30, 31), tm(28, 29), 1.0, tm(29, 30))
+    lin(tm(31, 32), cf(K8), -1.0, tm(30, 31))
+    lin(fl(O_MA, 1), tm(31, 32), cf(LO), cf(K8))
+    lin(cf(X10), cf(F5), 2.0, 0.0)
+    lin(tm(32, 34), kf(NI, 2), 1.0, cf(X10))
+    ts(tm(34, 36), tm(32, 34), 3.0, ALU.is_ge, -3.0, ALU.mult)
+    ts(tm(36, 38), tm(32, 34), 6.0, ALU.is_ge, -3.0, ALU.mult)
+    tt(tm(38, 40), tm(34, 36), tm(36, 38), ALU.add)
+    tt(tm(40, 42), tm(38, 40), tm(32, 34), ALU.add)
     lin(cf(W8), cf(I16), 8.0, 0.0)
-    ts(co(O_CM, 24), tm(32, 56), cf(W8), ALU.add)
-    lin(fl(O_MA, 1), tm(28, 29), 1.0, 0.0)
-    lin(fl(O_MA + 1, 1), tm(28, 29), 1.0, 0.0)
-    lin(fl(O_AO, 2), n2, 1.0, 0.0)
-    lin(fl(O_BO, 2), n1, 2.0, float(LB))
-    lin(fl(O_CO, 2), n0, 2.0, LB + 1.0)
-    lin(fl(O_WL, 2), kf(NI, 2), 0.0, cf(E))
-    cp(co(O_MA, 10), fl(O_MA, 10))
+    lin(tm(42, 44), tm(40, 42), 128.0, cf(W8))
+    for e in range(2):
+        lin(V("fl", O_TA + e, O_TA + 8, 2), tm(23, 27), 1.0, tm(42 + e, 43 + e))
+    cp(co(O_TA, 8), fl(O_TA, 8))
+    ts(co(O_UR, 8), kf(NI, 8), 0.0, ALU.mult, cf(Q4), ALU.add)
+    cp(co(O_MA, 1), fl(O_MA, 1))
+    iota(tm(164, 168), [[4, 2], [0, 2]])
+    lin(fl(O_AO, 4), tm(164, 168), 1.0, cf(HI))
+    lin(fl(O_BO, 4), tm(18, 22), 2.0, float(LB))
+    lin(fl(O_CO, 4), tm(14, 18), 2.0, LB + 1.0)
+    cp(co(O_AO, 12), fl(O_AO, 12))
+    iota(tm(102, 104), [[16, 2]], 0, 1)
+    iota(V("ag", 0, 32), [[1, 2], [0, 16]])
+    tr(V("ag", 32, 64), V("ag", 0, 32))
+    odd = V("ag", 32, 33)
+    ts(tm(104, 106), tm(102, 104), 65.0, ALU.is_ge, -float(S), ALU.mult)
+    ts(tm(106, 108), tm(102, 104), 17.0, ALU.is_lt, float(S), ALU.mult)
+    tt(tm(110, 112), tm(104, 106), tm(106, 108), ALU.add)
+    ts(tm(114, 116), tm(110, 112), 31.0, ALU.add, odd, ALU.mult)
+    ts(tm(108, 110), tm(102, 104), 64.0, ALU.is_lt, 31.0, ALU.add)
+    tt(tm(124, 126), tm(104, 106), tm(108, 110), ALU.add)
+    ts(tm(112, 114), tm(124, 126), odd, ALU.mult)
+    iota(tm(116, 120), [[0, 2], [16, 2]], PR, 1)
+    tt(tm(120, 124), tm(112, 116), tm(116, 120), ALU.add)
+    ts(co(O_M0, 4), tm(120, 124), 127.0, ALU.min)
+    for a in range(8):
+        (cp if a % 2 else ca)(V("vz", 128 * (a // 2) + 60 + 4 * (a % 2), 128 * (a // 2) + 64 + 4 * (a % 2)), V("sv", 0, 4))
+    quant("v0", 0, "vz", 128)
+    lin(cf(X9), cf(I8), 4.0, cf(Q4))
+    ts(co(O_VR, 2), kf(NI, 2), 8.0, ALU.mult, cf(X9), ALU.add)
+    for a in range(4):
+        out = V("vz", 128 * a + 60, 128 * a + 92)
+        if a % 2:
+            cp(out, V("sv", 0, 16), co(O_VR, 2))
+        else:
+            ca(out, V("sv", 0, 16), co(O_VR, 2))
+    iota(gl(0, 8), [[2, 2], [4, 2], [1, 2]])
+    iota(gl(128, 136), [[2, 2], [-4, 2], [1, 2]], 4)
+    iota(gl(8, 16), [[0, 8]], 8)
+    for a in (1, 3):
+        lin(V("gl", 0, 8, 1, 32 * a, 32 * a + 32), V("gl", 128, 136, 1, 32 * a, 32 * a + 32), 1.0, 0.0)
+    lin(gl(16, 32), gl(0, 16), 1.0, 0.0)
+    iota(gl(136, 168), [[0, 2], [1, 16]])
+    iota(gl(142, 146), [[0, 2], [1, 2]])
+    iota(gl(158, 162), [[3, 2], [1, 2]], 3)
+    for c0 in (146, 162):
+        lin(gl(c0, c0 + 2), kf(NI, 2), 1.0, -3.0)
+    for c0 in (6, 22):
+        lin(gl(136 + c0, 142 + c0), gl(136 + c0, 142 + c0), 1.0, cf(X10))
+    ts(gl(32, 64), gl(136, 168), 0.0, ALU.max, 11.0, ALU.min)
+    tr(gl(96, 128), gl(32, 64))
+    cp(co(O_GL + 4, 1), gl(96, 97))
+    lin(cf(X3), cf(I16), 1.0, float(PR))
+    lin(gl(168, 180), kf(NI, 12), 16.0, cf(X3))
+    lin(gl(174, 177), gl(174, 177), 1.0, -S - 1.0)
+    lin(gl(177, 180), gl(177, 180), 1.0, -2 * S - 1.0)
+    ts(cf(X11), cf(I16), 0.0, ALU.is_equal, float(S), ALU.mult)
+    lin(gl(174, 178, 3), gl(174, 178, 3), 1.0, cf(X11))
+    cp(kf(DEF, 16), gl(168, 180), co(O_GL + 4, 1))
+    cp(co(O_M0 + 4, 2), kf(DEF + 10, 2))
 
     mset(V("et", 0, 516), 0.0)
     for name, sign in (("em", -1.0), ("ep", 1.0)):
@@ -328,126 +405,124 @@ def rank_program(g, core, T, topo):
         for b in range(4):
             quant(name, 128 * b, "et", 128, 3 - b)
 
-    def dist(d):
-        return (d - m) % NR
+    def first(d):
+        return 4 * (path.index(d) & 6 if m == 4 else path.index(d))
 
-    def scores(t):
-        la, P = "la%d" % t, "P%d" % t
-        for j, v0 in enumerate((24, 8, 0)):
-            mm("pm", P, PR + S * j, "v3", v0, 128, j == 0, j == 2)
-        cp(V(la, 0, 4), V("pm", t, 16, 4))
+    def scores(t, n, off):
+        la = "la%d" % t
+        cp(V("mg", 0, 64), V("sr", 0, n), off(0, 4))
+        tr(V(la, 0, 64), V("mg", 0, 64))
 
-        def pair(d):
-            c0 = 2 if m + d >= NR else 0
-            return V(la, c0, c0 + 2)
+        def pair(d, more=0):
+            c0 = 47 if m + d >= NR else 15
+            return V(la, c0 - more, c0 + 2)
         for tab in (a1, a2):
             push(tab, "a%d" % t, pair, lambda d: V(la, LB + 2 * ((m - d) % NR), LB + 2 * ((m - d) % NR) + 2))
-        arrive("a%d" % t, (0, 1), [V(la, LB + 2, LB + 16)], 2.0)
-        act(V(la, LB, LB + 2), pair(m), ACT.Copy)
-        mm("pz", P, 0, "v3", 24, 128, True, True)
-        act(V(la, 4, 6), V("pz", t, t + 2), ACT.Copy)
+        came = arrive("a%d" % t, (0, 1), [V(la, LB + 2, LB + 16)])
+        ca(V(la, LB - 2, LB + 2), pair(m, 2))
+        ca(V("mg", 64, 96), V("sr", 0, n), off(4, 2))
+        tr(V(la, 64, 96), V("mg", 64, 96))
+        return came
 
     def table(frm):
-        for k in range(NR + 1):
-            mm("pa", frm, (DO + S * k) % (DO + C), "v3", 64 - 4 * min(k, NR - 1), 128, k == 0, k == NR)
+        mm("pa", "ur", 0, frm, 0, C, True, True)
+        ca(V("ar", 0, C), V("pa", 0, C))
+        ca(V("ag", 0, 128), V("ar", 0, C), co(O_TA, 8))
+        tr(V("ta", 0, 128), V("ag", 0, 128))
 
     def tell(t, own):
         la, ms = "la%d" % t, "ms%d" % t
-        cp(V(ms, 0, 16), own, co(O_MA, 1))
+        ca(V(ms, 0, 16), own, co(O_MA, 1))
         for tab in (a1, a2):
-            push(tab, "c%d" % t, lambda d: V(ms, (d + 7) % NR, (d + 7) % NR + 1), lambda d: V(la, LA + (m - d) % NR, LA + (m - d) % NR + 1))
-        came = arrive("c%d" % t, (0, 1), [V(la, LA + 1, LA + 8)], 2.6)
-        act(V(la, LA - 3, LA + 1), V(ms, (m + 7) % NR + 5, (m + 7) % NR + 9), ACT.Copy)
-        return came
+            push(tab, "c%d" % t, lambda d: V(ms, path.index(d), path.index(d) + 1), lambda d: V(la, LA + (m - d) % NR, LA + (m - d) % NR + 1))
+        arrive("c%d" % t, (0, 1), [V(la, LA + 1, LA + 8)])
+        ca(V(la, LA - 3, LA + 1), V(ms, path.index(m) + 5, path.index(m) + 9))
 
-    for name, c0 in (("v3", ZC), ("P0", 0), ("Dc", 0), ("Dc", YO - 128), ("N0", 0), ("N0", YO - 128)):
-        quant(name, c0, "vt", 128, ZT)
-    quant("P0", PR, "pt", PN - PR)
-    quant("v3", 0, "vt", 128)
-    scores(0)
+    quant("P0", 0, "bt", 128, PT - 4 * PR)
+    quant("vr", 0, "vz", 132)
+    quant("u1", 0, "bt", 128, UT)
+    pick("ur", 0, "u1", 128, co(O_UR, 8))
+    mm("pm", "v0", 0, "P0", 0, 128, True, True)
+    cp(V("sr", 0, 128), V("pm", 0, 128))
+    scores(0, 128, lambda c, n: co(O_M0 + c, n))
 
     H = ["h0", "h1", "h2", "h3"]
 
     def rewrite(t, c0, n):
         N_, L = "N%d" % t, "L%d" % t
         for b in range(4):
-            mm(H[b], "wt", 128 * b, "Dc", c0, n, True, True)
+            bank = ("py", "pm", "pz", "h3")[b] if c0 == 0 else H[b]
+            mm(bank, "wt", 128 * b, "Dc", c0, n, True, True)
             if n > 128 and b % 2:
-                ts(V("ht", b, 4 * n, 4), V(H[b], 0, n), 0.0, ALU.max, 0.0625, ALU.mult)
+                ts(V("ht", b, 4 * n, 4), V(bank, 0, n), 0.0, ALU.max, 0.0625, ALU.mult)
             else:
-                act(V("ht", b, 4 * n, 4), V(H[b], 0, n), ACT.Relu, 0.0625)
+                act(V("ht", b, 4 * n, 4), V(bank, 0, n), ACT.Relu, 0.0625)
             mm(H[b], "em", 128 * b, "Dc", c0, n, True, False)
         quant(N_, c0, "ht", n)
         for b in range(4):
             mm(H[b], "ep", 128 * b, N_, c0, n, False, True)
-            act(V("hu", b, 4 * n, 4), V(H[b], 0, n), ACT.Copy)
+            ca(V("hu", b, 4 * n, 4), V(H[b], 0, n))
         for c in range(0, n, 128):
             quant(L, c0 + c, "hu", 128, 4 * c)
 
-    quant("D0", 0, "xt", C)
-    pick("Dc", DO, "D0", C, co(O_CM, 24))
+    quant("Dc", 0, "bt", C, XT)
     table("Dc")
-    act(V("a0", 0, 8), V("pa", 0, 32, 4), ACT.Copy)
-    act(V("aa0", 16, 24), V("pa", 2, 32, 4), ACT.Copy)
-    act(V("aa0", 24, 32), V("pa", 1, 32, 4), ACT.Copy)
+    ca(V("a0", 0, 8), V("ta", 0, 128, 16))
+    ca(V("aa0", 16, 24), V("ta", 2, 128, 16))
+    ca(V("aa0", 24, 32), V("ta", 1, 128, 16))
+    ca(V("aa1", 8, 16), V("a0", 0, 8))
     mine = [V("a0", 0, 8), V("aa1", 24, 32), V("aa2", 16, 24)]
-    told = tell(0, mine[0])
-    rewrite(0, DO, C)
+    tell(0, mine[0])
+    rewrite(0, 0, C)
     table("N0")
-    act(V("aa0", 0, 8), V("pa", 2, 32, 4), ACT.Copy)
-    act(V("aa0", 8, 16), V("pa", 1, 32, 4), ACT.Copy)
-    for dst, d0, n in (("P1", 0, PR), ("P1", PN - 32, 32), ("P2", 0, PR), ("P2", PN - 32, 32), ("P3", 2 * S, 32), ("N1", 0, DO), ("N1", DE, YO - DE)):
-        u, v = V(dst + "q", d0, d0 + n), V("v3q", ZC, ZC + n)
-        loads.append(dma("s", "l%d" % len(loads), lambda u=u: ap(u).bitcast(dt.uint8), lambda v=v: ap(v).bitcast(dt.uint8), [v], [u], 2.0, [told]))
-        u, v = V(dst + "s", d0, d0 + n), V("v3s", ZC, ZC + n)
-        loads.append(dma("s", "l%d" % len(loads), lambda u=u: ap(u), lambda v=v: ap(v), [v], [u], 2.0, [told]))
+    ca(V("aa0", 0, 8), V("ta", 2, 128, 16))
+    ca(V("aa0", 8, 16), V("ta", 1, 128, 16))
 
     lin(fl(O_AT, 2), n1, 1.0, 3.0)
-    lin(tm(56, 58), n2, 2.0, LB - 4.0)
-    lin(fl(O_BT, 2), tm(56, 58), cf(LO), 4.0)
-    ts(tm(58, 60), n2, float(8 - m), ALU.is_ge, 2.0, ALU.mult)
-    ts(tm(60, 62), n2, float(m), ALU.is_gt, LB - 1.0, ALU.add)
+    lin(tm(56, 58), n2, 2.0, LB - 79.0)
+    lin(fl(O_BT, 2), tm(56, 58), cf(LO), 79.0)
+    ts(tm(58, 60), n2, float(8 - m), ALU.is_ge, 32.0, ALU.mult)
+    ts(tm(60, 62), n2, float(m), ALU.is_gt, LB - 16.0, ALU.add)
     for c in range(2):
-        lin(tm(62 + c, 63 + c), tm(26 + c, 27 + c), 2.0, tm(60 + c, 61 + c))
-        lin(tm(64 + c, 65 + c), tm(62 + c, 63 + c), -1.0, tm(58 + c, 59 + c))
-        lin(tm(66 + c, 67 + c), tm(62 + c, 63 + c), 1.0, 1.0)
-        lin(fl(O_CT + c, 1), tm(64 + c, 65 + c), cf(LO), tm(66 + c, 67 + c))
-    iota(tm(68, 72), [[16, 2], [0, 2]], 4 * m)
-    lin(cf(X2), cf(K1), float(4 * m), cf(Q4))
-    lin(cf(SG), cf(G3), 4.0, cf(X2))
-    ts(ib(10, 14), tm(68, 72), cf(SG), ALU.add)
-    ts(ib(10, 14), ib(10, 14), 31, ALU.bitwise_and)
-    cp(fl(O_SG, 4), ib(10, 14))
-    lin(tm(72, 73), tm(29, 30), 1.0, 1.0)
-    ts(tm(73, 74), tm(72, 73), 8.0, ALU.is_lt, tm(72, 73), ALU.mult)
-    lin(tm(74, 75), tm(73, 74), 4.0, 3.0)
-    lin(fl(O_MK, 2), kf(NI, 2), 0.0, tm(74, 75))
-    iota(kf(KM, 32), [[S, 8], [0, 4]])
-    lin(cf(PL), cf(LO), float(S), cf(PP))
-    lin(kf(KM, 32), kf(KM, 32), 1.0, cf(PL))
+        lin(tm(62 + c, 63 + c), tm(12 + c, 13 + c), 2.0, tm(60 + c, 61 + c))
+    tt(tm(64, 66), tm(58, 60), tm(62, 64), ALU.subtract)
+    ts(tm(66, 68), tm(64, 66), cf(LO), ALU.mult, 16.0, ALU.add)
+    tt(fl(O_CT, 2), tm(66, 68), tm(62, 64), ALU.add)
+    lin(tm(74, 75), cf(K8), 4.0, 3.0)
+    ts(co(O_MK, 2), kf(NI, 2), 0.0, ALU.mult, tm(74, 75), ALU.add)
+    for c in range(2):
+        iota(ib(32 + 16 * c, 48 + 16 * c), [[be, 2], [al, 2], [0, 4]], ga[c])
+    ts(ib(32, 64), ib(32, 64), 7, ALU.bitwise_and)
+    lin(cf(X12), cf(LO), float(S), cf(PP))
+    lin(cf(PL), cf(X12), 8.0, -8.0 * S)
+    ts(kf(KM, 32), ib(32, 64), cf(PL), ALU.add)
+    ts(tm(168, 176), V("ib", 32, 64, 4), cf(K8), ALU.is_equal)
+    tt(tm(176, 184), tm(168, 176), kf(NI, 8), ALU.mult)
+    act(tm(184, 192), tm(176, 184), ACT.Identity, 4.0, acc=cf(KI))
     iota(tm(76, 79), [[-1, 3]], 3)
     ts(tm(80, 83), tm(76, 79), cf(Q4), ALU.is_le, -0.5, ALU.add)
     lin(V("zz", 13, 16), tm(80, 83), 2.0 * BIG, 0.0)
     fill(kf(NEG, 48), -BIG)
-    fill(kf(WS, 52), 1)
-    fill(kf(WS + 3, 1), -1)
-    fill(V("ww", 155, 192), -US / 2)
-    lin(cf(C48), cf(R8), float(S), float(DO))
-    ts(cf(SH, 96), cf(R8, 96), float(8 - m), ALU.is_ge)
-    lin(cf(32, 64), cf(E, 64), 1.0, 32.0)
-    lin(cf(AK, 64, 96), cf(E, 64, 96), 1.0, 32.0)
-    lin(cf(FX, 96), cf(E, 96), -2.0, -32.0 * S)
-    lin(cf(AK, 96), cf(SH, 96), -32.0, cf(32, 96))
-    lin(V("tt", 0, 84, 1, 0, 32), kf(NI, 84, 1, 0, 32), 1.0, cf(C48, 0, 32))
-    lin(V("tt", 0, 84, 1, 64), kf(NI, 84, 1, 64), 32.0, cf(AK, 64))
-    lin(V("tt", 0, 1, 1, 96), cf(FX, 96), cf(SH, 96), cf(AK, 96))
-    lin(cf(VA, 64), cf(R8, 64), 16.0, cf(Q4, 64))
-    lin(cf(VA, 96), cf(VA, 96), 1.0, 4.0)
+    iota(kf(WS, 52), [[0, 52]], 1)
+    iota(kf(WS + 3, 1), [[0, 1]], -1)
+    iota(V("ww", 155, 192), [[0, 37]], int(-US / 2))
+    ts(cf(SH, 64), cf(R8, 64), float(8 - m), ALU.is_ge, cf(O32, 64), ALU.mult)
+    lin(cf(AK, 64), cf(SH, 64), -32.0, cf(E, 64))
+    lin(cf(FX, 64), cf(E, 64), -2.0, -32.0 * S - 32.0)
+    lin(cf(X6, 64), cf(E, 64), 1.0, 32.0)
+    lin(V("tt", 0, 84, 1, 0, 64), kf(NI, 84, 1, 0, 64), 8.0, V("tm", 22, 23, 1, 0, 64))
+    lin(V("tt", 1, 84, 1, 64), kf(NI + 2, 83, 1, 64), 32.0, cf(AK, 64))
+    lin(V("tt", 0, 1, 1, 64), cf(FX, 64), cf(SH, 64), cf(X6, 64))
+    lin(cf(Y2, 64), cf(O32, 64), 4.0, cf(Q4, 64))
+    lin(cf(VA, 64), cf(R8, 64), 16.0, cf(Y2, 64))
+    mine_row, mine_diag = 128 + 4 * path.index(m) - 16 * m, 128 + 4 * path.index(2 * m % NR) - 16 * m - 4
+    for r, row, diag in ((0, 0, -4 if m else 0), (4, 4 if m > 4 else 0, -4 if m > 4 else 0), (m, mine_row, mine_diag)):
+        lin(cf(Y3, 64), cf(O32, 64), float(diag - row), float(row))
+        ts(cf(Y4, 64), cf(R8, 64), float(r), ALU.is_equal, cf(Y3, 64), ALU.mult)
+        lin(cf(VA, 64), cf(VA, 64), 1.0, cf(Y4, 64))
     lin(cf(BF, 64), cf(E, 64), -1.0, -0.5)
-    lin(cf(BP, 64, 96), cf(E, 64, 96), -1.0 / 32, PR - 1.0)
-    lin(cf(BP, 96), cf(E, 96), -1.0 / 32, PR - 1.0 + S)
-    fill(cf(BN, 64, 96), PN + 15.5)
-    fill(cf(BN, 96), PN + 47.5)
+    lin(cf(BP, 64), cf(O32, 64), float(S), PR - 1.0 + 1.0 / 64)
+    lin(cf(BN, 64), cf(O32, 64), 32.0, PN + 15.5)
     fill(V("sa", 64, 65), -BIG)
     iota(kf(C1, 64), [[32, 2], [0, 2], [2, 16]], -31)
     iota(kf(C3, 96), [[16, 3], [0, 2], [1, 16]], PR)
@@ -455,53 +530,27 @@ def rank_program(g, core, T, topo):
     lin(kf(C3, 96, 1, 96), kf(C3, 96, 1, 96), 1.0, float(S))
     fill(kf(C3 + 96, 17, 16), PR + 2 * S - 1)
     iota(kf(RS, 192), [[0, 6], [1000, 32]])
-    iota(tm(96, 104), [[2, 2], [4, 2], [1, 2]])
-    iota(fl(80, 8), [[2, 2], [-4, 2], [1, 2]], 4)
-    fill(tm(104, 128), 8)
-    lin(tm(112, 115), kf(NI, 3), 1.0, 0.0)
-    lin(tm(115, 121), kf(NI, 6), 1.0, 6.0)
-    lin(tm(121, 124), kf(NI, 3), 1.0, 9.0)
+    tr(V("ff", 0, 32), gl(0, 32))
+    ts(tm(96, 97), gl(96, 97), 3.0, ALU.is_ge, 3.0, ALU.mult)
+    ts(tm(97, 98), gl(96, 97), 9.0, ALU.is_ge, -3.0, ALU.mult)
+    lin(tm(98, 99), gl(96, 97), 1.0, tm(97, 98))
+    lin(V("ff", 2, 3), tm(96, 97), 1.0, tm(98, 99))
     for a in (1, 3):
         p0, p1 = 32 * a, 32 * a + 32
-        lin(V("tm", 96, 104, 1, p0, p1), V("fl", 80, 88, 1, p0, p1), 1.0, 0.0)
-        lin(V("tm", 112, 115, 1, p0, p1), V("tm", 112, 115, 1, p0, p1), 1.0, 6.0)
-        lin(V("tm", 115, 124, 1, p0, p1), V("tm", 115, 124, 1, p0, p1), 1.0, -6.0)
-    cp(V("wf", 0, 32), tm(96, 128), co(O_WL, 2))
-    tr(V("ff", 0, 32), V("wf", 0, 32))
-    cp(co(O_GL, 4), V("ff", 0, 32, 8))
-    fill(V("wb", 8, 9), 0)
-    lin(cf(X3), cf(I16), 1.0, float(PR))
-    lin(kf(DEF, 16), kf(NI, 16), 16.0, cf(X3))
-    fill(kf(TK, 72), 0)
-    fill(kf(TK + 72, 72), 0)
-    fill(kf(TK, 1), 1)
-    iota(kf(TG, 96), [[16, 24], [0, 4]], DO)
-    lin(kf(TG, 96), kf(TG, 96), 1.0, cf(I16))
-    k = 0
-    while k < NR:
-        dl = (k - m) % NR
-        n = min(NR - dl, NR - k)
-        iota(kf(SP + 12 * k, 12 * n), [[8, n], [0, 3], [1, 4]], YO + 8 * dl)
-        k += n
-    lin(kf(SP + 96, 96), kf(SP, 96), 1.0, 64.0)
-    iota(kf(K4, 96), [[0, 24], [1000, 4]])
-    lin(cf(X1), cf(HI), 1.0 / 3.0, -1.0 / 3.0)
-    lin(tm(84, 90), kf(NI, 6), 4.0 / 3.0, cf(X1))
-    cp(ib(16, 22), tm(84, 90))
-    ts(fl(O_UP, 6), ib(16, 22), 4.0, ALU.mult, cf(Q4), ALU.add)
-    lin(cf(NAT), cf(K8), float(S), cf(I8))
-    lin(cf(NAT), cf(NAT), 1.0, float(DO))
-    lin(fl(O_NAT, 24), kf(NI, 24), 2.0, cf(NAT))
-    lin(cf(33), cf(F5), -2.0, cf(F4))
-    lin(cf(30), cf(K8), 4.0, cf(33))
+        lin(V("tm", 100, 101, 1, p0, p1), V("tm", 96, 97, 1, p0, p1), -3.0, V("tm", 98, 99, 1, p0, p1))
+        lin(V("ff", 2, 3, 1, p0, p1), V("tm", 100, 101, 1, p0, p1), 1.0, 6.0)
+    cp(co(O_GL, 4), V("ff", 0, 4))
+    iota(V("wb", 8, 9), [[0, 1]])
+    iota(kf(TK, 128), [[0, 128]])
+    iota(kf(TK, 1), [[0, 1]], 1)
+    iota(kf(K4, 32), [[0, 8], [1000, 4]])
+    lin(fl(O_NAT, 24), kf(NI, 24), 16.0, cf(I16))
+    lin(cf(X4), cf(KI), 1.0, cf(O16))
     iota(tm(90, 94), [[2, 2], [0, 2]])
-    lin(fl(O_CH, 4), tm(90, 94), 1.0, cf(30))
-    ts(cf(34), cf(K8), float(m), ALU.is_lt, 64.0, ALU.mult)
-    lin(cf(31), cf(K8), 8.0, cf(34))
-    iota(kf(SN, 12), [[64, 3], [1, 4]], YO - 8 * m)
-    lin(kf(SN, 12), kf(SN, 12), 1.0, cf(31))
-    cp(co(O_AT, 10), fl(O_AT, 10))
-    cp(co(O_MK, 12), fl(O_MK, 12))
+    ts(co(O_CH, 4), tm(90, 94), cf(X4), ALU.add)
+    iota(kf(SN, 12), [[48, 3], [1, 4]], YO)
+    lin(kf(SN, 12), kf(SN, 12), 1.0, cf(KI))
+    cp(co(O_AT, 6), fl(O_AT, 6))
 
     def choose(p0, p1):
         def Z(c0, c1, st=1):
@@ -530,14 +579,14 @@ def rank_program(g, core, T, topo):
         win = V(la, 0, LB + 16)
         N_, L, P, G, HS, SS = ("%s%d" % (x, t) for x in "NLPGHS")
         osn, oup, ow = ("%s%d" % (x, t) for x in ("osn", "oup", "ow"))
-        cp(V("nn", 0, 32), mine[t], co(O_AO, 2))
-        tt(V("nn", 32, 64), win, V("nn", 0, 32), ALU.subtract, co(O_BO, 2))
-        tt(V("nn", 64, 96), win, V("nn", 32, 64), ALU.add, co(O_CO, 2))
-        tr(Q("zz", 0, 160), Q("nn", 0, 64))
-        tr(Q("zz", 0, 192), Q("nn", 1, 64))
-        choose(0, 32)
-        a, off = V(la, LA - 3, LA + 8), co(O_AT, 2)
-        add("v", lambda a=a, off=off: g.vector.tensor_copy(ap(V("nn", 96, 128)), src(a, off)), [a, off, V(la, 0, 4)], [V("nn", 96, 128)], 0.108)
+        ca(V("nn", 0, 64), mine[t], co(O_AO, 4))
+        tt(V("nn", 192, 256), win, V("nn", 0, 64), ALU.subtract, co(O_BO, 4))
+        tt(V("nn", 0, 64), win, V("nn", 192, 256), ALU.add, co(O_CO, 4))
+        for a in range(2):
+            tr(Q("zz", a, 160), Q("nn", 0, 32 * a))
+            tr(Q("zz", a, 192), Q("nn", 1, 32 * a))
+        choose(0, 64)
+        ca(V("nn", 96, 128), V(la, LA - 3, LA + 8), co(O_AT, 2), V(la, 0, 64))
         tt(V("nn", 128, 160), win, V("nn", 96, 128), ALU.subtract, co(O_BT, 2))
         tt(V("nn", 160, 192), win, V("nn", 128, 160), ALU.add, co(O_CT, 2))
         tr(Q("zz", 2, 144), Q("nn", 1, 160))
@@ -546,67 +595,58 @@ def rank_program(g, core, T, topo):
         tr(Q("zz", 3, 192), Q("nn", 1, 160))
         choose(64, 128)
         for a in range(4):
-            tr(Q("ff", a, 0), Q("ww", 0, 240))
-        cp(V("ff", 32, 96), V("ff", 0, 32), co(O_SG, 4))
-        tr(V("ff", 96, 160), V("ff", 32, 96))
-        cp(V(osn, 0, 4), V("ff", 96, 160, 16))
-        pick(SS, 0, L, DE, V(osn, 0, 4))
-        push(b1, "b%d" % t, lambda d: V(SS + "q", 8 * dist(d), 8 * dist(d) + 8), lambda d: V(G + "q", 16 * m, 16 * m + 8), True)
-        push(b2, "b%d" % t, lambda d: V(SS + "s", 8 * dist(d), 8 * dist(d) + 8), lambda d: V(G + "s", 16 * m, 16 * m + 8))
-        came = arrive("b%d" % t, (2, 3), [V(G + x, 16 * r, 16 * r + 16) for x in "qs" for r in range(NR) if r != m], 2.9)
-        if t == 0:
-            load("s", V("uf", 0, 512), lambda: T.u[:], 2.5, [came])
-            load("s", V("vf", 0, 512), lambda: T.v[:], 2.5, [came])
-            quant("un", 0, "uf", 128)
-            quant("vn", 0, "vf", 128)
+            cp(Q(osn, a, 0, 1), Q("ww", 0, 240, 1))
+            cp(Q(osn, a, 1, 2), Q("ww", 1, 240, 2))
+        pick(SS, 0, L, C, V(osn, 0, 3))
+        push(b1, "b%d" % t, lambda d: V(SS + "q", first(d), first(d) + 8), lambda d: V(G + "q", 16 * m, 16 * m + 8), True)
+        push(b2, "b%d" % t, lambda d: V(SS + "s", first(d), first(d) + 8), lambda d: V(G + "s", 16 * m, 16 * m + 8))
+        arrive("b%d" % t, (2, 3), [V(G + x, 16 * r, 16 * r + 16) for x in "qs" for r in range(NR) if r != m])
+        for a in range(2):
+            tr(Q("ff", 0, 32 * a), Q("ww", a, 240))
+        ca(Q("ff", 1, 16), Q("ff", 0, 16))
+        ca(U("ff", 16, 48), V("ff", 16, 48, 1, 0, 64))
         if t < R - 1:
             aa, ab = "aa%d" % t, "aa%d" % (t + 1)
-            tt(V("mk", 0, 32), V("ff", 0, 32), kf(KM, 32), ALU.is_equal)
+            tt(V("mk", 0, 32), V("ff", 16, 48), kf(KM, 32), ALU.is_equal)
             scan(V("mk", 32, 64), kf(K4, 32), V("mk", 0, 32), 0.0, ALU.min, ALU.max)
             tt(V("mk", 64, 96), V("mk", 32, 64), V(aa, 0, 32), ALU.mult, co(O_MK, 2))
             tt(V("mk", 96, 112), V(aa, 16, 32), V("mk", 80, 96), ALU.subtract)
             tt(V(ab, 16, 32), V("mk", 96, 112), V("mk", 64, 80), ALU.add)
             tell(t + 1, mine[t + 1])
-        pick(G, 16 * m, L, DE, V(osn, 0, 1))
-        pick("Dc", YO + 64 * t, N_, DE, V(osn, 0, 4))
+        pick(G, 128, L, C, V(osn, 0, 3))
+        pick("Dc", YO + 48 * t, N_, C, V(osn, 0, 3))
         key = U("sa", 0, 1)
         act(U("sa", 0, 32), U("ww", 240, 272), ACT.Abs)
         tr(U("sa", 32, 64), U("sa", 0, 32))
-        act(U("sc", 1, 2), key, ACT.Identity, 1.0, None, cf(BF, 64))
-        act(U("sc", 2, 3), key, ACT.Identity, 1.0 / 32, None, cf(BP, 64))
+        lin(U("sc", 1, 2), key, 1.0, cf(BF, 64))
+        lin(U("sc", 2, 3), U("sc", 1, 2), 1.0 / 32, cf(BP, 64))
         act(U("sa", 72, 104), U("sa", 32, 64), ACT.Sign, -1.0, None, key, U("sc", 0, 1))
         act(U("sa", 104, 137), U("sa", 32, 65), ACT.Sign, -1.0, None, U("sc", 1, 2), U("sc", 3, 4))
-        act(U("sc", 4, 5), U("sc", 0, 1), ACT.Identity, 0.5, None, cf(BN, 64))
+        lin(U("sc", 4, 5), U("sc", 0, 1), 0.5, cf(BN, 64))
         ts(U("oh", 0, 64), kf(C1, 64, 1, 64), U("sc", 0, 1), ALU.is_equal, cf(VA, 64), ALU.mult)
         ts(U("oh", 64, 128), kf(C1, 64, 1, 64), U("sc", 3, 4), ALU.is_equal, U("sc", 2, 3), ALU.mult)
-        ts(U("oh", 128, 320), kf(C3, 192, 1, 64), U("sc", 2, 3), ALU.is_equal, U("sc", 4, 5), ALU.mult)
-        for c0, n, w in ((0, 4, 0), (128, 6, 16)):
+        nb = 6 if t < R - 1 else 3
+        ts(U("oh", 128, 128 + 32 * nb), kf(C3, 32 * nb, 1, 64), U("sc", 2, 3), ALU.is_equal, U("sc", 4, 5), ALU.mult)
+        for c0, n, w in ((0, 4, 0), (128, nb, 16)):
             c1 = c0 + 32 * n
             tr(U("ot", c0, c1), U("oh", c0, c1))
             scan(U("oc2", c0, c1), kf(RS, 32 * n, 1, 64), U("ot", c0, c1), 0.0, ALU.min, ALU.max)
-            cp(U("wb", w, w + n), U("oc2", c0 + 31, c1, 32))
-            act(V("wb", w, w + n, 1, 0, 64), U("oc2", c0 + 31, c1, 32), ACT.Copy)
+            (ca if w else cp)(U("wb", w, w + n), U("oc2", c0 + 31, c1, 32))
+            ca(V("wb", w, w + n, 1, 0, 64), U("oc2", c0 + 31, c1, 32))
             for a in range(4):
-                args = Q("wb", a, w + n, n), Q("oc2", 3 - a % 2, c0 + 31, 32 * n - 31, 32)
-                if a % 2:
-                    cp(*args)
-                else:
-                    act(*args, ACT.Copy)
+                (cp if a % 2 and (a == 1 or not w) else ca)(Q("wb", a, w + (6 if w else 4), n), Q("oc2", 3 - a % 2, c0 + 31, 32 * n - 31, 32))
         cp(V(ow, 0, 16), V("wb", 0, 9), co(O_GL, 1))
         tt(V("wf", 0, 16), V("wb", 16, 28), kf(DEF, 16), ALU.max, co(O_GL + 2, 1))
         cp(V(ow, 16, 32), V("wf", 0, 16))
-        pick(HS, 64, P, PR + 2 * S, V(ow, 4, 12))
+        pick(HS, 64, P, PN, V(ow, 4, 12))
+        if t < R - 1:
+            mm("pz", "vr", 2 * t + 2, P, 0, 128, True, True)
+            ca(V("sr", 0, 128), V("pz", 0, 128))
         for b in range(4):
             mm(H[b], "ep", 128 * b, HS, 64, 128, True, False)
         kp = V("kp", 0, 64)
-        act(kp, kf(TK, 144), ACT.Copy, off=V(ow, 4, 8))
-        if t < R - 1:
-            tt(V("up", 0, 96), V("ff", 0, 32), kf(TG, 96), ALU.is_equal, co(O_UP, 6))
-            tt(V("up", 96, 192), V("up", 0, 96), kf(SP + 96 * t, 96), ALU.mult)
-            scan(V("up", 192, 288), kf(K4, 96), V("up", 96, 192), 0.0, ALU.min, ALU.max)
-            tt(V("up", 288, 312), V("up", 195, 288, 4), kf(TG, 96, 4), ALU.max)
-            cp(V(oup, 0, 24), V("up", 288, 312))
-        cp(V("un2", 0, 64), V("ff", 0, 32), co(O_CH, 4))
+        ca(kp, kf(TK, 128), V(ow, 4, 8))
+        ca(V("un2", 0, 64), V("ff", 16, 48), co(O_CH, 4))
         tr(V("un2", 64, 128), V("un2", 0, 64))
         for q in range(4):
             ts(V("un2", 128 + 24 * q, 152 + 24 * q), fl(O_NAT, 24), V("un2", 64 + 16 * q, 65 + 16 * q), ALU.is_equal, kf(SN + 4 * t + q, 1), ALU.mult)
@@ -615,40 +655,53 @@ def rank_program(g, core, T, topo):
         now = V("un2", 296 + 24 * t, 320 + 24 * t)
         tt(now, V("un2", 272, 296), held, ALU.max)
         held = now
+        if t == 1:
+            now = V("un2", 368, 392)
+            tt(now, V("un2", 272, 296), fl(O_NAT, 24), ALU.max)
+        cp(V(oup, 0, 24), now)
         if t == R - 1:
-            cp(V(oup, 0, 24), now)
-            pick("Dn", 0, "Dc", YO + 64 * R, V(oup, 0, 24))
+            pick("Dn", 0, "Dc", YO + 48 * R, V(oup, 0, 24))
             mm("py", "un", 0, "Dn", 0, C, True, True)
-            dma("s", "stS", lambda: T.oc[:, 0:4 * C], lambda: T["Dnq"][:].bitcast(dt.uint8), [V("Dnq", 0, C)], [], 2.7)
+            dma("s", "stS", lambda: T.oc[:, 0:4 * C], lambda: T["Dnq"][:].bitcast(dt.uint8), [V("Dnq", 0, C)], [])
             for k in range(4):
                 dma("s", "stS", lambda k=k: T.osc[4 * k:4 * k + 4, 0:C], lambda k=k: T["Dns"][32 * k:32 * k + 4, 0:C], [V("Dns", 0, C)], [])
-            act(V("yb", 0, C), V("py", 0, C), ACT.Copy)
-            dma("s", "stS", lambda: T.y[:, 0:C], lambda: T["yb"][:, 0:C], [V("yb", 0, C)], [], 2.7)
-        pick(HS, 0, G, 128, V(ow, 0, 4))
+            ca(V("yb", 0, C), V("py", 0, C))
+            dma("s", "stS", lambda: T.y[:, 0:C], lambda: T["yb"][:, 0:C], [V("yb", 0, C)], [])
+        pick(HS, 0, G, 176, V(ow, 0, 4))
         for b in range(4):
             mm(H[b], "ep", 128 * b, HS, 0, 128, False, True)
-            scan(V("nt", b, 256, 4), kp, V(H[b], 0, 64), 0.0, ALU.mult, ALU.add)
-        quant(P, PN, "nt", 128)
-        pick("P%d" % (t + 1), PR if t < R - 1 else 0, P, PN + 128, V(ow, 16, 28 if t < R - 1 else 22))
+            scan(V("bt", b, 256, 4), kp, V(H[b], 0, 64), 0.0, ALU.mult, ALU.add)
+        quant(P, PN, "bt", 128)
         if t < R - 1:
-            scores(t + 1)
-            rewrite(t, YO + 64 * t - 64, 128)
-            pick("L%d" % (t + 1), DO, L, 640, V(oup, 0, 24))
-            pick("N%d" % (t + 1), DO, N_, 640, V(oup, 0, 24))
+            mm("pm", "vr", 2 * t + 2, P, PN, 128, True, True)
+            cp(V("sr", 128, 192), V("pm", 0, 64))
+            came = scores(t + 1, 192, lambda c, n, ow=ow: V(ow, 22 + c, 22 + c + n))
+            pick("P%d" % (t + 1), 0, P, PN + 64, V(ow, 14, 22))
+        else:
+            pick("P3", PR, P, PN + 64, V(ow, 16, 22))
+        if t == 0:
+            load("s", V("uf", 0, 512), lambda: T.u[:], [came])
+            load("s", V("vf", 0, 512), lambda: T.v[:], [came])
+            quant("un", 0, "uf", 128)
+            quant("vn", 0, "vf", 128)
+            pick("P3", 0, "P0", 16, V(ow, 8, 10))
+            pick("Dc", YO + 96, N_, C, V(ow, 8, 10))
+        if t < R - 1:
+            rewrite(t, YO + 80 * t - 80, 128)
+            pick("L%d" % (t + 1), 0, L, 480, V(oup, 0, 24))
+            pick("N%d" % (t + 1), 0, N_, 480, V(oup, 0, 24))
         if t == 0:
             table("N1")
-            act(V("aa1", 0, 16), V("pa", 2, 64, 4), ACT.Copy)
+            ca(V("aa1", 0, 8), V("ta", 2, 128, 16))
     mm("pz", "vn", 0, "P3", 0, 128, True, True)
-    dma("s", "stS", lambda: T.oc[:, 4 * C:4 * C + 8 * S], lambda: T["P3q"][:, 0:2 * S].bitcast(dt.uint8), [V("P3q", 0, 2 * S)], [])
+    dma("s", "stS", lambda: T.oc[:, 4 * C:4 * C + 8 * S], lambda: T["P3q"][:, PR:PN].bitcast(dt.uint8), [V("P3q", PR, PN)], [])
     for k in range(4):
         dma("a" if k % 2 else "s", "stA" if k % 2 else "stS", lambda k=k: T.osc[4 * k:4 * k + 4, C:C + 2 * S],
-            lambda k=k: T["P3s"][32 * k:32 * k + 4, 0:2 * S], [V("P3s", 0, 2 * S)], [])
-    cp(V("yb", C, C + 2 * S), V("pz", 0, 2 * S))
+            lambda k=k: T["P3s"][32 * k:32 * k + 4, PR:PN], [V("P3s", PR, PN)], [])
+    cp(V("yb", C, C + 2 * S), V("pz", PR, PN))
     dma("a", "stA", lambda: T.y[:, C:C + 2 * S], lambda: T["yb"][:, C:C + 2 * S], [V("yb", C, C + 2 * S)], [])
 
     ops = arrange(ops)
-    first = loads[:12]
-    ops = first + [o for o in ops if not any(o is x for x in first)]
     clock, seq = {q: {} for q in eng}, {q: 0 for q in eng}
     for i, o in enumerate(ops):
         q = o["q"]

from concourse.bass import DstId, RemoteDMATransfer
from concourse.mybir import dt, AluOpType, ActivationFunctionType

ALU = AluOpType
ACT = ActivationFunctionType
NR, C, S, R = 8, 384, 48, 3
BIG = 1.0e29
US = 262144.0
YO = C
PR, PN = 32, 128
LB, LA = 98, 123

SCRATCH = {}


def _pair(name, n):
    SCRATCH[name + "q"] = ("sbuf", [128, n], "float8_e4m3fn_x4")
    SCRATCH[name + "s"] = ("sbuf", [128, n], "uint8")


for _n, _w in (("Dc", 528), ("v0", 128), ("vr", 132), ("u1", 128), ("ur", 128), ("vn", 128), ("un", 128), ("ep", 512), ("em", 512),
               ("wt", 512), ("Dn", C),
               ("N0", 512), ("N1", 512), ("N2", C), ("L0", 512), ("L1", 512), ("L2", C),
               ("P0", 256), ("P1", 256), ("P2", 256), ("P3", 128)):
    _pair(_n, _w)
for _t in range(R):
    _pair("S%d" % _t, 48)
    _pair("G%d" % _t, 176)
    _pair("H%d" % _t, 192)
    SCRATCH["la%d" % _t] = ("sbuf", [128, 136], "float32")
    SCRATCH["ms%d" % _t] = ("sbuf", [128, 16], "float32")
    SCRATCH["aa%d" % _t] = ("sbuf", [128, 32], "float32")
    SCRATCH["osn%d" % _t] = ("sbuf", [128, 4], "uint16")
    SCRATCH["oup%d" % _t] = ("sbuf", [128, 24], "uint16")
    SCRATCH["ow%d" % _t] = ("sbuf", [128, 32], "uint16")
for _n, _w in (("bt", 2304), ("vz", 528), ("sv", 16), ("vf", 512), ("uf", 512), ("et", 520), ("ht", 1536), ("hu", 1536)):
    SCRATCH[_n] = ("sbuf", [128, _w], "bfloat16")
for _n, _w in (("cf", 48), ("kf", 1600), ("tt", 84), ("yb", 480), ("nn", 288), ("zz", 224), ("ww", 272),
               ("ff", 64), ("sa", 144), ("sc", 8), ("oh", 320), ("ot", 320), ("oc2", 320), ("wb", 32), ("wf", 32),
               ("ar", 384), ("ag", 128), ("ta", 128), ("un2", 392), ("kp", 64), ("tm", 192), ("fl", 96), ("mk", 112),
               ("a0", 8), ("sr", 192), ("mg", 96), ("gl", 192)):
    SCRATCH[_n] = ("sbuf", [128, _w], "float32")
for _n, _w in (("ci", 16), ("ib", 64)):
    SCRATCH[_n] = ("sbuf", [128, _w], "int32")
SCRATCH["co"] = ("sbuf", [128, 96], "uint16")
for _n in ("h0", "h1", "h2", "h3", "pa", "pm", "py", "pz"):
    SCRATCH[_n] = ("psum", [128, 512], "float32")

SEMAPHORES = (["qv", "qa", "qp", "qg", "sent", "stS", "stA"] + ["l%d" % _i for _i in range(12)]
              + [_x + "%d" % _t for _t in range(R) for _x in "abc"])


def deal(src, cores, topo):
    near = [d for d in cores if d != src and d in topo.cores_of(src)]
    far = [d for d in cores if d != src and d not in near]
    far.sort(key=lambda d: (topo.mates(src, d), topo.same_plane(src, d), topo.die(d) == topo.die(src)))
    out = topo.engines(src, far[0])
    inn = [e for e in topo.engines(src, near[0]) if e not in out]

    def m(es):
        return sum(1 << e for e in es)
    a1 = {far[i]: m(out[2 * i:2 * i + 2]) for i in range(4)}
    a2 = {far[4]: m(out[:4]), far[5]: m(out[4:])}
    b1 = {far[0]: m(out[0:2]), far[1]: m(out[2:4])}
    b1.update({far[2 + i]: m(out[4 + i:5 + i]) for i in range(4)})
    b2 = {far[0]: m(out[4:6]), far[1]: m(out[6:8])}
    b2.update({far[2 + i]: m(out[i:i + 1]) for i in range(4)})
    for tab in (a1, b1, b2):
        tab[near[0]] = m(inn[:2])
    return a1, a2, b1, b2


def bits(x):
    return bin(x).count("1")


ORDER = [
    0,1,2,3,4,5,6,7,8,9,11,12,10,67,15,22,23,70,16,13,17,18,68,29,21,71,238,27,19,74,69,82,20,77,72,85,26,81,28,83,87,24,84,75,86,80,101,37,73,88,130,62,
    33,31,30,224,76,102,60,49,135,38,25,34,78,42,50,44,55,36,79,32,104,111,136,14,213,103,105,51,35,210,63,112,107,52,137,214,226,39,113,237,199,216,53,114,219,
    43,138,106,40,225,220,139,140,132,142,54,145,236,134,41,133,89,159,235,64,65,215,45,108,190,146,115,193,56,192,46,109,162,66,189,116,57,217,211,58,110,227,
    247,47,165,147,59,117,48,119,194,195,118,246,148,141,200,61,196,120,143,160,204,168,90,221,149,197,163,122,150,191,154,223,198,121,169,265,166,212,248,228,161,
    158,229,266,123,124,250,155,153,252,218,205,164,151,156,157,95,91,97,167,171,170,93,239,259,125,144,230,92,126,127,222,183,152,231,232,240,267,172,96,128,268,
    174,129,270,269,271,173,176,175,272,233,280,201,178,273,94,274,179,202,275,263,255,177,99,256,281,257,258,203,276,98,184,100,261,244,241,282,277,284,283,243,
    285,278,185,234,286,182,279,287,180,181,296,294,299,298,297,242,301,300,295,245,288,302,289,249,206,308,251,253,290,303,186,324,291,254,187,207,188,292,307,208,
    293,322,304,305,306,309,323,131,209,325,310,260,264,326,327,311,262,321,329,312,332,330,328,331,313,333,356,357,363,334,335,314,364,336,343,337,340,338,342,339,
    344,341,351,315,367,347,354,355,368,350,358,359,374,361,365,362,373,402,346,360,349,366,400,348,375,316,377,345,379,369,435,381,317,376,403,378,320,380,382,404,
    407,318,405,319,370,410,383,352,413,353,371,408,384,406,414,409,411,385,392,395,412,372,386,416,419,387,393,428,391,417,401,420,415,421,418,423,394,422,424,429,
    425,525,426,526,430,449,427,388,389,390,436,396,397,450,437,431,451,441,438,439,440,452,453,432,442,455,454,443,456,444,457,445,433,434,458,446,459,447,460,448,
    461,465,464,468,470,466,467,463,469,462,477,476,471,494,490,478,492,472,496,479,495,398,498,480,499,399,497,491,501,481,500,502,532,482,504,493,503,505,483,533,
    509,507,506,511,510,508,512,484,485,520,534,592,473,474,535,513,524,536,514,537,523,515,517,516,475,486,487,527,519,528,488,538,529,530,543,518,544,545,521,539,
    522,541,540,547,549,551,531,546,489,566,548,550,552,569,572,575,567,542,553,573,554,570,571,555,576,568,565,574,556,577,562,578,579,581,557,583,558,563,585,590,
    561,580,582,584,586,587,589,564,606,588,591,559,560,593,607,594,608,597,596,595,598,610,611,599,609,612,600,613,601,614,602,615,603,616,604,617,605,618,623,622,
    626,620,627,621,624,625,633,634,619,629,628,635,637,641,636,642,643,630,631,639,677,645,646,644,678,638,632,648,647,649,640,681,682,679,680,651,650,683,652,659,
    684,653,656,654,658,657,660,655,685,667,664,661,666,662,686,663,670,671,672,687,688,673,674,675,697,690,689,691,665,698,693,694,676,668,695,699,669,700,705,706,
    703,704,696,701,702,707,708,711,709,715,710,712,713,714,716,692,717]


def arrange(ops):
    if len(ORDER) != len(ops):
        return list(ops)
    place = {k: i for i, k in enumerate(ORDER)}
    assert all(place[x["at"]] < place[o["at"]] for o in ops for x in o["deps"])
    return [ops[i] for i in ORDER]


def rank_program(g, core, T, topo):
    m = T.rank_of(core)
    if m is None:
        return
    cores = list(T.cores)
    eng = {"v": g.vector, "a": g.scalar, "p": g.tensor, "g": g, "s": g.sync}
    qsem = {"v": "qv", "a": "qa", "p": "qp", "g": "qg"}

    ops, touch = [], {}

    def V(name, c0, c1, step=1, p0=0, p1=128):
        return (name, p0, p1, c0, c1, step)

    def ap(v):
        if v[5] == 1:
            return T[v[0]][v[1]:v[2], v[3]:v[4]]
        return T[v[0]][v[1]:v[2], v[3]:v[4]:v[5]]

    def wide(v):
        return len(range(v[3], v[4], v[5]))

    def meet(a, b):
        if SCRATCH[a[0]][0] == "psum":
            return True
        if a[2] <= b[1] or b[2] <= a[1] or a[4] <= b[3] or b[4] <= a[3]:
            return False
        if a[5] == 1 and b[5] == 1:
            return True
        return bool(set(range(a[3], a[4], a[5])) & set(range(b[3], b[4], b[5])))

    def add(q, fn, reads, writes, sem=None, count=16, after=()):
        o = {"q": q, "fn": fn, "inc": False, "sem": sem, "count": count, "at": len(ops), "deps": list(after)}
        seen = {x["at"] for x in after}
        for v, wr in [(v, False) for v in reads] + [(v, True) for v in writes]:
            ps = SCRATCH[v[0]][0] == "psum"
            for u, uw, x in touch.get(v[0], []):
                if x["at"] not in seen and (wr or uw or ps) and meet(u, v) and not (q is None and x["q"] is None):
                    seen.add(x["at"])
                    o["deps"].append(x)
        ops.append(o)
        for v in reads:
            touch.setdefault(v[0], []).append((v, False, o))
        for v in writes:
            touch.setdefault(v[0], []).append((v, True, o))
        return o

    def sc(x):
        return ap(x) if isinstance(x, tuple) else x

    def src(v, off):
        return ap(v) if off is None else ap(v).indirect(ap(off))

    def vs(*xs):
        return [x for x in xs if isinstance(x, tuple)]

    def ts(out, a, s1, op0, s2=None, op1=None):
        if op1 is None:
            add("v", lambda: g.vector.tensor_scalar(ap(out), ap(a), sc(s1), None, op0), vs(a, s1), [out])
        else:
            add("v", lambda: g.vector.tensor_scalar(ap(out), ap(a), sc(s1), sc(s2), op0, op1), vs(a, s1, s2), [out])

    def tt(out, a, b, op, off=None):
        add("v", lambda: g.vector.tensor_tensor(ap(out), src(a, off), ap(b), op), vs(a, b, off), [out])

    def cp(out, a, off=None):
        add("v", lambda: g.vector.tensor_copy(ap(out), src(a, off)), vs(a, off), [out])

    def act(out, a, func, scale=1.0, off=None, bias=None, acc=None, behind=None):
        kw = {}
        if bias is not None:
            kw["bias"] = sc(bias)
        if scale != 1.0:
            kw["scale"] = sc(scale)
        if acc is not None:
            kw["accum_out"] = ap(acc)
        add("a", lambda: g.scalar.activation(ap(out), src(a, off), func, **kw), vs(a, off, bias, scale, behind), vs(out, acc))

    def ca(out, a, off=None, behind=None):
        act(out, a, ACT.Copy, off=off, behind=behind)

    def lin(out, a, scale, bias):
        act(out, a, ACT.Identity, scale, None, bias)

    def scan(out, d0, d1, init, op0, op1):
        add("v", lambda: g.vector.tensor_tensor_scan(ap(out), ap(d0), ap(d1), sc(init), op0, op1), vs(d0, d1, init), [out])

    def tr(out, a):
        add("v", lambda: g.vector.transpose(ap(out), ap(a)), [a], [out])

    def mset(out, x):
        add("v", lambda: g.vector.memset(ap(out), x), [], [out])

    def iota(out, pat, base=0, mult=0):
        if SCRATCH[out[0]][2] == "int32":
            add("g", lambda: g.iota(ap(out), pat, base, mult), [], [out])
        else:
            add("g", lambda: g.iota(ap(out), pat, base, mult, allow_small_or_imprecise_dtypes=True), [], [out])

    def quant(name, c0, tile, n, e0=0):
        q, s, a = V(name + "q", c0, c0 + n), V(name + "s", c0, c0 + n), V(tile, e0, e0 + 4 * n)
        add("v", lambda: g.vector.quantize_mx(ap(q), ap(s), ap(a)), [a], [q, s])

    def mm(bank, st, s0, mv, m0, n, start, stop):
        o = V(bank, 0, n)
        r = [V(st + "q", s0, s0 + 128), V(st + "s", s0, s0 + 128), V(mv + "q", m0, m0 + n), V(mv + "s", m0, m0 + n)]
        add("p", lambda: g.tensor.matmul_mx(ap(o), ap(r[0]), ap(r[1]), ap(r[2]), ap(r[3]), start, stop), r, [o])

    def pick(dst, d0, frm, n, off):
        oq, iq = V(dst + "q", d0, d0 + 16 * wide(off)), V(frm + "q", 0, n)
        add("v", lambda: g.vector.tensor_copy(ap(oq).bitcast(dt.uint32), ap(iq).bitcast(dt.uint32).indirect(ap(off))), [iq, off], [oq])
        o2, i2 = V(dst + "s", d0, d0 + 16 * wide(off)), V(frm + "s", 0, n)
        add("a", lambda: g.scalar.activation(ap(o2), ap(i2).indirect(ap(off)), ACT.Copy), [i2, off], [o2])

    def dma(q, sem, fo, fi, reads, writes, after=()):
        return add(q, lambda: eng[q].dma_start(fo(), fi()), reads, writes, sem=sem, after=after)

    plans = {c: deal(c, cores, topo) for c in cores}
    sent, calls = [0], []

    def push(tab, sem, frm, to, code=False):
        items = [(d, frm(T.rank_of(d)), to(T.rank_of(d))) for d in tab]

        def fn():
            trs = []
            for d, u, v in items:
                rid, pid = topo.addr(d, core)
                a, b = ap(u), ap(v)
                if code:
                    a, b = a.bitcast(dt.uint8), b.bitcast(dt.uint8)
                trs.append(RemoteDMATransfer(dst_ids=[DstId(rid=rid, pnc=pid)], dma_engine_mask=tab[d], remote_sem=T.sem[sem], src=a, dst=b))
            return g.remote_dma_fused(trs, local_sem=T.sem["sent"])
        o = add("g", fn, [u for d, u, v in items], [], sem="sent", after=calls[-1:])
        o["remote"] = True
        calls.append(o)
        sent[0] += sum(bits(x) for x in tab.values())

    def arrive(sem, which, writes):
        n = sum(bits(plans[c][w].get(core, 0)) for c in cores if c != core for w in which)
        return add(None, None, [], writes, sem=sem, count=n, after=calls[-1:])

    a1, a2, b1, b2 = plans[core]

    al, be, ga = (4, 1, (0, 2)) if m == 4 else (1, 2, (1, 5)) if m == 0 else (m, 2 * m, (2 * m, 6 * m) if m % 2 else (4, 1))
    path = [(al * (k % 2) + be * (k // 2 % 2) + ga[k // 4]) % NR for k in range(NR)]

    loads = []

    def load(q, dst, fi, after=()):
        loads.append(dma(q, "l%d" % len(loads), lambda: ap(dst), fi, [], [dst], after))
    PT, UT, XT = 384, 240, 768
    load("s", V("sv", 0, 16), lambda: T.v[:, 0:16])
    load("a", V("bt", PT + 192, PT + 384), lambda: T.pd[:])
    load("s", V("bt", PT, PT + 192), lambda: T.pr[:])
    load("a", V("bt", UT, UT + 16), lambda: T.u[:, 0:16])
    load("s", V("bt", XT, XT + 1536), lambda: T.x[:])
    load("s", V("wts", 0, 512), lambda: T.ws[:])
    for b in range(4):
        w = V("wtq", 128 * b, 128 * b + 128)
        loads.append(dma("s", "l%d" % len(loads), lambda w=w: ap(w).bitcast(dt.uint8), lambda b=b: T.wc[:, 512 * b:512 * b + 512], [], [w]))
    mset(V("bt", PT - 4 * PR, PT), 0.0)
    mset(V("vz", 0, 528), 0.0)

    def cf(k, p0=0, p1=128):
        return V("cf", k, k + 1, 1, p0, p1)

    def cf2(k):
        return V("cf", k, k + 2)

    def ib(c0, c1):
        return V("ib", c0, c1)

    def tm(c0, c1, st=1):
        return V("tm", c0, c1, st)

    def gl(c0, c1, st=1):
        return V("gl", c0, c1, st)

    def fl(k, n):
        return V("fl", k, k + n)

    def co(k, n):
        return V("co", k, k + n)

    def kf(k, n, st=1, p0=0, p1=128):
        return V("kf", k, k + n, st, p0, p1)
    PP, F2, F3, F4, F5, Q4, HI, G3, K1, I8, O16, O32, K8, R8, I16, E, LO = range(17)
    SG, W8, AK, SH, VA, BF, BP, BN, FX, PL = range(18, 28)
    X1, X2, X3, X4, X5, X6, X8, X9, X10, X11, X12, KA, KI, Y1, Y2, Y3, Y4 = range(28, 45)
    O_TA, O_UR, O_MA, O_AO, O_BO, O_CO, O_VR, O_M0 = 0, 8, 18, 20, 24, 28, 32, 82
    O_AT, O_BT, O_CT, O_MK, O_CH, O_NAT, O_GL = 34, 36, 38, 44, 52, 56, 76
    NI, SN, K4, WS, C1, C3, RS, DEF, TK, NEG, KM = 0, 416, 512, 608, 664, 728, 920, 1240, 1272, 1416, 1464

    def fill(out, x):
        lin(out, kf(NI, wide(out), 1, out[1], out[2]), 0.0, float(x))
    iota(V("ci", 0, 1), [[0, 1]], 0, 1)
    iota(kf(NI, 32), [[1, 32]])
    iota(kf(NI + 32, 96), [[1, 96]], 32)
    for k, sh in ((F2, 2), (F3, 3), (F4, 4), (F5, 5)):
        ts(V("ci", k, k + 1), V("ci", 0, 1), sh, ALU.arith_shift_right)
    for k, c0, n, an in ((Q4, 0, 3, 3), (K1, 1, 4, 1), (K8, 0, 2, 7), (I16, 0, 1, 15), (E, 0, 1, 31)):
        ts(V("ci", k, k + n), V("ci", c0, c0 + n), an, ALU.bitwise_and)
    cp(V("cf", 0, 16), V("ci", 0, 16))
    ts(cf2(LO), V("cf", PP, PP + 2), float(S), ALU.is_lt)
    iota(tm(0, 4), [[m, 2], [4, 2]], 8 - m)
    iota(tm(6, 8), [[-4, 2]], 8)
    iota(tm(128, 136), [[m, 2], [ga[1] - ga[0], 2], [0, 2]], ga[0] - 2 * m + 16)
    iota(tm(136, 140), [[ga[1] - ga[0], 2], [be, 2]], ga[0])
    lin(tm(144, 148), tm(0, 4), 1.0, cf(HI))
    lin(cf(X1), cf(HI), -1.0, 0.0)
    lin(tm(148, 150), tm(6, 8), 1.0, cf(X1))
    lin(cf(X2), cf(K1), float(al), float(ga[0]))
    lin(cf(SG), cf(I8), float(be), cf(X2))
    ts(tm(150, 158), tm(128, 136), cf(SG), ALU.add, -float(ga[0]), ALU.add)
    lin(tm(158, 159), cf(O32), float(ga[1] - ga[0]), cf(SG))
    lin(cf(Y1), cf(O16), float(al), 0.0)
    lin(tm(159, 163), tm(136, 140), 1.0, cf(Y1))
    cp(ib(0, 19), tm(144, 163))
    ts(ib(0, 19), ib(0, 19), 7, ALU.bitwise_and)
    cp(tm(8, 27), ib(0, 19))
    n1, n2 = tm(8, 10), tm(10, 12)
    keep, turn, by = (6, 1, 1) if m == 4 else (0, 7, 0) if m == 0 else (0, 7, 1) if m % 2 else (4, 3, 1)
    ts(ib(20, 21), cf(K8), float(by), ALU.add)
    ts(ib(21, 22), ib(20, 21), turn, ALU.bitwise_and)
    ts(ib(22, 23), V("ci", K8, K8 + 1), keep, ALU.bitwise_and)
    cp(tm(28, 30), ib(21, 23))
    lin(tm(30, 31), tm(28, 29), 1.0, tm(29, 30))
    lin(tm(31, 32), cf(K8), -1.0, tm(30, 31))
    lin(fl(O_MA, 1), tm(31, 32), cf(LO), cf(K8))
    lin(cf(X10), cf(F5), 2.0, 0.0)
    lin(tm(32, 34), kf(NI, 2), 1.0, cf(X10))
    ts(tm(34, 36), tm(32, 34), 3.0, ALU.is_ge, -3.0, ALU.mult)
    ts(tm(36, 38), tm(32, 34), 6.0, ALU.is_ge, -3.0, ALU.mult)
    tt(tm(38, 40), tm(34, 36), tm(36, 38), ALU.add)
    tt(tm(40, 42), tm(38, 40), tm(32, 34), ALU.add)
    lin(cf(W8), cf(I16), 8.0, 0.0)
    lin(tm(42, 44), tm(40, 42), 128.0, cf(W8))
    for e in range(2):
        lin(V("fl", O_TA + e, O_TA + 8, 2), tm(23, 27), 1.0, tm(42 + e, 43 + e))
    cp(co(O_TA, 8), fl(O_TA, 8))
    ts(co(O_UR, 8), kf(NI, 8), 0.0, ALU.mult, cf(Q4), ALU.add)
    cp(co(O_MA, 1), fl(O_MA, 1))
    iota(tm(164, 168), [[4, 2], [0, 2]])
    lin(fl(O_AO, 4), tm(164, 168), 1.0, cf(HI))
    lin(fl(O_BO, 4), tm(18, 22), 2.0, float(LB))
    lin(fl(O_CO, 4), tm(14, 18), 2.0, LB + 1.0)
    cp(co(O_AO, 12), fl(O_AO, 12))
    iota(tm(102, 104), [[16, 2]], 0, 1)
    iota(V("ag", 0, 32), [[1, 2], [0, 16]])
    tr(V("ag", 32, 64), V("ag", 0, 32))
    odd = V("ag", 32, 33)
    ts(tm(104, 106), tm(102, 104), 65.0, ALU.is_ge, -float(S), ALU.mult)
    ts(tm(106, 108), tm(102, 104), 17.0, ALU.is_lt, float(S), ALU.mult)
    tt(tm(110, 112), tm(104, 106), tm(106, 108), ALU.add)
    ts(tm(114, 116), tm(110, 112), 31.0, ALU.add, odd, ALU.mult)
    ts(tm(108, 110), tm(102, 104), 64.0, ALU.is_lt, 31.0, ALU.add)
    tt(tm(124, 126), tm(104, 106), tm(108, 110), ALU.add)
    ts(tm(112, 114), tm(124, 126), odd, ALU.mult)
    iota(tm(116, 120), [[0, 2], [16, 2]], PR, 1)
    tt(tm(120, 124), tm(112, 116), tm(116, 120), ALU.add)
    ts(co(O_M0, 4), tm(120, 124), 127.0, ALU.min)
    for a in range(8):
        (cp if a % 2 else ca)(V("vz", 128 * (a // 2) + 60 + 4 * (a % 2), 128 * (a // 2) + 64 + 4 * (a % 2)), V("sv", 0, 4))
    quant("v0", 0, "vz", 128)
    lin(cf(X9), cf(I8), 4.0, cf(Q4))
    ts(co(O_VR, 2), kf(NI, 2), 8.0, ALU.mult, cf(X9), ALU.add)
    for a in range(4):
        out = V("vz", 128 * a + 60, 128 * a + 92)
        if a % 2:
            cp(out, V("sv", 0, 16), co(O_VR, 2))
        else:
            ca(out, V("sv", 0, 16), co(O_VR, 2))
    iota(gl(0, 8), [[2, 2], [4, 2], [1, 2]])
    iota(gl(128, 136), [[2, 2], [-4, 2], [1, 2]], 4)
    iota(gl(8, 16), [[0, 8]], 8)
    for a in (1, 3):
        lin(V("gl", 0, 8, 1, 32 * a, 32 * a + 32), V("gl", 128, 136, 1, 32 * a, 32 * a + 32), 1.0, 0.0)
    lin(gl(16, 32), gl(0, 16), 1.0, 0.0)
    iota(gl(136, 168), [[0, 2], [1, 16]])
    iota(gl(142, 146), [[0, 2], [1, 2]])
    iota(gl(158, 162), [[3, 2], [1, 2]], 3)
    for c0 in (146, 162):
        lin(gl(c0, c0 + 2), kf(NI, 2), 1.0, -3.0)
    for c0 in (6, 22):
        lin(gl(136 + c0, 142 + c0), gl(136 + c0, 142 + c0), 1.0, cf(X10))
    ts(gl(32, 64), gl(136, 168), 0.0, ALU.max, 11.0, ALU.min)
    tr(gl(96, 128), gl(32, 64))
    cp(co(O_GL + 4, 1), gl(96, 97))
    lin(cf(X3), cf(I16), 1.0, float(PR))
    lin(gl(168, 180), kf(NI, 12), 16.0, cf(X3))
    lin(gl(174, 177), gl(174, 177), 1.0, -S - 1.0)
    lin(gl(177, 180), gl(177, 180), 1.0, -2 * S - 1.0)
    ts(cf(X11), cf(I16), 0.0, ALU.is_equal, float(S), ALU.mult)
    lin(gl(174, 178, 3), gl(174, 178, 3), 1.0, cf(X11))
    cp(kf(DEF, 16), gl(168, 180), co(O_GL + 4, 1))
    cp(co(O_M0 + 4, 2), kf(DEF + 10, 2))

    mset(V("et", 0, 516), 0.0)
    for name, sign in (("em", -1.0), ("ep", 1.0)):
        ts(V("et", 3, 515, 4), kf(NI, 128), cf(PP), ALU.is_equal, sign, ALU.mult)
        for b in range(4):
            quant(name, 128 * b, "et", 128, 3 - b)

    def first(d):
        return 4 * (path.index(d) & 6 if m == 4 else path.index(d))

    def scores(t, n, off):
        la = "la%d" % t
        cp(V("mg", 0, 64), V("sr", 0, n), off(0, 4))
        tr(V(la, 0, 64), V("mg", 0, 64))

        def pair(d, more=0):
            c0 = 47 if m + d >= NR else 15
            return V(la, c0 - more, c0 + 2)
        for tab in (a1, a2):
            push(tab, "a%d" % t, pair, lambda d: V(la, LB + 2 * ((m - d) % NR), LB + 2 * ((m - d) % NR) + 2))
        came = arrive("a%d" % t, (0, 1), [V(la, LB + 2, LB + 16)])
        ca(V(la, LB - 2, LB + 2), pair(m, 2))
        ca(V("mg", 64, 96), V("sr", 0, n), off(4, 2))
        tr(V(la, 64, 96), V("mg", 64, 96))
        return came

    def table(frm):
        mm("pa", "ur", 0, frm, 0, C, True, True)
        ca(V("ar", 0, C), V("pa", 0, C))
        ca(V("ag", 0, 128), V("ar", 0, C), co(O_TA, 8))
        tr(V("ta", 0, 128), V("ag", 0, 128))

    def tell(t, own):
        la, ms = "la%d" % t, "ms%d" % t
        ca(V(ms, 0, 16), own, co(O_MA, 1))
        for tab in (a1, a2):
            push(tab, "c%d" % t, lambda d: V(ms, path.index(d), path.index(d) + 1), lambda d: V(la, LA + (m - d) % NR, LA + (m - d) % NR + 1))
        arrive("c%d" % t, (0, 1), [V(la, LA + 1, LA + 8)])
        ca(V(la, LA - 3, LA + 1), V(ms, path.index(m) + 5, path.index(m) + 9))

    quant("P0", 0, "bt", 128, PT - 4 * PR)
    quant("vr", 0, "vz", 132)
    quant("u1", 0, "bt", 128, UT)
    pick("ur", 0, "u1", 128, co(O_UR, 8))
    mm("pm", "v0", 0, "P0", 0, 128, True, True)
    cp(V("sr", 0, 128), V("pm", 0, 128))
    scores(0, 128, lambda c, n: co(O_M0 + c, n))

    H = ["h0", "h1", "h2", "h3"]

    def rewrite(t, c0, n):
        N_, L = "N%d" % t, "L%d" % t
        for b in range(4):
            bank = ("py", "pm", "pz", "h3")[b] if c0 == 0 else H[b]
            mm(bank, "wt", 128 * b, "Dc", c0, n, True, True)
            if n > 128 and b % 2:
                ts(V("ht", b, 4 * n, 4), V(bank, 0, n), 0.0, ALU.max, 0.0625, ALU.mult)
            else:
                act(V("ht", b, 4 * n, 4), V(bank, 0, n), ACT.Relu, 0.0625)
            mm(H[b], "em", 128 * b, "Dc", c0, n, True, False)
        quant(N_, c0, "ht", n)
        for b in range(4):
            mm(H[b], "ep", 128 * b, N_, c0, n, False, True)
            ca(V("hu", b, 4 * n, 4), V(H[b], 0, n))
        for c in range(0, n, 128):
            quant(L, c0 + c, "hu", 128, 4 * c)

    quant("Dc", 0, "bt", C, XT)
    table("Dc")
    ca(V("a0", 0, 8), V("ta", 0, 128, 16))
    ca(V("aa0", 16, 24), V("ta", 2, 128, 16))
    ca(V("aa0", 24, 32), V("ta", 1, 128, 16))
    ca(V("aa1", 8, 16), V("a0", 0, 8))
    mine = [V("a0", 0, 8), V("aa1", 24, 32), V("aa2", 16, 24)]
    tell(0, mine[0])
    rewrite(0, 0, C)
    table("N0")
    ca(V("aa0", 0, 8), V("ta", 2, 128, 16))
    ca(V("aa0", 8, 16), V("ta", 1, 128, 16))

    lin(fl(O_AT, 2), n1, 1.0, 3.0)
    lin(tm(56, 58), n2, 2.0, LB - 79.0)
    lin(fl(O_BT, 2), tm(56, 58), cf(LO), 79.0)
    ts(tm(58, 60), n2, float(8 - m), ALU.is_ge, 32.0, ALU.mult)
    ts(tm(60, 62), n2, float(m), ALU.is_gt, LB - 16.0, ALU.add)
    for c in range(2):
        lin(tm(62 + c, 63 + c), tm(12 + c, 13 + c), 2.0, tm(60 + c, 61 + c))
    tt(tm(64, 66), tm(58, 60), tm(62, 64), ALU.subtract)
    ts(tm(66, 68), tm(64, 66), cf(LO), ALU.mult, 16.0, ALU.add)
    tt(fl(O_CT, 2), tm(66, 68), tm(62, 64), ALU.add)
    lin(tm(74, 75), cf(K8), 4.0, 3.0)
    ts(co(O_MK, 2), kf(NI, 2), 0.0, ALU.mult, tm(74, 75), ALU.add)
    for c in range(2):
        iota(ib(32 + 16 * c, 48 + 16 * c), [[be, 2], [al, 2], [0, 4]], ga[c])
    ts(ib(32, 64), ib(32, 64), 7, ALU.bitwise_and)
    lin(cf(X12), cf(LO), float(S), cf(PP))
    lin(cf(PL), cf(X12), 8.0, -8.0 * S)
    ts(kf(KM, 32), ib(32, 64), cf(PL), ALU.add)
    ts(tm(168, 176), V("ib", 32, 64, 4), cf(K8), ALU.is_equal)
    tt(tm(176, 184), tm(168, 176), kf(NI, 8), ALU.mult)
    act(tm(184, 192), tm(176, 184), ACT.Identity, 4.0, acc=cf(KI))
    iota(tm(76, 79), [[-1, 3]], 3)
    ts(tm(80, 83), tm(76, 79), cf(Q4), ALU.is_le, -0.5, ALU.add)
    lin(V("zz", 13, 16), tm(80, 83), 2.0 * BIG, 0.0)
    fill(kf(NEG, 48), -BIG)
    iota(kf(WS, 52), [[0, 52]], 1)
    iota(kf(WS + 3, 1), [[0, 1]], -1)
    iota(V("ww", 155, 192), [[0, 37]], int(-US / 2))
    ts(cf(SH, 64), cf(R8, 64), float(8 - m), ALU.is_ge, cf(O32, 64), ALU.mult)
    lin(cf(AK, 64), cf(SH, 64), -32.0, cf(E, 64))
    lin(cf(FX, 64), cf(E, 64), -2.0, -32.0 * S - 32.0)
    lin(cf(X6, 64), cf(E, 64), 1.0, 32.0)
    lin(V("tt", 0, 84, 1, 0, 64), kf(NI, 84, 1, 0, 64), 8.0, V("tm", 22, 23, 1, 0, 64))
    lin(V("tt", 1, 84, 1, 64), kf(NI + 2, 83, 1, 64), 32.0, cf(AK, 64))
    lin(V("tt", 0, 1, 1, 64), cf(FX, 64), cf(SH, 64), cf(X6, 64))
    lin(cf(Y2, 64), cf(O32, 64), 4.0, cf(Q4, 64))
    lin(cf(VA, 64), cf(R8, 64), 16.0, cf(Y2, 64))
    mine_row, mine_diag = 128 + 4 * path.index(m) - 16 * m, 128 + 4 * path.index(2 * m % NR) - 16 * m - 4
    for r, row, diag in ((0, 0, -4 if m else 0), (4, 4 if m > 4 else 0, -4 if m > 4 else 0), (m, mine_row, mine_diag)):
        lin(cf(Y3, 64), cf(O32, 64), float(diag - row), float(row))
        ts(cf(Y4, 64), cf(R8, 64), float(r), ALU.is_equal, cf(Y3, 64), ALU.mult)
        lin(cf(VA, 64), cf(VA, 64), 1.0, cf(Y4, 64))
    lin(cf(BF, 64), cf(E, 64), -1.0, -0.5)
    lin(cf(BP, 64), cf(O32, 64), float(S), PR - 1.0 + 1.0 / 64)
    lin(cf(BN, 64), cf(O32, 64), 32.0, PN + 15.5)
    fill(V("sa", 64, 65), -BIG)
    iota(kf(C1, 64), [[32, 2], [0, 2], [2, 16]], -31)
    iota(kf(C3, 96), [[16, 3], [0, 2], [1, 16]], PR)
    lin(kf(C3 + 96, 96), kf(C3, 96), 1.0, S - 1.0)
    lin(kf(C3, 96, 1, 96), kf(C3, 96, 1, 96), 1.0, float(S))
    fill(kf(C3 + 96, 17, 16), PR + 2 * S - 1)
    iota(kf(RS, 192), [[0, 6], [1000, 32]])
    tr(V("ff", 0, 32), gl(0, 32))
    ts(tm(96, 97), gl(96, 97), 3.0, ALU.is_ge, 3.0, ALU.mult)
    ts(tm(97, 98), gl(96, 97), 9.0, ALU.is_ge, -3.0, ALU.mult)
    lin(tm(98, 99), gl(96, 97), 1.0, tm(97, 98))
    lin(V("ff", 2, 3), tm(96, 97), 1.0, tm(98, 99))
    for a in (1, 3):
        p0, p1 = 32 * a, 32 * a + 32
        lin(V("tm", 100, 101, 1, p0, p1), V("tm", 96, 97, 1, p0, p1), -3.0, V("tm", 98, 99, 1, p0, p1))
        lin(V("ff", 2, 3, 1, p0, p1), V("tm", 100, 101, 1, p0, p1), 1.0, 6.0)
    cp(co(O_GL, 4), V("ff", 0, 4))
    iota(V("wb", 8, 9), [[0, 1]])
    iota(kf(TK, 128), [[0, 128]])
    iota(kf(TK, 1), [[0, 1]], 1)
    iota(kf(K4, 32), [[0, 8], [1000, 4]])
    lin(fl(O_NAT, 24), kf(NI, 24), 16.0, cf(I16))
    lin(cf(X4), cf(KI), 1.0, cf(O16))
    iota(tm(90, 94), [[2, 2], [0, 2]])
    ts(co(O_CH, 4), tm(90, 94), cf(X4), ALU.add)
    iota(kf(SN, 12), [[48, 3], [1, 4]], YO)
    lin(kf(SN, 12), kf(SN, 12), 1.0, cf(KI))
    cp(co(O_AT, 6), fl(O_AT, 6))

    def choose(p0, p1):
        def Z(c0, c1, st=1):
            return V("zz", c0, c1, st, p0, p1)

        def W(c0, c1):
            return V("ww", c0, c1, 1, p0, p1)
        sc0 = Z(160, 208)
        scan(Z(16, 160, 3), sc0, kf(NEG, 48, 1, p0, p1), Z(13, 14), ALU.min, ALU.max)
        scan(Z(17, 160, 3), sc0, Z(13, 157, 3), Z(14, 15), ALU.min, ALU.max)
        scan(Z(18, 160, 3), sc0, Z(14, 158, 3), Z(15, 16), ALU.min, ALU.max)
        scan(W(0, 48), sc0, Z(15, 159, 3), BIG, ALU.min, ALU.max)
        ts(W(48, 99), Z(157, 208), W(47, 48), ALU.is_equal, US, ALU.mult)
        scan(W(104, 155), kf(WS, 51, 1, p0, p1), W(48, 99), -US / 2, ALU.mult, ALU.subtract)
        scan(W(192, 272), W(107, 187), V("tt", 1, 81, 1, p0, p1), V("tt", 0, 1, 1, p0, p1), ALU.max, ALU.min)

    def Q(name, a, c0, n=32, st=1):
        return V(name, c0, c0 + n, st, 32 * a, 32 * a + 32)

    def U(name, c0, c1, st=1):
        return V(name, c0, c1, st, 64, 128)

    held = fl(O_NAT, 24)
    for t in range(R):
        la = "la%d" % t
        win = V(la, 0, LB + 16)
        N_, L, P, G, HS, SS = ("%s%d" % (x, t) for x in "NLPGHS")
        osn, oup, ow = ("%s%d" % (x, t) for x in ("osn", "oup", "ow"))
        ca(V("nn", 0, 64), mine[t], co(O_AO, 4))
        tt(V("nn", 192, 256), win, V("nn", 0, 64), ALU.subtract, co(O_BO, 4))
        tt(V("nn", 0, 64), win, V("nn", 192, 256), ALU.add, co(O_CO, 4))
        for a in range(2):
            tr(Q("zz", a, 160), Q("nn", 0, 32 * a))
            tr(Q("zz", a, 192), Q("nn", 1, 32 * a))
        choose(0, 64)
        ca(V("nn", 96, 128), V(la, LA - 3, LA + 8), co(O_AT, 2), V(la, 0, 64))
        tt(V("nn", 128, 160), win, V("nn", 96, 128), ALU.subtract, co(O_BT, 2))
        tt(V("nn", 160, 192), win, V("nn", 128, 160), ALU.add, co(O_CT, 2))
        tr(Q("zz", 2, 144), Q("nn", 1, 160))
        tr(Q("zz", 2, 176), Q("nn", 2, 160))
        tr(Q("zz", 3, 160), Q("nn", 0, 160))
        tr(Q("zz", 3, 192), Q("nn", 1, 160))
        choose(64, 128)
        for a in range(4):
            cp(Q(osn, a, 0, 1), Q("ww", 0, 240, 1))
            cp(Q(osn, a, 1, 2), Q("ww", 1, 240, 2))
        pick(SS, 0, L, C, V(osn, 0, 3))
        push(b1, "b%d" % t, lambda d: V(SS + "q", first(d), first(d) + 8), lambda d: V(G + "q", 16 * m, 16 * m + 8), True)
        push(b2, "b%d" % t, lambda d: V(SS + "s", first(d), first(d) + 8), lambda d: V(G + "s", 16 * m, 16 * m + 8))
        arrive("b%d" % t, (2, 3), [V(G + x, 16 * r, 16 * r + 16) for x in "qs" for r in range(NR) if r != m])
        for a in range(2):
            tr(Q("ff", 0, 32 * a), Q("ww", a, 240))
        ca(Q("ff", 1, 16), Q("ff", 0, 16))
        ca(U("ff", 16, 48), V("ff", 16, 48, 1, 0, 64))
        if t < R - 1:
            aa, ab = "aa%d" % t, "aa%d" % (t + 1)
            tt(V("mk", 0, 32), V("ff", 16, 48), kf(KM, 32), ALU.is_equal)
            scan(V("mk", 32, 64), kf(K4, 32), V("mk", 0, 32), 0.0, ALU.min, ALU.max)
            tt(V("mk", 64, 96), V("mk", 32, 64), V(aa, 0, 32), ALU.mult, co(O_MK, 2))
            tt(V("mk", 96, 112), V(aa, 16, 32), V("mk", 80, 96), ALU.subtract)
            tt(V(ab, 16, 32), V("mk", 96, 112), V("mk", 64, 80), ALU.add)
            tell(t + 1, mine[t + 1])
        pick(G, 128, L, C, V(osn, 0, 3))
        pick("Dc", YO + 48 * t, N_, C, V(osn, 0, 3))
        key = U("sa", 0, 1)
        act(U("sa", 0, 32), U("ww", 240, 272), ACT.Abs)
        tr(U("sa", 32, 64), U("sa", 0, 32))
        lin(U("sc", 1, 2), key, 1.0, cf(BF, 64))
        lin(U("sc", 2, 3), U("sc", 1, 2), 1.0 / 32, cf(BP, 64))
        act(U("sa", 72, 104), U("sa", 32, 64), ACT.Sign, -1.0, None, key, U("sc", 0, 1))
        act(U("sa", 104, 137), U("sa", 32, 65), ACT.Sign, -1.0, None, U("sc", 1, 2), U("sc", 3, 4))
        lin(U("sc", 4, 5), U("sc", 0, 1), 0.5, cf(BN, 64))
        ts(U("oh", 0, 64), kf(C1, 64, 1, 64), U("sc", 0, 1), ALU.is_equal, cf(VA, 64), ALU.mult)
        ts(U("oh", 64, 128), kf(C1, 64, 1, 64), U("sc", 3, 4), ALU.is_equal, U("sc", 2, 3), ALU.mult)
        nb = 6 if t < R - 1 else 3
        ts(U("oh", 128, 128 + 32 * nb), kf(C3, 32 * nb, 1, 64), U("sc", 2, 3), ALU.is_equal, U("sc", 4, 5), ALU.mult)
        for c0, n, w in ((0, 4, 0), (128, nb, 16)):
            c1 = c0 + 32 * n
            tr(U("ot", c0, c1), U("oh", c0, c1))
            scan(U("oc2", c0, c1), kf(RS, 32 * n, 1, 64), U("ot", c0, c1), 0.0, ALU.min, ALU.max)
            (ca if w else cp)(U("wb", w, w + n), U("oc2", c0 + 31, c1, 32))
            ca(V("wb", w, w + n, 1, 0, 64), U("oc2", c0 + 31, c1, 32))
            for a in range(4):
                (cp if a % 2 and (a == 1 or not w) else ca)(Q("wb", a, w + (6 if w else 4), n), Q("oc2", 3 - a % 2, c0 + 31, 32 * n - 31, 32))
        cp(V(ow, 0, 16), V("wb", 0, 9), co(O_GL, 1))
        tt(V("wf", 0, 16), V("wb", 16, 28), kf(DEF, 16), ALU.max, co(O_GL + 2, 1))
        cp(V(ow, 16, 32), V("wf", 0, 16))
        pick(HS, 64, P, PN, V(ow, 4, 12))
        if t < R - 1:
            mm("pz", "vr", 2 * t + 2, P, 0, 128, True, True)
            ca(V("sr", 0, 128), V("pz", 0, 128))
        for b in range(4):
            mm(H[b], "ep", 128 * b, HS, 64, 128, True, False)
        kp = V("kp", 0, 64)
        ca(kp, kf(TK, 128), V(ow, 4, 8))
        ca(V("un2", 0, 64), V("ff", 16, 48), co(O_CH, 4))
        tr(V("un2", 64, 128), V("un2", 0, 64))
        for q in range(4):
            ts(V("un2", 128 + 24 * q, 152 + 24 * q), fl(O_NAT, 24), V("un2", 64 + 16 * q, 65 + 16 * q), ALU.is_equal, kf(SN + 4 * t + q, 1), ALU.mult)
        tt(V("un2", 224, 272), V("un2", 128, 176), V("un2", 176, 224), ALU.max)
        tt(V("un2", 272, 296), V("un2", 224, 248), V("un2", 248, 272), ALU.max)
        now = V("un2", 296 + 24 * t, 320 + 24 * t)
        tt(now, V("un2", 272, 296), held, ALU.max)
        held = now
        if t == 1:
            now = V("un2", 368, 392)
            tt(now, V("un2", 272, 296), fl(O_NAT, 24), ALU.max)
        cp(V(oup, 0, 24), now)
        if t == R - 1:
            pick("Dn", 0, "Dc", YO + 48 * R, V(oup, 0, 24))
            mm("py", "un", 0, "Dn", 0, C, True, True)
            dma("s", "stS", lambda: T.oc[:, 0:4 * C], lambda: T["Dnq"][:].bitcast(dt.uint8), [V("Dnq", 0, C)], [])
            for k in range(4):
                dma("s", "stS", lambda k=k: T.osc[4 * k:4 * k + 4, 0:C], lambda k=k: T["Dns"][32 * k:32 * k + 4, 0:C], [V("Dns", 0, C)], [])
            ca(V("yb", 0, C), V("py", 0, C))
            dma("s", "stS", lambda: T.y[:, 0:C], lambda: T["yb"][:, 0:C], [V("yb", 0, C)], [])
        pick(HS, 0, G, 176, V(ow, 0, 4))
        for b in range(4):
            mm(H[b], "ep", 128 * b, HS, 0, 128, False, True)
            scan(V("bt", b, 256, 4), kp, V(H[b], 0, 64), 0.0, ALU.mult, ALU.add)
        quant(P, PN, "bt", 128)
        if t < R - 1:
            mm("pm", "vr", 2 * t + 2, P, PN, 128, True, True)
            cp(V("sr", 128, 192), V("pm", 0, 64))
            came = scores(t + 1, 192, lambda c, n, ow=ow: V(ow, 22 + c, 22 + c + n))
            pick("P%d" % (t + 1), 0, P, PN + 64, V(ow, 14, 22))
        else:
            pick("P3", PR, P, PN + 64, V(ow, 16, 22))
        if t == 0:
            load("s", V("uf", 0, 512), lambda: T.u[:], [came])
            load("s", V("vf", 0, 512), lambda: T.v[:], [came])
            quant("un", 0, "uf", 128)
            quant("vn", 0, "vf", 128)
            pick("P3", 0, "P0", 16, V(ow, 8, 10))
            pick("Dc", YO + 96, N_, C, V(ow, 8, 10))
        if t < R - 1:
            rewrite(t, YO + 80 * t - 80, 128)
            pick("L%d" % (t + 1), 0, L, 480, V(oup, 0, 24))
            pick("N%d" % (t + 1), 0, N_, 480, V(oup, 0, 24))
        if t == 0:
            table("N1")
            ca(V("aa1", 0, 8), V("ta", 2, 128, 16))
    mm("pz", "vn", 0, "P3", 0, 128, True, True)
    dma("s", "stS", lambda: T.oc[:, 4 * C:4 * C + 8 * S], lambda: T["P3q"][:, PR:PN].bitcast(dt.uint8), [V("P3q", PR, PN)], [])
    for k in range(4):
        dma("a" if k % 2 else "s", "stA" if k % 2 else "stS", lambda k=k: T.osc[4 * k:4 * k + 4, C:C + 2 * S],
            lambda k=k: T["P3s"][32 * k:32 * k + 4, PR:PN], [V("P3s", PR, PN)], [])
    cp(V("yb", C, C + 2 * S), V("pz", PR, PN))
    dma("a", "stA", lambda: T.y[:, C:C + 2 * S], lambda: T["yb"][:, C:C + 2 * S], [V("yb", C, C + 2 * S)], [])

    ops = arrange(ops)
    clock, seq = {q: {} for q in eng}, {q: 0 for q in eng}
    for i, o in enumerate(ops):
        q = o["q"]
        o["at"], o["waits"], o["clock"] = i, [], {}
        if q is not None:
            known = clock[q]
            for x in sorted(o["deps"], key=lambda y: -y["at"]):
                if x.get("remote") or x["q"] == q == "p":
                    continue
                k, n = x["tok"]
                if known.get(k, 0) < n:
                    o["waits"].append(x)
                    x["inc"] = True
                    for kk, nn in list(x["clock"].items()) + [(k, n)]:
                        if known.get(kk, 0) < nn:
                            known[kk] = nn
            o["clock"] = dict(known)
        if o["sem"] is None:
            seq[q] += 1
            o["tok"] = (q, seq[q])
        else:
            o["tok"] = ("#" + o["sem"], o["count"])
    cnt = {q: 0 for q in qsem}
    stores = {"stS": 0, "stA": 0}
    for o in ops:
        if o["sem"] is None and o["inc"]:
            cnt[o["q"]] += 1
            o["val"] = cnt[o["q"]]
    for o in ops:
        if o["q"] is None:
            continue
        for x in o["waits"]:
            if x["sem"] is None:
                eng[o["q"]].wait_ge(T.sem[qsem[x["q"]]], x["val"])
            else:
                eng[o["q"]].wait_ge(T.sem[x["sem"]], x["tok"][1])
        ins = o["fn"]()
        if o.get("remote"):
            continue
        if o["sem"] is not None:
            ins.then_inc(T.sem[o["sem"]], 16)
            if o["sem"] in stores:
                stores[o["sem"]] += 16
        elif o["inc"]:
            ins.then_inc(T.sem[qsem[o["q"]]], 1)
    g.sync.wait_ge(T.sem["stS"], stores["stS"])
    g.scalar.wait_ge(T.sem["stA"], stores["stA"])
    g.wait_ge(T.sem["sent"], sent[0])
